import numpy as np, ml_dtypes
CORES = [5,29,101,125,133,157,229,253]
N = 8
BF = ml_dtypes.bfloat16
def gentries(a):
    return np.ascontiguousarray(a.reshape(8, 16, -1).transpose(0, 2, 1)).reshape(8, -1)
def gtable(e):
    e = np.asarray(e); return np.ascontiguousarray(e.reshape(8, -1, 16).transpose(0, 2, 1)).reshape(128, -1).astype(np.int32)
W, K, R, B, S, HOP, T = 1024, 1024, 512, 2, 2, 3, 4
LO = 256
def parts(rng):
    sh = (N, 8, 16, W)
    s = np.minimum(15, np.floor(16 * rng.random(sh) ** 2)); a = rng.integers(32, 257, sh) * 0.00390625
    m = np.exp2(-rng.choice(np.arange(5), sh, p=np.array([0.05, 0.1, 0.2, 0.3, 0.35])).astype(np.float64))
    x = rng.integers(-256, 256, sh); c = rng.integers(0, W, (N, 8, K))
    u = np.where(rng.random((N, 8, T, K)) < 0.5, np.floor(np.exp2(8 * rng.random((N, 8, T, K)))), rng.integers(0, 256, (N, 8, T, K)))
    z = rng.integers(0, 256, (N, 8, T, K))
    r = np.ascontiguousarray(np.argsort(rng.random((N, 8, T - 1, W // 2)), axis=-1)[..., :R])
    return s, a, m, x, c, np.clip(u, 0, 255), z, r
def pack(s, a, m, x, c, u, z, r):
    b = lambda v, p, n: np.ascontiguousarray(np.asarray(v, np.float32).reshape(N, p, n)).astype(BF)
    return {"sg": b(s, 128, W), "al": b(a, 128, W), "mj": b(m, 128, W), "nx": b(x, 128, W), "ce": np.stack([gtable(v) for v in c]),
            "uu": b(u, 8, T * K), "zz": b(z, 8, T * K), "rp": np.stack([gtable(v.reshape(8, -1)) for v in r])}
def two(rng, shape, lo, hi):
    return np.where(rng.random(shape) < 0.5, lo, hi)
def setup_inputs(rng):
    return pack(*parts(rng))
def setup_inputs_spread(rng):
    s, a, m, x, c, u, z, r = parts(rng); sh = (N, 8, 16, W); col = (N, 8, 1, W)
    s = np.minimum(15, np.floor(16 * rng.random(sh) * np.exp2(-3 * rng.random(col))))
    a = np.clip(np.exp2(-2 * rng.random(col)) * (0.5 + 0.5 * rng.random(sh)), 0.125, 1.0)
    m = np.exp2(-np.clip(rng.integers(0, 5, col) + rng.integers(-1, 2, sh), 0, 4).astype(np.float64))
    x = np.clip(np.floor((2 * rng.random(sh) - 1) * 256 * np.exp2(-6 * rng.random(col))), -256, 255)
    u = np.clip(np.floor(np.exp2(8 * rng.random((N, 8, 1, K))) * rng.random((N, 8, T, K))), 0, 255)
    z = np.clip(np.floor(256 * rng.random((N, 8, T, K)) ** 2), 0, 255)
    return pack(s, a, m, x, c, u, z, r)
def setup_inputs_ends(rng):
    s, a, m, x, c, u, z, r = parts(rng)
    s = two(rng, s.shape, 0, 15); a = two(rng, a.shape, 0.125, 1.0); m = two(rng, m.shape, 0.0625, 1.0); x = two(rng, x.shape, -256, 255)
    c = two(rng, c.shape, 0, W - 1); u = two(rng, u.shape, 0, 255); z = two(rng, z.shape, 0, 255)
    s[:, :, 0] = 0; s[:, :, 15] = 15; a[:, :, 15] = 1.0; m[:, :, 15] = 1.0
    c[..., K - 1] = W - 1; z[..., 15] = 0; z[..., K - 1] = 0
    places = np.concatenate([np.arange(R // 2), np.arange(W // 2 - R // 2, W // 2)])
    r = places[np.argsort(rng.random((N, 8, T - 1, R)), axis=-1)]
    return pack(s, a, m, x, c, u, z, r)
def setup_inputs_corners(rng):
    s, a, m, x, c, u, z, r = parts(rng); o = int(rng.integers(0, 4)); sh = (16, W)
    for q in range(N):
        for g in range(8):
            kind = (q + g + o) % 4
            if kind == 0:
                e = rng.integers(0, 4, sh); s[q, g] = 2 ** e; m[q, g] = np.exp2(-np.clip(e + rng.integers(-1, 2, sh), 0, 4).astype(np.float64))
            if kind == 1:
                s[q, g] = np.where(rng.random(sh) < 0.9, 15, s[q, g]); m[q, g] = np.where(rng.random(sh) < 0.9, 1.0, m[q, g])
            if kind == 2: m[q, g] = np.where(rng.random(sh) < 0.9, 0.0625, m[q, g])
            if kind == 3: x[q, g] = np.where(rng.random(sh) < 0.5, two(rng, sh, -256, 255), x[q, g])
    c = np.where(rng.random(c.shape) < 0.3, two(rng, c.shape, 0, W - 1), c)
    u = np.clip(rng.integers(0, 17, u.shape) * 2 ** rng.integers(0, 5, u.shape) + rng.integers(-1, 2, u.shape), 0, 255)
    z = np.clip(16 * rng.integers(0, 17, z.shape) + rng.integers(-1, 2, z.shape), 0, 255)
    return pack(s, a, m, x, c, u, z, r)
def setup_inputs_crowd(rng):
    s, a, m, x, c, u, z, r = parts(rng)
    c[:] = rng.integers(0, W, (N, 8, 1)); c[:, 1::4, K - 1] = (c[:, 1::4, K - 1] + rng.integers(1, W, (N, 2))) % W
    few = rng.integers(0, W, (N, 2, 4)); few[:, 0, 0] = W - 1; few[:, 0, 1] = 0
    c[:, 3::4] = np.take_along_axis(few, rng.integers(0, 4, (N, 2, K)), 2)
    u[:, :6] = u[:, :6, :, :1].copy(); z[:, :5] = z[:, :5, :, :1].copy()
    m[:, ::2] = m[:, ::2, :1].copy(); s[:, ::4] = s[:, ::4, :1].copy()
    h = W // 2; h0 = int(rng.integers(0, N)); st = int(rng.integers(1, 101)) * (2 * int(rng.integers(0, 2)) - 1)
    v = (int(rng.integers(0, h)) + st * np.arange(T + 1)) % h; odd = rng.integers(0, 2, T + 1)
    for t in range(T):
        for i in range(2): x[..., 2 * v[t] + i] = 2 * st + odd[t + 1] - i
    for i in range(2):
        e = 2 * v[1:] + i
        m[..., e] = 0.0625; s[..., e] = rng.integers(1, 16, (N, 8, 16, T)); s[:, :, 15, e] = 15
        a[..., e] = rng.integers(192, 257, (N, 8, 16, T)) * 0.00390625
    first = 255 * int(rng.integers(0, 2))
    for q in (h0, (h0 + HOP) % N):
        c[q] = 2 * v[0] + odd[0]
        z[q, :, 0] = first; z[q, :, 1] = 0; z[q, :, 2] = 255; z[q, :, 3:4] = 0
        z[q, 3::4, 1:4, K - 1] = 255 - z[q, 3::4, 1:4, K - 1]
    c[h0, 1::4, K - 1] = (c[h0, 1::4, K - 1] + rng.integers(1, W, 2)) % W
    return pack(s, a, m, x, c, u, z, r)
def setup_inputs_calm(rng):
    s, a, m, x, c, u, z, r = parts(rng)
    s = 8 + rng.integers(0, 2, s.shape); m = two(rng, m.shape, 0.0625, 0.125)
    for q in range(N): m[q, int(rng.integers(0, 8))] = 0.0625
    u = np.where(rng.random(u.shape) < 0.5, 8 * rng.integers(0, 32, u.shape), rng.integers(0, 256, u.shape))
    z = rng.choice(np.array([0, 127, 128, 143, 144, 255]), z.shape)
    h = W // 2; qa = int(rng.integers(0, N)); qb = (qa - HOP) % N; cell = np.arange(W); low = cell // h * h
    for q in (qa, qb): x[q] = np.clip(cell + x[q], low, low + h - 1) - cell
    s[qa, :, :, h:] = 8; c[qb] = rng.integers(h, W, (8, K))
    return pack(s, a, m, x, c, u, z, r)
def check_ranges(d):
    bad = []
    for k, lo, hi in (("sg", 0, 15), ("al", 0.125, 1), ("mj", 0.0625, 1), ("nx", -256, 255), ("ce", 0, W - 1), ("uu", 0, 255), ("zz", 0, 255), ("rp", 0, W // 2 - 1)):
        v = np.asarray(d[k]).astype(np.float64)
        if not (np.min(v) >= lo and np.max(v) <= hi): bad.append("range of " + k)
        elif k != "al" and k != "mj" and np.any(v != np.floor(v)): bad.append("whole numbers of " + k)
    if not np.all(np.isin(np.asarray(d["mj"]).astype(np.float64), np.array([0.0625, 0.125, 0.25, 0.5, 1.0]))): bad.append("powers of two of mj")
    e = np.sort(np.stack([gentries(np.asarray(v)) for v in d["rp"]]).reshape(N, 8, T - 1, R), axis=-1)
    if np.any(e[..., 1:] == e[..., :-1]): bad.append("distinct pairs of rp")
    return bad
def move(v, n):
    v = np.roll(v, n * HOP, axis=0); h = K // 2
    return np.concatenate([v[..., :h], np.roll(v[..., h:], n, axis=1)], axis=-1)
def reference(sg, al, mj, nx, ce, uu, zz, rp):
    s, a, m = [v.astype(np.float64).reshape(N, 8, 16, W) for v in (sg, al, mj)]; x = nx.astype(np.float32).astype(np.int64).reshape(N, 8, 16, W)
    u, z = [v.astype(np.float64).reshape(N, 8, T, K) for v in (uu, zz)]
    c = np.stack([gentries(v) for v in ce]).astype(np.int64); pairs = np.stack([gentries(v) for v in rp]).astype(np.int64).reshape(N, 8, T - 1, R)
    w = np.ones((N, 8, 16, K)); tally = np.zeros((N, 8, 16, K))
    qi = np.arange(N)[:, None, None]; gi = np.arange(8)[None, :, None]; slot = np.arange(K)[None, None, :]; hero = slot % 16
    for t in range(T):
        p = np.minimum(np.floor(u[:, :, t] * m[qi, gi, hero, c]), 15).astype(np.int64)
        d = (c + x[qi, gi, p, c]) & (W - 1); dd = d[:, :, None, :]
        rho = np.take_along_axis(s, dd, 3) * np.take_along_axis(m, dd, 3)
        real = 256 * rho[qi, gi, hero, slot] > z[:, :, t]
        w = np.clip(w * np.where(real[:, :, None, :], 2 * np.take_along_axis(a, dd, 3) * rho, 2 * np.maximum(1 - rho, 0)), 0.125, 4.0)
        tally = tally + w
        if t < T - 1:
            e = (2 * pairs[:, :, t] + (d[..., LO:LO + R] & 1))[:, :, None, :]; old = np.take_along_axis(m, e, 3)
            np.put_along_axis(m, e, np.where(rho[..., LO:LO + R] > 1, np.maximum(old * 0.5, 0.0625), old), 3)
        c = np.where(real, d ^ 1, d)
        if t < T - 1 and (t + 1) % S == 0: c, w, tally, u, z = [move(v, 1) for v in (c, w, tally, u, z)]
    return {"tl": move(tally, -(B - 1)).reshape(N, 128, K).astype(np.float32)}

def check_inputs(d):
    bad = list(check_ranges(d))
    if not bad:
        for name, y in reference(**d).items():
            for q in range(N):
                v = np.abs(np.asarray(y[q], np.float64)); s = np.sqrt(np.mean(v * v))
                if v.max() > 7 * s or s < 2.0 ** 0: bad.append('%s of rank %d is uneven or too small' % (name, q))
    return bad

@@ -1,0 +1,594 @@
+from concourse.bass import DstId, RemoteDMATransfer
+from concourse.mybir import AluOpType as A, ActivationFunctionType as AF
+
+SIM_CORES = 256
+HOP = 3
+
+SCRATCH = {
+    "tab": ("sbuf", [128, 3072], "bfloat16"),
+    "rtab": ("sbuf", [128, 3072], "bfloat16"),
+    "mm": ("sbuf", [128, 1024], "bfloat16"),
+    "rm": ("sbuf", [128, 1024], "bfloat16"),
+    "rpi": ("sbuf", [128, 96], "int32"),
+    "rrp": ("sbuf", [128, 32], "int32"),
+    "v2": ("sbuf", [128, 96], "int32"),
+    "cei": ("sbuf", [128, 64], "int32"),
+    "uz": ("sbuf", [128, 512], "bfloat16"),
+    "uz1": ("sbuf", [128, 512], "bfloat16"),
+    "uzt": ("sbuf", [128, 1024], "bfloat16"),
+    "ul": ("sbuf", [128, 256], "bfloat16"),
+    "zl": ("sbuf", [128, 256], "bfloat16"),
+    "qi": ("sbuf", [128, 8], "int32"),
+    "qj": ("sbuf", [128, 4], "int32"),
+    "qf": ("sbuf", [128, 4], "float32"),
+    "pp": ("sbuf", [128, 4], "float32"),
+    "jj": ("sbuf", [128, 144], "bfloat16"),
+    "xx": ("sbuf", [128, 256], "bfloat16"),
+    "oi": ("sbuf", [128, 48], "int32"),
+    "o16": ("sbuf", [128, 48], "uint16"),
+    "big": ("sbuf", [128, 16], "bfloat16"),
+    "msk": ("sbuf", [128, 16], "float32"),
+    "dm": ("sbuf", [128, 2048], "bfloat16"),
+    "bw": ("sbuf", [128, 144], "bfloat16"),
+    "i1": ("sbuf", [128, 128], "bfloat16"),
+    "i2": ("sbuf", [128, 128], "bfloat16"),
+    "oh": ("sbuf", [128, 256], "bfloat16"),
+    "six": ("sbuf", [128, 512], "bfloat16"),
+    "ng": ("sbuf", [128, 1024], "bfloat16"),
+    "dg": ("sbuf", [128, 1024], "bfloat16"),
+    "sel": ("sbuf", [128, 1024], "bfloat16"),
+    "rg": ("sbuf", [128, 1024], "bfloat16"),
+    "nd": ("sbuf", [128, 1024], "bfloat16"),
+    "old": ("sbuf", [128, 512], "bfloat16"),
+    "fac": ("sbuf", [128, 512], "bfloat16"),
+    "xv": ("sbuf", [128, 64], "float32"),
+    "v16": ("sbuf", [128, 64], "uint16"),
+    "yi": ("sbuf", [128, 64], "int32"),
+    "ib": ("sbuf", [128, 128], "int32"),
+    "par": ("sbuf", [128, 64], "int32"),
+    "ee": ("sbuf", [128, 32], "int32"),
+    "d16": ("sbuf", [128, 64], "uint16"),
+    "e16": ("sbuf", [128, 32], "uint16"),
+    "rr": ("sbuf", [128, 64], "int32"),
+    "rb": ("sbuf", [128, 128], "int32"),
+    "c2": ("sbuf", [128, 64], "float32"),
+    "c216": ("sbuf", [128, 64], "uint16"),
+    "ce16": ("sbuf", [128, 64], "uint16"),
+    "wr": ("sbuf", [128, 512], "float32"),
+    "psa": ("psum", [128, 512], "float32"),
+    "psb": ("psum", [128, 512], "float32"),
+    "psm0": ("psum", [128, 512], "float32"),
+    "psm1": ("psum", [128, 512], "float32"),
+    "psr0": ("psum", [128, 512], "float32"),
+    "psr1": ("psum", [128, 512], "float32"),
+    "psr2": ("psum", [128, 512], "float32"),
+    "psr3": ("psum", [128, 512], "float32"),
+    "i32": ("sbuf", [128, 128], "float32"),
+    "fin": ("sbuf", [128, 512], "float32"),
+}
+for _t in range(4):
+    SCRATCH["ff%d" % _t] = ("sbuf", [128, 2048], "float32")
+    SCRATCH["ww%d" % _t] = ("sbuf", [128, 1024], "float32")
+    SCRATCH["cn%d" % _t] = ("sbuf", [128, 128], "float32")
+    SCRATCH["co%d" % _t] = ("sbuf", [128, 128], "uint16")
+
+NDMA = 40
+SEMAPHORES = ["eV", "eS", "eP", "eG", "h_tab", "h_rp", "h_m", "a_tab", "a_rp", "a_m", "sent"] + ["d%d" % i for i in range(NDMA)]
+
+
+def helpers(src, dst, T, topo):
+    def per_die(cands):
+        out = {}
+        for c in cands:
+            if T.rank_of(c) is None and topo.may_write(src, c) and topo.may_write(c, dst):
+                out.setdefault(topo.die(c), c)
+        return [out[d] for d in sorted(out)]
+    near = per_die(topo.cores_of(src))
+    far = per_die([c for c in range(SIM_CORES) if topo.mates(c, dst)])
+    return near + far
+
+
+def masks(src, hs, topo):
+    off = topo.engines(src, hs[2])
+    on = [e for e in topo.engines(src, hs[0]) if e not in off]
+    sets = [on[:len(on) // 2], on[len(on) // 2:], off[:len(off) // 2], off[len(off) // 2:]]
+    return [sum(1 << e for e in s) for s in sets], [len(s) for s in sets]
+
+
+def helper_program(g, core, src, dst, k, hs, T, topo):
+    _, cnt = masks(src, hs, topo)
+    rid, pid = topo.addr(dst, core)
+    m = topo.mask(core, dst)
+    n = len(topo.engines(core, dst))
+    sent = 0
+    g.wait_ge(T.sem.h_tab, cnt[k])
+    g.remote_dma(T.rtab[:, 768 * k:768 * (k + 1)], T.rtab[:, 768 * k:768 * (k + 1)], T.sem.a_tab, T.sem.sent, pid, rid, m)
+    sent += n
+    if k == 0:
+        g.wait_ge(T.sem.h_rp, cnt[k])
+        g.remote_dma(T.rrp[:], T.rrp[:], T.sem.a_rp, T.sem.sent, pid, rid, m)
+        sent += n
+    g.wait_ge(T.sem.h_m, cnt[k])
+    g.remote_dma(T.rm[:, 256 * k:256 * (k + 1)], T.rm[:, 256 * k:256 * (k + 1)], T.sem.a_m, T.sem.sent, pid, rid, m)
+    sent += n
+    g.wait_ge(T.sem.sent, sent)
+
+
+def emit(g, T, ops, ext):
+    q = {"V": g.vector, "S": g.scalar, "P": g.tensor, "G": g, "Y": g.sync}
+    writer, readers = dict(ext), {}
+    known = {e: {} for e in q}
+    clock, waits, marked = {}, [], set()
+    for k in ext.values():
+        clock[k] = {k: 1}
+    for n, (eng, fn, rd, wr, kind) in enumerate(ops):
+        deps = set()
+        for key in rd:
+            if key in writer:
+                deps.add(writer[key])
+            if key.startswith("ps"):
+                deps.update(r for r in readers.get(key, ()) if ops[r][0] != eng)
+        for key in wr:
+            if key in writer:
+                deps.add(writer[key])
+            deps.update(readers.get(key, ()))
+        need = []
+        for d in sorted(deps, key=lambda x: -x if isinstance(x, int) else 1):
+            if isinstance(d, int) and ops[d][4] == "c":
+                have = known[eng].get(ops[d][0], -1) >= d or (eng == "P" and ops[d][0] == "P")
+            else:
+                have = d in known[eng]
+            if not have:
+                need.append(d)
+                marked.add(d)
+                for a, b in clock[d].items():
+                    known[eng][a] = max(known[eng].get(a, -1), b)
+        waits.append(need)
+        c = dict(known[eng])
+        c[eng if kind == "c" else n] = n
+        clock[n] = c
+        for key in rd:
+            readers.setdefault(key, []).append(n)
+        for key in wr:
+            writer[key] = n
+            readers[key] = []
+    where, count, nd = {}, {e: 0 for e in q}, 0
+    left = []
+    for n, (eng, fn, rd, wr, kind) in enumerate(ops):
+        for d in waits[n]:
+            s, v = where[d] if isinstance(d, int) else (T.sem[d[0]], d[1])
+            q[eng].wait_ge(s, v)
+        if kind == "c":
+            ins = fn()
+            if n in marked:
+                count[eng] += 1
+                ins.then_inc(T.sem["e" + eng], 1)
+                where[n] = (T.sem["e" + eng], count[eng])
+        else:
+            s = T.sem["d%d" % nd]
+            nd += 1
+            if kind == "d":
+                fn().then_inc(s, 16)
+                where[n] = (s, 16)
+            else:
+                where[n] = (s, fn(s))
+            if n not in marked:
+                left.append(where[n])
+    for s, v in left:
+        g.wait_ge(s, v)
+
+
+def rank_program(g, core, T, topo):
+    N = len(T.cores)
+    rank = T.rank_of(core)
+    if rank is None:
+        for s in range(N):
+            src, dst = T.cores[s], T.cores[(s - HOP) % N]
+            hs = helpers(src, dst, T, topo)
+            if core in hs:
+                helper_program(g, core, src, dst, hs.index(core), hs, T, topo)
+        return
+    dst = T.cores[(rank - HOP) % N]
+    hs = helpers(core, dst, T, topo)
+    mk, cnt = masks(core, hs, topo)
+    hin = helpers(T.cores[(rank + HOP) % N], core, T, topo)
+    nin = [len(topo.engines(h, core)) for h in hin]
+    ext = {"rtab": ("a_tab", sum(nin)), "rrp": ("a_rp", nin[0]), "rm": ("a_m", sum(nin))}
+
+    ops = []
+    V, S, P = g.vector, g.scalar, g.tensor
+
+    def op(eng, fn, rd, wr, kind="c"):
+        ops.append((eng, fn, rd, wr, kind))
+
+    def dma(eng, out, in_, rd, wr, add=False):
+        qq = {"S": g.scalar, "Y": g.sync, "G": g}[eng]
+        if add:
+            op(eng, lambda: qq.dma_start(out, in_, accum_op=A.add), rd, wr, "d")
+        else:
+            op(eng, lambda: qq.dma_start(out, in_), rd, wr, "d")
+
+    def ts(out, in0, s1, s2, o0, o1, rd, wr):
+        if o1 is None:
+            op("V", lambda: V.tensor_scalar(out, in0, s1, None, o0), rd, wr)
+        else:
+            op("V", lambda: V.tensor_scalar(out, in0, s1, s2, o0, o1), rd, wr)
+
+    def tt(out, a, b, o, rd, wr):
+        op("V", lambda: V.tensor_tensor(out, a, b, o), rd, wr)
+
+    def cp(out, a, rd, wr):
+        op("V", lambda: V.tensor_copy(out, a), rd, wr)
+
+    def act(out, a, f, bias, scale, rd, wr):
+        op("S", lambda: S.activation(out, a, f, bias=bias, scale=scale), rd, wr)
+
+    def mms(lst, rd, wr):
+        def fn():
+            ins = None
+            for n, (o, l, r) in enumerate(lst):
+                ins = P.matmul(o, l, r, n == 0, n == len(lst) - 1)
+            return ins
+        op("P", fn, rd, wr)
+
+    def send(src_of, dst_of, sem, ks, rd):
+        def fn(s):
+            tr = []
+            for k in ks:
+                rid, pid = topo.addr(hs[k], core)
+                tr.append(RemoteDMATransfer(dst_ids=[DstId(rid=rid, pnc=pid)], dma_engine_mask=mk[k], remote_sem=sem,
+                                            src=src_of(k), dst=dst_of(k)))
+            g.remote_dma_fused(tr, local_sem=s)
+            return sum(cnt[k] for k in ks)
+        op("G", fn, rd, [], "r")
+
+    dma("S", T.mm[:], T.mj[:], [], ["mm"])
+    dma("Y", T.cei[:], T.ce[:], [], ["cei"])
+    dma("S", T.tab[:, 0:1024], T.nx[:], [], ["nx"])
+    dma("Y", T.uz[:, 0:128], T.uu[0:8:2, :], [], ["u_a"])
+    dma("Y", T.uz[:, 128:256], T.uu[1:8:2, :], [], ["u_b"])
+    dma("Y", T.tab[:, 1024:2048], T.sg[:], [], ["sg"])
+    dma("S", T.tab[:, 2048:3072], T.al[:], [], ["al"])
+    dma("Y", T.uz[:, 256:384], T.zz[0:8:2, :], [], ["z_a"])
+    dma("Y", T.uz[:, 384:512], T.zz[1:8:2, :], [], ["z_b"])
+    dma("Y", T.rpi[:], T.rp[:], [], ["rpi"])
+
+    op("G", lambda: g.iota(T.qi[:], [[0, 8]], 0, 1), [], ["qi"])
+    op("G", lambda: g.iota(T.jj[:], [[1, 144]], 0, -1, allow_small_or_imprecise_dtypes=True), [], ["jj"])
+    op("G", lambda: g.iota(T.oi[:, 0:32], [[256, 2], [16, 8], [128, 2]], 0, 0), [], ["oi0"])
+    op("G", lambda: g.iota(T.oi[:, 32:40], [[2, 8]], 0, 0), [], ["oi1"])
+    op("G", lambda: g.iota(T.oi[:, 40:48], [[8, 2], [516, 2], [2, 2]], 16, 0), [], ["oi2"])
+    op("G", lambda: g.iota(T.xx[:], [[1, 16], [0, 16]], 0, 0, allow_small_or_imprecise_dtypes=True), [], ["xx"])
+    send(lambda k: T.tab[:, 768 * k:768 * (k + 1)], lambda k: T.rtab[:, 768 * k:768 * (k + 1)], T.sem.h_tab, range(4), ["nx", "sg", "al"])
+    send(lambda k: T.rpi[:, 64:96], lambda k: T.rrp[:], T.sem.h_rp, [0], ["rpi"])
+
+    op("V", lambda: V.memset(T.six[:], 0.0625), [], ["six"])
+    ts(T.qj[:, 0:1], T.qi[:, 0:1], 15, None, A.bitwise_and, None, ["qi"], ["qj0"])
+    ts(T.qj[:, 1:2], T.qi[:, 0:1], 112, None, A.bitwise_and, None, ["qi"], ["qj1"])
+    ts(T.qj[:, 2:3], T.qi[:, 0:1], 7, None, A.bitwise_and, None, ["qi"], ["qj2"])
+    ts(T.qj[:, 3:4], T.qi[:, 0:1], 3, 1, A.logical_shift_right, A.bitwise_and, ["qi"], ["qj3"])
+    cp(T.qf[:], T.qj[:], ["qj0", "qj1", "qj2", "qj3"], ["qf"])
+    ts(T.i2[:], T.jj[:, 0:128], 0.0, 2.0, A.is_equal, A.mult, ["jj"], ["i2"])
+    ts(T.big[:], T.jj[:, 0:16], T.qf[:, 1:2], 256.0, A.add, A.mult, ["jj", "qf"], ["big"])
+    ts(T.pp[:, 0:1], T.qf[:, 2:3], 32.0, T.qf[:, 3:4], A.mult, A.add, ["qf"], ["pp"])
+    ts(T.i1[:], T.jj[:, 0:128], 0.0, None, A.is_equal, None, ["jj"], ["i1"])
+    ts(T.o16[:, 0:32], T.oi[:, 0:32], T.qf[:, 0:1], None, A.add, None, ["oi0", "qf"], ["o1"])
+
+    def dms(a, b):
+        for i in range(a, b):
+            ts(T.dm[:, 128 * i:128 * (i + 1)], T.jj[:, 0:128], T.big[:, i:i + 1], None, A.is_equal, None, ["jj", "big"], ["dm%d" % i])
+    DM = ["dm%d" % i for i in range(16)]
+    ts(T.msk[:], T.big[:], 0.0, None, A.is_equal, None, ["big"], ["msk"])
+    dms(0, 9)
+    for i in range(9, 16):
+        act(T.dm[:, 128 * i:128 * (i + 1)], T.i1[:], AF.Copy, 0.0, T.msk[:, i:i + 1], ["i1", "msk"], ["dm%d" % i])
+    ts(T.o16[:, 32:48], T.oi[:, 32:48], T.pp[:, 0:1], None, A.add, None, ["oi1", "oi2", "pp"], ["o2"])
+    cp(T.ce16[:], T.cei[:], ["cei"], ["ce16"])
+
+    def pick(eng, out, src, rd, wr):
+        if eng == "S":
+            act(out, src, AF.Copy, 0.0, 1.0, rd, wr)
+        else:
+            cp(out, src, rd, wr)
+
+    def gather1(a, key, eng):
+        pick(eng, T.uz1[:, a:a + 256], T.uz[:, a:a + 256].indirect(T.o16[:, 0:16]), [key + "_a", key + "_b", "o1"], [key + "1"])
+
+    def turn(a, key):
+        op("V", lambda: V.transpose(T.uzt[:, a:a + 256], T.uz1[:, a:a + 256]), [key + "1"], [key + "t"])
+
+    def lists1(a, key, eng):
+        gather1(a, key, eng)
+        turn(a, key)
+
+    def lists2(a, key, lst, b, eng):
+        if b == 0:
+            pick(eng, lst[:, 0:128], T.uzt[:, a:a + 256].indirect(T.o16[:, 32:40]), [key + "t", "o2"], [key + "l0"])
+        else:
+            pick(eng, lst[:, 128:256], T.uzt[:, a:a + 768].indirect(T.o16[:, 40:48]), ["ut", "zt", "uzr0", "uzr1", "o2"], [key + "l1"])
+
+    psm, psr = [T.psm0, T.psm1], [T.psr0, T.psr1]
+
+    def tabs(t):
+        return (T.tab, "nx", "sg", "al", T.mm, "mm") if t < 2 else (T.rtab, "rtab", "rtab", "rtab", T.rm, "rm")
+
+    def cells(t):
+        if t == 0:
+            return T.cei[:], "cei", T.ce16, "ce16"
+        if t == 2:
+            return T.c2[:], "c2", T.c216, "c216"
+        return T["cn%d" % (t - 1)][:, 0:64], "cn%d" % (t - 1), T["co%d" % (t - 1)], "co%d" % (t - 1)
+
+    def g1(t, eng, a, b):
+        M, mk_ = tabs(t)[4:6]
+        c16, ck = cells(t)[2:4]
+        src = M[:].indirect(c16[:, a:b])
+        keys = ["ng%d" % h for h in range(a // 32, b // 32)]
+        if eng == "S":
+            act(T.ng[:, 16 * a:16 * b], src, AF.Relu, -0.0625, 1.0, [mk_, ck], keys)
+        else:
+            ts(T.ng[:, 16 * a:16 * b], src, -0.0625, 0.0, A.add, A.max, [mk_, ck], keys)
+
+    def g2(t):
+        tb, nk = tabs(t)[0:2]
+        c16, ck = cells(t)[2:4]
+        act(T.dg[:], tb[:, 0:1024].indirect(c16[:, 0:64]), AF.Copy, 0.0, 1.0, [nk, ck], ["dg"])
+
+    def ndense(t, h):
+        M, mk_ = tabs(t)[4:6]
+        act(T.nd[:, 512 * h:512 * (h + 1)], M[:, 512 * h:512 * (h + 1)], AF.Relu, -0.0625, 1.0, [mk_], ["nd%d" % h])
+
+    def pe_m(t, h):
+        if t == 0:
+            mms([(psm[h][:], T.i2[:], T.mm[:, 512 * h:512 * (h + 1)])], ["i2", "mm"], ["psm%d" % h])
+        else:
+            op("P", lambda: P.matmul(psm[h][:], T.i2[:], T.nd[:, 512 * h:512 * (h + 1)], False, True), ["i2", "nd%d" % h], ["psm%d" % h])
+
+    def pe_six(h):
+        op("P", lambda: P.matmul(psm[h][:], T.i2[:], T.six[:], True, False), ["i2", "six"], ["psm%d" % h])
+
+    def pe_a(t):
+        mms([(T.psa[:, 0:64], T.i1[:], T.six[:, 0:64])] +
+            [(T.psa[:, 0:64], T.dm[:, 128 * i:128 * (i + 1)], T.ng[:, i:1024:16]) for i in range(16)],
+            ["i1", "six", "ng0", "ng1"] + DM, ["psa"])
+
+    def v_a(t):
+        tt(T.xv[:], T.psa[:, 0:64], T.ul[:, 64 * t:64 * (t + 1)], A.mult, ["psa", "ul%d" % (t // 2)], ["xv"])
+        ts(T.v16[:], T.xv[:], 16.0, 255.0, A.mult, A.min, ["xv"], ["v16"])
+        tt(T.sel[:], T.oh[:].indirect(T.v16[:]), T.dg[:], A.mult, ["oh", "v16", "dg"], ["sel"])
+
+    def pe_b(t):
+        mms([(T.psb[:, 0:64], T.bw[:, 15 - i:143 - i], T.sel[:, i:1024:16]) for i in range(16)], ["bw", "sel"], ["psb"])
+
+    def pr(t, h):
+        return "psr%d" % (h + (2 if t == 0 else 0))
+
+    def rho(t, h):
+        tb, _, sk = tabs(t)[0:3]
+        tt(T[pr(t, h)][:], tb[:, 1024 + 512 * h:1536 + 512 * h], psm[h][:], A.mult, [sk, "psm%d" % h], [pr(t, h)])
+
+    def fnull(t, h):
+        act(T["ff%d" % t][:, 512 * h:512 * (h + 1)], T[pr(t, h)][:], AF.Identity, 2.0, -1.0, [pr(t, h)], ["fn%d_%d" % (t, h)])
+
+    def freal(t, h):
+        tb, ak = tabs(t)[0], tabs(t)[3]
+        tt(T["ff%d" % t][:, 1024 + 512 * h:1536 + 512 * h], tb[:, 2048 + 512 * h:2560 + 512 * h], T[pr(t, h)][:], A.mult,
+           [ak, pr(t, h)], ["fr%d_%d" % (t, h)])
+
+    def pe_sum(t, a, b):
+        op("P", lambda: P.matmul(T.psr2[:, a:b], T.i32[:], T["ww%d" % t][:, a:b], t == 0, t == 2 and b == 512),
+           ["i32", "w%d_0" % t], ["psr2"])
+
+    def v_b(t):
+        c, ck = cells(t)[0:2]
+        tt(T.yi[:], T.psb[:, 0:64], c, A.add, ["psb", ck], ["yi"])
+        ts(T.ib[:, 64:128], T.yi[:], 1023, None, A.bitwise_and, None, ["yi"], ["ibd"])
+        if t < 3:
+            ts(T.par[:], T.yi[:], 1, None, A.bitwise_and, None, ["yi"], ["par"])
+        cp(T.d16[:], T.ib[:, 64:128], ["ibd"], ["d16"])
+        if t < 3:
+            tt(T.ee[:], T.par[:, 16:48], T.v2[:, 32 * t:32 * (t + 1)], A.add, ["par", "v2_%d" % (t // 2)], ["ee"])
+            ts(T.ib[:, 0:64], T.yi[:], 1022, None, A.bitwise_and, None, ["yi"], ["ibe"])
+            cp(T.e16[:], T.ee[:], ["ee"], ["e16"])
+
+    def g4(t, a, b, keys, eng="S"):
+        src = T["ff%d" % t][:, 0:1024].indirect(T.d16[:, a:b])
+        rd = ["fn%d_0" % t, "fn%d_1" % t, "d16"]
+        if eng == "S":
+            act(T.rg[:, 16 * a:16 * b], src, AF.Identity, 256.0, -128.0, rd, keys)
+        else:
+            ts(T.rg[:, 16 * a:16 * b], src, -128.0, 256.0, A.mult, A.add, rd, keys)
+
+    def oldm(t, eng):
+        M, mk_ = tabs(t)[4:6]
+        if eng == "S":
+            act(T.old[:], M[:].indirect(T.e16[:]), AF.Copy, 0.0, 1.0, [mk_, "e16"], ["old"])
+        else:
+            cp(T.old[:], M[:].indirect(T.e16[:]), [mk_, "e16"], ["old"])
+
+    def fac(t):
+        ts(T.fac[:], T.rg[:, 256:768], 256.0, 0.5, A.is_le, A.max, ["rg1"], ["fac"])
+
+    def scat(t):
+        M, mk_ = tabs(t)[4:6]
+        tt(M[:].indirect(T.e16[:]), T.old[:], T.fac[:], A.mult, ["old", "fac", "e16"], [mk_])
+
+    def pe_c(t):
+        mms([(T.psa[:, 64:128], T.dm[:, 128 * i:128 * (i + 1)], T.rg[:, i:1024:16]) for i in range(16)], ["rg0", "rg1", "rg2"] + DM, ["psa"])
+
+    def v_r(t):
+        cn, co = T["cn%d" % t], T["co%d" % t]
+        tt(T.rr[:], T.psa[:, 64:128], T.zl[:, 64 * t:64 * (t + 1)], A.is_gt, ["psa", "zl%d" % (t // 2)], ["rr"])
+        if t < 3:
+            tt(T.rb[:, 0:64], T.rr[:], T.par[:], A.not_equal, ["rr", "par"], ["rbe"])
+        ts(T.rb[:, 64:128], T.rr[:], 1024.0, None, A.mult, None, ["rr"], ["rbd"])
+        if t < 3:
+            tt(cn[:, 0:64], T.ib[:, 0:64], T.rb[:, 0:64], A.add, ["ibe", "rbe"], ["cn%d" % t])
+        tt(cn[:, 64:128], T.ib[:, 64:128], T.rb[:, 64:128], A.add, ["ibd", "rbd"], ["on%d" % t])
+        if t in (0, 2):
+            cp(co[:, 0:64], cn[:, 0:64], ["cn%d" % t], ["co%d" % t])
+        if t == 1:
+            cp(T.c2[:, 0:32], T.cn1[:, 0:32], ["cn1"], ["c2c"])
+        cp(co[:, 64:128], cn[:, 64:128], ["on%d" % t], ["oo%d" % t])
+
+    def clip(t, a, b):
+        w = T["ww%d" % t]
+        keys = ["w%d_%d" % (t, h) for h in range(a // 512, b // 512)]
+        ts(w[:, a:b], w[:, a:b], 0.125, 4.0, A.max, A.min, keys, keys)
+
+    def weights(t, a, b):
+        w = T["ww%d" % t]
+        src = T["ff%d" % t][:].indirect(T["co%d" % t][:, 64 + a // 16:64 + b // 16])
+        rd = ["fn%d_0" % t, "fn%d_1" % t, "fr%d_0" % t, "fr%d_1" % t, "oo%d" % t]
+        keys = ["w%d_%d" % (t, h) for h in range(a // 512, b // 512)]
+        if t == 0:
+            ts(w[:, a:b], src, 0.125, 4.0, A.max, A.min, rd, keys)
+            return
+        if t == 2 and a == 512:
+            prev, pk = T.wr[:], ["wr0", "wr1"]
+        else:
+            prev, pk = T["ww%d" % (t - 1)][:, a:b], ["w%d_%d" % (t - 1, h) for h in range(a // 512, b // 512)]
+        tt(w[:, a:b], src, prev, A.mult, rd + pk, keys)
+
+    def out_hi(t):
+        w = T["ww%d" % t]
+        dma("G", T.tl[0:112, 512:1024], w[16:128, 512:1024], ["w%d_1" % t], ["tl1"], True)
+        dma("G", T.tl[112:128, 512:1024], w[0:16, 512:1024], ["w%d_1" % t], ["tl2"], True)
+
+    def reports(t, eng, fill):
+        g4(t, 16, 48, ["rg1"])
+        if eng == "S":
+            freal(t, 0)
+        oldm(t, eng)
+        fac(t)
+        if eng == "S":
+            freal(t, 1)
+        g4(t, 0, 16, ["rg0"])
+        g4(t, 48, 64, ["rg2"])
+        scat(t)
+        pe_c(t)
+
+    g1(0, "S", 0, 32)
+    g2(0)
+    pe_m(0, 0)
+    g1(0, "V", 32, 64)
+    pe_a(0)
+    pe_m(0, 1)
+    lists1(0, "u", "V")
+    ts(T.oh[:], T.xx[:], T.qf[:, 0:1], None, A.is_equal, None, ["xx", "qf"], ["oh"])
+    lists2(0, "u", T.ul, 0, "V")
+    ts(T.bw[:], T.jj[:], T.qf[:, 0:1], 15.0, A.add, A.is_equal, ["jj", "qf"], ["bw"])
+    v_a(0)
+    pe_b(0)
+    gather1(256, "z", "S")
+    rho(0, 0)
+    fnull(0, 0)
+    rho(0, 1)
+    fnull(0, 1)
+    ts(T.v2[:, 0:64], T.rpi[:, 0:64], 2.0, None, A.mult, None, ["rpi"], ["v2_0"])
+    v_b(0)
+    turn(256, "z")
+    dma("Y", T.uzt[16:128, 512:1024], T.uzt[0:112, 0:512], ["ut", "zt"], ["uzr0"])
+    dma("Y", T.uzt[0:16, 512:1024], T.uzt[112:128, 0:512], ["ut", "zt"], ["uzr1"])
+    reports(0, "V", None)
+    lists2(256, "z", T.zl, 0, "S")
+    pe_six(0)
+    ndense(1, 0)
+    v_r(0)
+    pe_m(1, 0)
+    g1(1, "S", 0, 32)
+    g1(1, "V", 32, 64)
+    g2(1)
+    pe_a(1)
+    pe_six(1)
+    rho(1, 0)
+    ndense(1, 1)
+    v_a(1)
+    pe_m(1, 1)
+    pe_b(1)
+    fnull(1, 0)
+    rho(1, 1)
+    fnull(1, 1)
+    freal(1, 0)
+    v_b(1)
+    reports(1, "V", None)
+    send(lambda k: T.mm[:, 256 * k:256 * (k + 1)], lambda k: T.rm[:, 256 * k:256 * (k + 1)], T.sem.h_m, range(4), ["mm"])
+    v_r(1)
+    dma("Y", T.c2[16:128, 32:64], T.cn1[0:112, 32:64], ["cn1"], ["c2a"])
+    dma("S", T.c2[0:16, 32:64], T.cn1[112:128, 32:64], ["cn1"], ["c2b"])
+    lists2(0, "u", T.ul, 1, "S")
+    lists2(256, "z", T.zl, 1, "S")
+    freal(0, 0)
+    freal(0, 1)
+    freal(1, 1)
+    pe_six(0)
+    pe_six(1)
+    cp(T.c216[:], T.c2[:], ["c2a", "c2b", "c2c"], ["c216", "c2"])
+    g2(2)
+    weights(0, 0, 1024)
+    ts(T.i32[:], T.jj[:, 0:128], 0.0, None, A.is_equal, None, ["jj"], ["i32"])
+    dma("Y", T.tl[:, 512:1024], T.ww0[:, 512:1024], ["w0_1"], ["tl1", "tl2"])
+    pe_sum(0, 0, 512)
+    weights(1, 512, 1024)
+    ts(T.v2[:, 64:96], T.rrp[:], 2.0, None, A.mult, None, ["rrp"], ["v2_1"])
+    clip(1, 512, 1024)
+    dma("Y", T.wr[16:128, :], T.ww1[0:112, 512:1024], ["w1_1"], ["wr0"])
+    dma("Y", T.wr[0:16, :], T.ww1[112:128, 512:1024], ["w1_1"], ["wr1"])
+    dma("G", T.tl[:, 512:1024], T.ww1[:, 512:1024], ["w1_1"], ["tl1", "tl2"], True)
+    g1(2, "S", 0, 32)
+    g1(2, "V", 32, 64)
+    ndense(2, 0)
+    ndense(2, 1)
+    pe_a(2)
+    weights(1, 0, 512)
+    clip(1, 0, 512)
+    pe_m(2, 0)
+    pe_m(2, 1)
+    v_a(2)
+    pe_b(2)
+    rho(2, 0)
+    fnull(2, 0)
+    rho(2, 1)
+    fnull(2, 1)
+    pe_sum(1, 0, 256)
+    v_b(2)
+    reports(2, "S", None)
+    pe_sum(1, 256, 512)
+    pe_six(0)
+    pe_six(1)
+    ndense(3, 0)
+    v_r(2)
+    pe_m(3, 0)
+    g1(3, "S", 0, 64)
+    g2(3)
+    pe_a(3)
+    weights(2, 0, 512)
+    weights(2, 512, 1024)
+    clip(2, 0, 1024)
+    out_hi(2)
+    ndense(3, 1)
+    v_a(3)
+    pe_sum(2, 0, 128)
+    pe_m(3, 1)
+    pe_b(3)
+    rho(3, 0)
+    fnull(3, 0)
+    rho(3, 1)
+    fnull(3, 1)
+    pe_sum(2, 128, 384)
+    v_b(3)
+    g4(3, 0, 32, ["rg0"], "V")
+    g4(3, 32, 64, ["rg1", "rg2"])
+    pe_c(3)
+    pe_sum(2, 384, 512)
+    freal(3, 0)
+    freal(3, 1)
+    v_r(3)
+    weights(3, 512, 1024)
+    clip(3, 512, 1024)
+    out_hi(3)
+    weights(3, 0, 512)
+    clip(3, 0, 512)
+    tt(T.fin[:], T.ww3[:, 0:512], T.psr2[:], A.add, ["w3_0", "psr2"], ["fin"])
+    dma("Y", T.tl[:, 0:512], T.fin[:], ["fin"], ["tl0"])
+    emit(g, T, ops, ext)

@@ -3,6 +3,8 @@ from concourse.mybir import AluOpType as A, ActivationFunctionType as AF
 
 SIM_CORES = 256
 HOP = 3
+MODE0 = 0
+MODE2 = 0
 
 SCRATCH = {
     "tab": ("sbuf", [128, 3072], "bfloat16"),
@@ -27,7 +29,14 @@ SCRATCH = {
     "oi": ("sbuf", [128, 48], "int32"),
     "o16": ("sbuf", [128, 48], "uint16"),
     "big": ("sbuf", [128, 16], "bfloat16"),
+    "m1": ("sbuf", [128, 1024], "bfloat16"),
+    "m3": ("sbuf", [128, 1024], "bfloat16"),
+    "fa0": ("sbuf", [128, 1024], "float32"),
+    "fa2": ("sbuf", [128, 1024], "float32"),
     "msk": ("sbuf", [128, 16], "float32"),
+    "re16": ("sbuf", [128, 32], "uint16"),
+    "rrg": ("sbuf", [128, 512], "bfloat16"),
+    "xr": ("sbuf", [128, 512], "float32"),
     "dm": ("sbuf", [128, 2048], "bfloat16"),
     "bw": ("sbuf", [128, 144], "bfloat16"),
     "i1": ("sbuf", [128, 128], "bfloat16"),
@@ -73,7 +82,7 @@ for _t in range(4):
     SCRATCH["co%d" % _t] = ("sbuf", [128, 128], "uint16")
 
 NDMA = 40
-SEMAPHORES = ["eV", "eS", "eP", "eG", "h_tab", "h_rp", "h_m", "a_tab", "a_rp", "a_m", "sent"] + ["d%d" % i for i in range(NDMA)]
+SEMAPHORES = ["eV", "eS", "eP", "eG", "h_tab", "h_rp", "h_m", "a_tab", "a_rp", "a_m", "h_e", "h_f", "a_e", "a_f", "sent"] + ["d%d" % i for i in range(NDMA)]
 
 
 def helpers(src, dst, T, topo):
@@ -101,15 +110,22 @@ def helper_program(g, core, src, dst, k, hs, T, topo):
     m = topo.mask(core, dst)
     n = len(topo.engines(core, dst))
     sent = 0
-    g.wait_ge(T.sem.h_tab, cnt[k])
-    g.remote_dma(T.rtab[:, 768 * k:768 * (k + 1)], T.rtab[:, 768 * k:768 * (k + 1)], T.sem.a_tab, T.sem.sent, pid, rid, m)
-    sent += n
     if k == 0:
         g.wait_ge(T.sem.h_rp, cnt[k])
         g.remote_dma(T.rrp[:], T.rrp[:], T.sem.a_rp, T.sem.sent, pid, rid, m)
         sent += n
+    g.wait_ge(T.sem.h_tab, cnt[k])
+    g.remote_dma(T.rtab[:, 768 * k:768 * (k + 1)], T.rtab[:, 768 * k:768 * (k + 1)], T.sem.a_tab, T.sem.sent, pid, rid, m)
+    sent += n
     g.wait_ge(T.sem.h_m, cnt[k])
     g.remote_dma(T.rm[:, 256 * k:256 * (k + 1)], T.rm[:, 256 * k:256 * (k + 1)], T.sem.a_m, T.sem.sent, pid, rid, m)
+    sent += n
+    if k == 0:
+        g.wait_ge(T.sem.h_e, cnt[k])
+        g.remote_dma(T.re16[:], T.re16[:], T.sem.a_e, T.sem.sent, pid, rid, m)
+        sent += n
+    g.wait_ge(T.sem.h_f, cnt[k])
+    g.remote_dma(T.rrg[:, 128 * k:128 * (k + 1)], T.rrg[:, 128 * k:128 * (k + 1)], T.sem.a_f, T.sem.sent, pid, rid, m)
     sent += n
     g.wait_ge(T.sem.sent, sent)
 
@@ -193,7 +209,8 @@ def rank_program(g, core, T, topo):
     mk, cnt = masks(core, hs, topo)
     hin = helpers(T.cores[(rank + HOP) % N], core, T, topo)
     nin = [len(topo.engines(h, core)) for h in hin]
-    ext = {"rtab": ("a_tab", sum(nin)), "rrp": ("a_rp", nin[0]), "rm": ("a_m", sum(nin))}
+    ext = {"rtab": ("a_tab", sum(nin)), "rrp": ("a_rp", nin[0]), "rm": ("a_m", sum(nin)),
+           "re16": ("a_e", nin[0]), "rrg": ("a_f", sum(nin))}
 
     ops = []
     V, S, P = g.vector, g.scalar, g.tensor
@@ -247,11 +264,11 @@ def rank_program(g, core, T, topo):
     dma("S", T.tab[:, 0:1024], T.nx[:], [], ["nx"])
     dma("Y", T.uz[:, 0:128], T.uu[0:8:2, :], [], ["u_a"])
     dma("Y", T.uz[:, 128:256], T.uu[1:8:2, :], [], ["u_b"])
+    dma("Y", T.rpi[:], T.rp[:], [], ["rpi"])
     dma("Y", T.tab[:, 1024:2048], T.sg[:], [], ["sg"])
     dma("S", T.tab[:, 2048:3072], T.al[:], [], ["al"])
     dma("Y", T.uz[:, 256:384], T.zz[0:8:2, :], [], ["z_a"])
     dma("Y", T.uz[:, 384:512], T.zz[1:8:2, :], [], ["z_b"])
-    dma("Y", T.rpi[:], T.rp[:], [], ["rpi"])
 
     op("G", lambda: g.iota(T.qi[:], [[0, 8]], 0, 1), [], ["qi"])
     op("G", lambda: g.iota(T.jj[:], [[1, 144]], 0, -1, allow_small_or_imprecise_dtypes=True), [], ["jj"])
@@ -259,10 +276,15 @@ def rank_program(g, core, T, topo):
     op("G", lambda: g.iota(T.oi[:, 32:40], [[2, 8]], 0, 0), [], ["oi1"])
     op("G", lambda: g.iota(T.oi[:, 40:48], [[8, 2], [516, 2], [2, 2]], 16, 0), [], ["oi2"])
     op("G", lambda: g.iota(T.xx[:], [[1, 16], [0, 16]], 0, 0, allow_small_or_imprecise_dtypes=True), [], ["xx"])
-    send(lambda k: T.tab[:, 768 * k:768 * (k + 1)], lambda k: T.rtab[:, 768 * k:768 * (k + 1)], T.sem.h_tab, range(4), ["nx", "sg", "al"])
+    if MODE0 and MODE2:
+        op("G", lambda: g.iota(T.fa2[:], [[0, 1024]], 1, 0, allow_small_or_imprecise_dtypes=True), [], ["fa2_0", "fa2_1"])
     send(lambda k: T.rpi[:, 64:96], lambda k: T.rrp[:], T.sem.h_rp, [0], ["rpi"])
+    send(lambda k: T.tab[:, 768 * k:768 * (k + 1)], lambda k: T.rtab[:, 768 * k:768 * (k + 1)], T.sem.h_tab, range(4), ["nx", "sg", "al"])
 
-    op("V", lambda: V.memset(T.six[:], 0.0625), [], ["six"])
+    op("V", lambda: V.memset(T.six[:], 0.125), [], ["six"])
+    ft = 0 if MODE0 else 2
+    for h in range(2 if MODE0 or MODE2 else 0):
+        act(T["fa%d" % ft][:, 512 * h:512 * (h + 1)], T.six[:], AF.Sigmoid, 0.0, 800.0, ["six"], ["fa%d_%d" % (ft, h)])
     ts(T.qj[:, 0:1], T.qi[:, 0:1], 15, None, A.bitwise_and, None, ["qi"], ["qj0"])
     ts(T.qj[:, 1:2], T.qi[:, 0:1], 112, None, A.bitwise_and, None, ["qi"], ["qj1"])
     ts(T.qj[:, 2:3], T.qi[:, 0:1], 7, None, A.bitwise_and, None, ["qi"], ["qj2"])
@@ -285,9 +307,9 @@ def rank_program(g, core, T, topo):
     ts(T.o16[:, 32:48], T.oi[:, 32:48], T.pp[:, 0:1], None, A.add, None, ["oi1", "oi2", "pp"], ["o2"])
     cp(T.ce16[:], T.cei[:], ["cei"], ["ce16"])
 
-    def pick(eng, out, src, rd, wr):
+    def pick(eng, out, src, rd, wr, scale=1.0):
         if eng == "S":
-            act(out, src, AF.Copy, 0.0, 1.0, rd, wr)
+            act(out, src, AF.Copy, 0.0, scale, rd, wr)
         else:
             cp(out, src, rd, wr)
 
@@ -302,15 +324,17 @@ def rank_program(g, core, T, topo):
         turn(a, key)
 
     def lists2(a, key, lst, b, eng):
+        sc = -1.0 if key == "z" else 1.0
         if b == 0:
-            pick(eng, lst[:, 0:128], T.uzt[:, a:a + 256].indirect(T.o16[:, 32:40]), [key + "t", "o2"], [key + "l0"])
+            pick(eng, lst[:, 0:128], T.uzt[:, a:a + 256].indirect(T.o16[:, 32:40]), [key + "t", "o2"], [key + "l0"], sc)
         else:
-            pick(eng, lst[:, 128:256], T.uzt[:, a:a + 768].indirect(T.o16[:, 40:48]), ["ut", "zt", "uzr0", "uzr1", "o2"], [key + "l1"])
+            pick(eng, lst[:, 128:256], T.uzt[:, a:a + 768].indirect(T.o16[:, 40:48]), ["ut", "zt", "uzr0", "uzr1", "o2"], [key + "l1"], sc)
 
     psm, psr = [T.psm0, T.psm1], [T.psr0, T.psr1]
 
     def tabs(t):
-        return (T.tab, "nx", "sg", "al", T.mm, "mm") if t < 2 else (T.rtab, "rtab", "rtab", "rtab", T.rm, "rm")
+        mk_ = ("mm", "m1", "rm", "m3" if MODE2 else "rm")[t]
+        return (T.tab, "nx", "sg", "al", T[mk_], mk_) if t < 2 else (T.rtab, "rtab", "rtab", "rtab", T[mk_], mk_)
 
     def cells(t):
         if t == 0:
@@ -325,27 +349,29 @@ def rank_program(g, core, T, topo):
         src = M[:].indirect(c16[:, a:b])
         keys = ["ng%d" % h for h in range(a // 32, b // 32)]
         if eng == "S":
-            act(T.ng[:, 16 * a:16 * b], src, AF.Relu, -0.0625, 1.0, [mk_, ck], keys)
+            act(T.ng[:, 16 * a:16 * b], src, AF.Relu, -0.125, 2.0 if t == 0 else 1.0, [mk_, ck], keys)
+        elif t == 0:
+            ts(T.ng[:, 16 * a:16 * b], src, 2.0, -0.125, A.mult, A.add, [mk_, ck], keys)
         else:
-            ts(T.ng[:, 16 * a:16 * b], src, -0.0625, 0.0, A.add, A.max, [mk_, ck], keys)
+            ts(T.ng[:, 16 * a:16 * b], src, -0.125, 0.0, A.add, A.max, [mk_, ck], keys)
 
-    def g2(t):
+    def g2(t, eng="S", a=0, b=64):
         tb, nk = tabs(t)[0:2]
         c16, ck = cells(t)[2:4]
-        act(T.dg[:], tb[:, 0:1024].indirect(c16[:, 0:64]), AF.Copy, 0.0, 1.0, [nk, ck], ["dg"])
+        pick(eng, T.dg[:, 16 * a:16 * b], tb[:, 0:1024].indirect(c16[:, a:b]), [nk, ck], ["dg%d" % h for h in range(a // 16, b // 16)])
 
     def ndense(t, h):
         M, mk_ = tabs(t)[4:6]
-        act(T.nd[:, 512 * h:512 * (h + 1)], M[:, 512 * h:512 * (h + 1)], AF.Relu, -0.0625, 1.0, [mk_], ["nd%d" % h])
+        act(T.nd[:, 512 * h:512 * (h + 1)], M[:, 512 * h:512 * (h + 1)], AF.Relu, -0.125, 1.0, [mk_ + "h%d" % h if (0, MODE0, 0, MODE2)[t] else mk_], ["nd%d" % h])
 
     def pe_m(t, h):
         if t == 0:
             mms([(psm[h][:], T.i2[:], T.mm[:, 512 * h:512 * (h + 1)])], ["i2", "mm"], ["psm%d" % h])
         else:
-            op("P", lambda: P.matmul(psm[h][:], T.i2[:], T.nd[:, 512 * h:512 * (h + 1)], False, True), ["i2", "nd%d" % h], ["psm%d" % h])
+            op("P", lambda: P.matmul(psm[h][:], T.i1[:], T.nd[:, 512 * h:512 * (h + 1)], False, True), ["i1", "nd%d" % h], ["psm%d" % h])
 
     def pe_six(h):
-        op("P", lambda: P.matmul(psm[h][:], T.i2[:], T.six[:], True, False), ["i2", "six"], ["psm%d" % h])
+        op("P", lambda: P.matmul(psm[h][:], T.i1[:], T.six[:], True, False), ["i1", "six"], ["psm%d" % h])
 
     def pe_a(t):
         mms([(T.psa[:, 0:64], T.i1[:], T.six[:, 0:64])] +
@@ -354,8 +380,8 @@ def rank_program(g, core, T, topo):
 
     def v_a(t):
         tt(T.xv[:], T.psa[:, 0:64], T.ul[:, 64 * t:64 * (t + 1)], A.mult, ["psa", "ul%d" % (t // 2)], ["xv"])
-        ts(T.v16[:], T.xv[:], 16.0, 255.0, A.mult, A.min, ["xv"], ["v16"])
-        tt(T.sel[:], T.oh[:].indirect(T.v16[:]), T.dg[:], A.mult, ["oh", "v16", "dg"], ["sel"])
+        ts(T.v16[:], T.xv[:], 8.0, 255.0, A.mult, A.min, ["xv"], ["v16"])
+        tt(T.sel[:], T.oh[:].indirect(T.v16[:]), T.dg[:], A.mult, ["oh", "v16", "dg0", "dg1", "dg2", "dg3"], ["sel"])
 
     def pe_b(t):
         mms([(T.psb[:, 0:64], T.bw[:, 15 - i:143 - i], T.sel[:, i:1024:16]) for i in range(16)], ["bw", "sel"], ["psb"])
@@ -400,7 +426,7 @@ def rank_program(g, core, T, topo):
             ts(T.rg[:, 16 * a:16 * b], src, -128.0, 256.0, A.mult, A.add, rd, keys)
 
     def oldm(t, eng):
-        M, mk_ = tabs(t)[4:6]
+        M, mk_ = tabs(max(t, 1))[4:6]
         if eng == "S":
             act(T.old[:], M[:].indirect(T.e16[:]), AF.Copy, 0.0, 1.0, [mk_, "e16"], ["old"])
         else:
@@ -410,18 +436,26 @@ def rank_program(g, core, T, topo):
         ts(T.fac[:], T.rg[:, 256:768], 256.0, 0.5, A.is_le, A.max, ["rg1"], ["fac"])
 
     def scat(t):
-        M, mk_ = tabs(t)[4:6]
+        M, mk_ = tabs(max(t, 1))[4:6]
         tt(M[:].indirect(T.e16[:]), T.old[:], T.fac[:], A.mult, ["old", "fac", "e16"], [mk_])
 
     def pe_c(t):
-        mms([(T.psa[:, 64:128], T.dm[:, 128 * i:128 * (i + 1)], T.rg[:, i:1024:16]) for i in range(16)], ["rg0", "rg1", "rg2"] + DM, ["psa"])
+        op("P", lambda: P.matmul(T.psa[:, 64:128], T.i1[:], T.zl[:, 64 * t:64 * (t + 1)], True, False), ["i1", "zl%d" % (t // 2)], ["psa"])
+
+        def fn():
+            ins = None
+            for i in range(16):
+                ins = P.matmul(T.psa[:, 64:128], T.dm[:, 128 * i:128 * (i + 1)], T.rg[:, i:1024:16], False, i == 15)
+            return ins
+        op("P", fn, ["rg0", "rg1", "rg2"] + DM, ["psa"])
 
     def v_r(t):
         cn, co = T["cn%d" % t], T["co%d" % t]
-        tt(T.rr[:], T.psa[:, 64:128], T.zl[:, 64 * t:64 * (t + 1)], A.is_gt, ["psa", "zl%d" % (t // 2)], ["rr"])
+        if t < 3:
+            ts(T.rr[:], T.psa[:, 64:128], 0.0, None, A.is_gt, None, ["psa"], ["rr"])
+        ts(T.rb[:, 64:128], T.psa[:, 64:128], 0.0, 1024.0, A.is_gt, A.mult, ["psa"], ["rbd"])
         if t < 3:
             tt(T.rb[:, 0:64], T.rr[:], T.par[:], A.not_equal, ["rr", "par"], ["rbe"])
-        ts(T.rb[:, 64:128], T.rr[:], 1024.0, None, A.mult, None, ["rr"], ["rbd"])
         if t < 3:
             tt(cn[:, 0:64], T.ib[:, 0:64], T.rb[:, 0:64], A.add, ["ibe", "rbe"], ["cn%d" % t])
         tt(cn[:, 64:128], T.ib[:, 64:128], T.rb[:, 64:128], A.add, ["ibd", "rbd"], ["on%d" % t])
@@ -435,6 +469,16 @@ def rank_program(g, core, T, topo):
         w = T["ww%d" % t]
         keys = ["w%d_%d" % (t, h) for h in range(a // 512, b // 512)]
         ts(w[:, a:b], w[:, a:b], 0.125, 4.0, A.max, A.min, keys, keys)
+
+    def sclip(t, a, b, k):
+        w = T["ww%d" % t]
+        keys = ["w%d_%d" % (t, h) for h in range(a // 512, b // 512)]
+        if k == 0 and t == 0:
+            src = T.ff0[:].indirect(T.co0[:, 64 + a // 16:64 + b // 16])
+            act(w[:, a:b], src, AF.Relu, 4.0, -1.0, ["fn0_0", "fn0_1", "fr0_0", "fr0_1", "oo0"], keys)
+        else:
+            f, bias, scale = ((AF.Relu, 4.0, -1.0), (AF.Relu, 3.875, -1.0), (AF.Identity, 0.125, 1.0))[k]
+            act(w[:, a:b], w[:, a:b], f, bias, scale, keys, keys)
 
     def weights(t, a, b):
         w = T["ww%d" % t]
@@ -454,6 +498,19 @@ def rank_program(g, core, T, topo):
         w = T["ww%d" % t]
         dma("G", T.tl[0:112, 512:1024], w[16:128, 512:1024], ["w%d_1" % t], ["tl1"], True)
         dma("G", T.tl[112:128, 512:1024], w[0:16, 512:1024], ["w%d_1" % t], ["tl2"], True)
+
+    def reports_s(t):
+        fa, fk = T["fa%d" % t], ["fa%d_0" % t, "fa%d_1" % t]
+        act(T.xr[:], T["ff%d" % t][:, 0:1024].indirect(T.d16[:, 16:48]), AF.Relu, 128.0, 2048.0, ["fn%d_0" % t, "fn%d_1" % t, "d16"], ["xr"])
+        op("S", lambda: S.activation(fa[:].indirect(T.e16[:]), T.xr[:], AF.Sigmoid), ["xr", "e16"], fk)
+        g4(t, 0, 64, ["rg0", "rg1", "rg2"], "V")
+        pe_c(t)
+        freal(t, 0)
+        freal(t, 1)
+
+    def dense(t, h):
+        M, mk_ = tabs(t + 1)[4:6]
+        tt(M[:, 512 * h:512 * (h + 1)], T["fa%d" % t][:, 512 * h:512 * (h + 1)], psm[h][:], A.mult, ["fa%d_%d" % (t, h), "psm%d" % h], [mk_ + "h%d" % h] + [mk_] * h)
 
     def reports(t, eng, fill):
         g4(t, 16, 48, ["rg1"])
@@ -481,106 +538,183 @@ def rank_program(g, core, T, topo):
     v_a(0)
     pe_b(0)
     gather1(256, "z", "S")
+    if not MODE0:
+        act(T.m1[:], T.mm[:], AF.Copy, 0.0, 2.0, ["mm"], ["m1"])
     rho(0, 0)
     fnull(0, 0)
     rho(0, 1)
     fnull(0, 1)
     ts(T.v2[:, 0:64], T.rpi[:, 0:64], 2.0, None, A.mult, None, ["rpi"], ["v2_0"])
-    v_b(0)
     turn(256, "z")
+    lists2(256, "z", T.zl, 0, "S")
+    v_b(0)
     dma("Y", T.uzt[16:128, 512:1024], T.uzt[0:112, 0:512], ["ut", "zt"], ["uzr0"])
     dma("Y", T.uzt[0:16, 512:1024], T.uzt[112:128, 0:512], ["ut", "zt"], ["uzr1"])
-    reports(0, "V", None)
-    lists2(256, "z", T.zl, 0, "S")
-    pe_six(0)
-    ndense(1, 0)
-    v_r(0)
-    pe_m(1, 0)
-    g1(1, "S", 0, 32)
-    g1(1, "V", 32, 64)
-    g2(1)
-    pe_a(1)
-    pe_six(1)
-    rho(1, 0)
-    ndense(1, 1)
-    v_a(1)
-    pe_m(1, 1)
-    pe_b(1)
-    fnull(1, 0)
-    rho(1, 1)
-    fnull(1, 1)
+    if MODE0:
+        reports_s(0)
+        v_r(0)
+        g2(1, "S", 0, 32)
+        dense(0, 0)
+        dense(0, 1)
+        pe_six(0)
+        g1(1, "S", 0, 32)
+        g1(1, "V", 32, 64)
+        pe_a(1)
+        g2(1, "S", 32, 64)
+        pe_six(1)
+        weights(0, 0, 512)
+        ndense(1, 0)
+        ndense(1, 1)
+        v_a(1)
+        pe_m(1, 0)
+        pe_m(1, 1)
+        pe_b(1)
+        rho(1, 0)
+        fnull(1, 0)
+        rho(1, 1)
+        fnull(1, 1)
+        v_b(1)
+        reports(1, "V", None)
+        lo0 = 512
+    else:
+        reports(0, "V", None)
+        send(lambda k: T.m1[:, 256 * k:256 * (k + 1)], lambda k: T.rm[:, 256 * k:256 * (k + 1)], T.sem.h_m, range(4), ["m1"])
+        pe_six(0)
+        ndense(1, 0)
+        v_r(0)
+        pe_m(1, 0)
+        g1(1, "S", 0, 32)
+        g1(1, "V", 32, 64)
+        g2(1)
+        pe_a(1)
+        pe_six(1)
+        rho(1, 0)
+        freal(0, 0)
+        ndense(1, 1)
+        v_a(1)
+        pe_m(1, 1)
+        pe_b(1)
+        fnull(1, 0)
+        rho(1, 1)
+        fnull(1, 1)
+        freal(0, 1)
+        v_b(1)
+        lo0 = 512
+    send(lambda k: T.e16[:], lambda k: T.re16[:], T.sem.h_e, [0], ["e16"])
+    g4(1, 16, 48, ["rg1"])
+    send(lambda k: T.rg[:, 256 + 128 * k:384 + 128 * k], lambda k: T.rrg[:, 128 * k:128 * (k + 1)], T.sem.h_f, range(4), ["rg1"])
+    g4(1, 0, 16, ["rg0"], "V")
+    g4(1, 48, 64, ["rg2"], "V")
+    pe_c(1)
     freal(1, 0)
-    v_b(1)
-    reports(1, "V", None)
-    send(lambda k: T.mm[:, 256 * k:256 * (k + 1)], lambda k: T.rm[:, 256 * k:256 * (k + 1)], T.sem.h_m, range(4), ["mm"])
+    freal(1, 1)
+    sclip(0, lo0, 1024, 0)
     v_r(1)
     dma("Y", T.c2[16:128, 32:64], T.cn1[0:112, 32:64], ["cn1"], ["c2a"])
-    dma("S", T.c2[0:16, 32:64], T.cn1[112:128, 32:64], ["cn1"], ["c2b"])
+    dma("Y", T.c2[0:16, 32:64], T.cn1[112:128, 32:64], ["cn1"], ["c2b"])
+    sclip(0, lo0, 1024, 1)
+    sclip(0, lo0, 1024, 2)
     lists2(0, "u", T.ul, 1, "S")
     lists2(256, "z", T.zl, 1, "S")
-    freal(0, 0)
-    freal(0, 1)
-    freal(1, 1)
+    sclip(0, 0, 512, 0)
+    act(T.old[:], T.rm[:].indirect(T.re16[:]), AF.Copy, 0.0, 1.0, ["rm", "re16"], ["old"])
+    sclip(0, 0, 512, 1)
+    sclip(0, 0, 512, 2)
     pe_six(0)
     pe_six(1)
-    cp(T.c216[:], T.c2[:], ["c2a", "c2b", "c2c"], ["c216", "c2"])
-    g2(2)
-    weights(0, 0, 1024)
-    ts(T.i32[:], T.jj[:, 0:128], 0.0, None, A.is_equal, None, ["jj"], ["i32"])
     dma("Y", T.tl[:, 512:1024], T.ww0[:, 512:1024], ["w0_1"], ["tl1", "tl2"])
-    pe_sum(0, 0, 512)
     weights(1, 512, 1024)
-    ts(T.v2[:, 64:96], T.rrp[:], 2.0, None, A.mult, None, ["rrp"], ["v2_1"])
+    ts(T.i32[:], T.jj[:, 0:128], 0.0, None, A.is_equal, None, ["jj"], ["i32"])
     clip(1, 512, 1024)
+    ts(T.v2[:, 64:96], T.rrp[:], 2.0, None, A.mult, None, ["rrp"], ["v2_1"])
+    cp(T.c216[:], T.c2[:], ["c2a", "c2b", "c2c"], ["c216", "c2"])
+    g2(2, "S", 0, 32)
+    ts(T.fac[:], T.rrg[:], 256.0, 0.5, A.is_le, A.max, ["rrg"], ["fac"])
+    tt(T.rm[:].indirect(T.re16[:]), T.old[:], T.fac[:], A.mult, ["old", "fac", "re16"], ["rm"])
     dma("Y", T.wr[16:128, :], T.ww1[0:112, 512:1024], ["w1_1"], ["wr0"])
     dma("Y", T.wr[0:16, :], T.ww1[112:128, 512:1024], ["w1_1"], ["wr1"])
     dma("G", T.tl[:, 512:1024], T.ww1[:, 512:1024], ["w1_1"], ["tl1", "tl2"], True)
     g1(2, "S", 0, 32)
     g1(2, "V", 32, 64)
+    g2(2, "S", 32, 64)
     ndense(2, 0)
     ndense(2, 1)
     pe_a(2)
     weights(1, 0, 512)
-    clip(1, 0, 512)
     pe_m(2, 0)
     pe_m(2, 1)
     v_a(2)
+    sclip(1, 0, 512, 0)
+    sclip(1, 0, 512, 1)
     pe_b(2)
     rho(2, 0)
     fnull(2, 0)
     rho(2, 1)
     fnull(2, 1)
-    pe_sum(1, 0, 256)
+    pe_sum(0, 0, 512)
     v_b(2)
-    reports(2, "S", None)
-    pe_sum(1, 256, 512)
-    pe_six(0)
-    pe_six(1)
-    ndense(3, 0)
-    v_r(2)
-    pe_m(3, 0)
-    g1(3, "S", 0, 64)
-    g2(3)
-    pe_a(3)
-    weights(2, 0, 512)
-    weights(2, 512, 1024)
-    clip(2, 0, 1024)
-    out_hi(2)
-    ndense(3, 1)
-    v_a(3)
-    pe_sum(2, 0, 128)
-    pe_m(3, 1)
-    pe_b(3)
-    rho(3, 0)
-    fnull(3, 0)
+    if MODE2:
+        reports_s(2)
+        pe_sum(1, 256, 512)
+        v_r(2)
+        g2(3, "S", 0, 32)
+        dense(2, 0)
+        dense(2, 1)
+        pe_six(0)
+        pe_six(1)
+        g1(3, "S", 0, 64)
+        pe_a(3)
+        g2(3, "S", 32, 64)
+        weights(2, 512, 1024)
+        weights(2, 0, 512)
+        clip(2, 512, 1024)
+        out_hi(2)
+        ndense(3, 0)
+        ndense(3, 1)
+        v_a(3)
+        pe_m(3, 0)
+        pe_m(3, 1)
+        sclip(2, 0, 512, 0)
+        pe_b(3)
+        rho(3, 0)
+        sclip(2, 0, 512, 1)
+        sclip(2, 0, 512, 2)
+        fnull(3, 0)
+    else:
+        reports(2, "S", None)
+        sclip(1, 0, 512, 2)
+        pe_six(0)
+        pe_sum(1, 0, 256)
+        ndense(3, 0)
+        v_r(2)
+        pe_m(3, 0)
+        g1(3, "S", 0, 64)
+        g2(3, "S", 0, 48)
+        pe_a(3)
+        pe_six(1)
+        pe_sum(1, 256, 512)
+        weights(2, 512, 1024)
+        weights(2, 0, 512)
+        clip(2, 512, 1024)
+        out_hi(2)
+        g2(3, "V", 48, 64)
+        ndense(3, 1)
+        v_a(3)
+        sclip(2, 0, 512, 0)
+        sclip(2, 0, 512, 1)
+        pe_m(3, 1)
+        pe_b(3)
+        rho(3, 0)
+        sclip(2, 0, 512, 2)
+        fnull(3, 0)
     rho(3, 1)
     fnull(3, 1)
-    pe_sum(2, 128, 384)
+    pe_sum(2, 0, 256)
     v_b(3)
     g4(3, 0, 32, ["rg0"], "V")
     g4(3, 32, 64, ["rg1", "rg2"])
     pe_c(3)
-    pe_sum(2, 384, 512)
+    pe_sum(2, 256, 512)
     freal(3, 0)
     freal(3, 1)
     v_r(3)

@@ -3,8 +3,7 @@ from concourse.mybir import AluOpType as A, ActivationFunctionType as AF
 
 SIM_CORES = 256
 HOP = 3
-MODE0 = 0
-MODE2 = 0
+KK = 98304.0
 
 SCRATCH = {
     "tab": ("sbuf", [128, 3072], "bfloat16"),
@@ -15,34 +14,34 @@ SCRATCH = {
     "rrp": ("sbuf", [128, 32], "int32"),
     "v2": ("sbuf", [128, 96], "int32"),
     "cei": ("sbuf", [128, 64], "int32"),
-    "uz": ("sbuf", [128, 512], "bfloat16"),
-    "uz1": ("sbuf", [128, 512], "bfloat16"),
-    "uzt": ("sbuf", [128, 1024], "bfloat16"),
+    "ce16": ("sbuf", [128, 64], "uint16"),
+    "cf": ("sbuf", [128, 64], "float32"),
+    "us": ("sbuf", [128, 1024], "bfloat16"),
+    "zs": ("sbuf", [128, 1024], "bfloat16"),
     "ul": ("sbuf", [128, 256], "bfloat16"),
-    "zl": ("sbuf", [128, 256], "bfloat16"),
     "qi": ("sbuf", [128, 8], "int32"),
-    "qj": ("sbuf", [128, 4], "int32"),
     "qf": ("sbuf", [128, 4], "float32"),
-    "pp": ("sbuf", [128, 4], "float32"),
+    "col": ("sbuf", [128, 4], "float32"),
     "jj": ("sbuf", [128, 144], "bfloat16"),
-    "xx": ("sbuf", [128, 256], "bfloat16"),
-    "oi": ("sbuf", [128, 48], "int32"),
-    "o16": ("sbuf", [128, 48], "uint16"),
     "big": ("sbuf", [128, 16], "bfloat16"),
-    "m1": ("sbuf", [128, 1024], "bfloat16"),
-    "m3": ("sbuf", [128, 1024], "bfloat16"),
-    "fa0": ("sbuf", [128, 1024], "float32"),
-    "fa2": ("sbuf", [128, 1024], "float32"),
     "msk": ("sbuf", [128, 16], "float32"),
-    "re16": ("sbuf", [128, 32], "uint16"),
-    "rrg": ("sbuf", [128, 512], "bfloat16"),
-    "xr": ("sbuf", [128, 512], "float32"),
+    "kt": ("sbuf", [128, 512], "bfloat16"),
+    "six": ("sbuf", [128, 64], "bfloat16"),
+    "k2": ("sbuf", [128, 64], "bfloat16"),
+    "cc": ("sbuf", [128, 64], "float32"),
     "dm": ("sbuf", [128, 2048], "bfloat16"),
+    "bc": ("sbuf", [128, 2048], "bfloat16"),
     "bw": ("sbuf", [128, 144], "bfloat16"),
+    "ew": ("sbuf", [128, 144], "bfloat16"),
+    "ez": ("sbuf", [128, 144], "bfloat16"),
     "i1": ("sbuf", [128, 128], "bfloat16"),
     "i2": ("sbuf", [128, 128], "bfloat16"),
-    "oh": ("sbuf", [128, 256], "bfloat16"),
-    "six": ("sbuf", [128, 512], "bfloat16"),
+    "dk": ("sbuf", [128, 128], "bfloat16"),
+    "i32": ("sbuf", [128, 128], "float32"),
+    "sq": ("sbuf", [128, 128], "float32"),
+    "s32": ("sbuf", [128, 128], "float32"),
+    "re16": ("sbuf", [128, 32], "uint16"),
+    "rfac": ("sbuf", [128, 512], "bfloat16"),
     "ng": ("sbuf", [128, 1024], "bfloat16"),
     "dg": ("sbuf", [128, 1024], "bfloat16"),
     "sel": ("sbuf", [128, 1024], "bfloat16"),
@@ -51,37 +50,30 @@ SCRATCH = {
     "old": ("sbuf", [128, 512], "bfloat16"),
     "fac": ("sbuf", [128, 512], "bfloat16"),
     "xv": ("sbuf", [128, 64], "float32"),
-    "v16": ("sbuf", [128, 64], "uint16"),
+    "pb": ("sbuf", [128, 64], "bfloat16"),
     "yi": ("sbuf", [128, 64], "int32"),
     "ib": ("sbuf", [128, 128], "int32"),
     "par": ("sbuf", [128, 64], "int32"),
+    "sn": ("sbuf", [128, 64], "float32"),
     "ee": ("sbuf", [128, 32], "int32"),
     "d16": ("sbuf", [128, 64], "uint16"),
     "e16": ("sbuf", [128, 32], "uint16"),
-    "rr": ("sbuf", [128, 64], "int32"),
     "rb": ("sbuf", [128, 128], "int32"),
     "c2": ("sbuf", [128, 64], "float32"),
     "c216": ("sbuf", [128, 64], "uint16"),
-    "ce16": ("sbuf", [128, 64], "uint16"),
+    "fl": ("sbuf", [128, 2048], "float32"),
     "wr": ("sbuf", [128, 512], "float32"),
-    "psa": ("psum", [128, 512], "float32"),
-    "psb": ("psum", [128, 512], "float32"),
-    "psm0": ("psum", [128, 512], "float32"),
-    "psm1": ("psum", [128, 512], "float32"),
-    "psr0": ("psum", [128, 512], "float32"),
-    "psr1": ("psum", [128, 512], "float32"),
-    "psr2": ("psum", [128, 512], "float32"),
-    "psr3": ("psum", [128, 512], "float32"),
-    "i32": ("sbuf", [128, 128], "float32"),
     "fin": ("sbuf", [128, 512], "float32"),
 }
+for _n in ("psa", "psc", "pss0", "pss1", "psm0", "psm1", "pst", "psu"):
+    SCRATCH[_n] = ("psum", [128, 512], "float32")
 for _t in range(4):
-    SCRATCH["ff%d" % _t] = ("sbuf", [128, 2048], "float32")
+    SCRATCH["ff%d" % _t] = ("sbuf", [128, 2560], "float32")
     SCRATCH["ww%d" % _t] = ("sbuf", [128, 1024], "float32")
     SCRATCH["cn%d" % _t] = ("sbuf", [128, 128], "float32")
     SCRATCH["co%d" % _t] = ("sbuf", [128, 128], "uint16")
 
-NDMA = 40
+NDMA = 60
 SEMAPHORES = ["eV", "eS", "eP", "eG", "h_tab", "h_rp", "h_m", "a_tab", "a_rp", "a_m", "h_e", "h_f", "a_e", "a_f", "sent"] + ["d%d" % i for i in range(NDMA)]
 
 
@@ -120,13 +112,13 @@ def helper_program(g, core, src, dst, k, hs, T, topo):
     g.wait_ge(T.sem.h_m, cnt[k])
     g.remote_dma(T.rm[:, 256 * k:256 * (k + 1)], T.rm[:, 256 * k:256 * (k + 1)], T.sem.a_m, T.sem.sent, pid, rid, m)
     sent += n
+    g.wait_ge(T.sem.h_f, cnt[k])
+    g.remote_dma(T.rfac[:, 128 * k:128 * (k + 1)], T.rfac[:, 128 * k:128 * (k + 1)], T.sem.a_f, T.sem.sent, pid, rid, m)
+    sent += n
     if k == 0:
         g.wait_ge(T.sem.h_e, cnt[k])
         g.remote_dma(T.re16[:], T.re16[:], T.sem.a_e, T.sem.sent, pid, rid, m)
         sent += n
-    g.wait_ge(T.sem.h_f, cnt[k])
-    g.remote_dma(T.rrg[:, 128 * k:128 * (k + 1)], T.rrg[:, 128 * k:128 * (k + 1)], T.sem.a_f, T.sem.sent, pid, rid, m)
-    sent += n
     g.wait_ge(T.sem.sent, sent)
 
 
@@ -151,7 +143,7 @@ def emit(g, T, ops, ext):
         need = []
         for d in sorted(deps, key=lambda x: -x if isinstance(x, int) else 1):
             if isinstance(d, int) and ops[d][4] == "c":
-                have = known[eng].get(ops[d][0], -1) >= d or (eng == "P" and ops[d][0] == "P")
+                have = known[eng].get(ops[d][0], -1) >= d or (eng == "P" and ops[d][0] == "P" and "psu" not in wr)
             else:
                 have = d in known[eng]
             if not have:
@@ -210,7 +202,7 @@ def rank_program(g, core, T, topo):
     hin = helpers(T.cores[(rank + HOP) % N], core, T, topo)
     nin = [len(topo.engines(h, core)) for h in hin]
     ext = {"rtab": ("a_tab", sum(nin)), "rrp": ("a_rp", nin[0]), "rm": ("a_m", sum(nin)),
-           "re16": ("a_e", nin[0]), "rrg": ("a_f", sum(nin))}
+           "re16": ("a_e", nin[0]), "rfac": ("a_f", sum(nin))}
 
     ops = []
     V, S, P = g.vector, g.scalar, g.tensor
@@ -240,11 +232,17 @@ def rank_program(g, core, T, topo):
     def act(out, a, f, bias, scale, rd, wr):
         op("S", lambda: S.activation(out, a, f, bias=bias, scale=scale), rd, wr)
 
-    def mms(lst, rd, wr):
+    def lin(eng, out, src, scale, bias, rd, wr):
+        if eng == "S":
+            act(out, src, AF.Identity, bias, scale, rd, wr)
+        else:
+            ts(out, src, scale, bias, A.mult, A.add, rd, wr)
+
+    def mms(lst, rd, wr, start=True, stop=True):
         def fn():
             ins = None
             for n, (o, l, r) in enumerate(lst):
-                ins = P.matmul(o, l, r, n == 0, n == len(lst) - 1)
+                ins = P.matmul(o, l, r, start and n == 0, stop and n == len(lst) - 1)
             return ins
         op("P", fn, rd, wr)
 
@@ -259,470 +257,341 @@ def rank_program(g, core, T, topo):
             return sum(cnt[k] for k in ks)
         op("G", fn, rd, [], "r")
 
-    dma("S", T.mm[:], T.mj[:], [], ["mm"])
-    dma("Y", T.cei[:], T.ce[:], [], ["cei"])
-    dma("S", T.tab[:, 0:1024], T.nx[:], [], ["nx"])
-    dma("Y", T.uz[:, 0:128], T.uu[0:8:2, :], [], ["u_a"])
-    dma("Y", T.uz[:, 128:256], T.uu[1:8:2, :], [], ["u_b"])
-    dma("Y", T.rpi[:], T.rp[:], [], ["rpi"])
-    dma("Y", T.tab[:, 1024:2048], T.sg[:], [], ["sg"])
-    dma("S", T.tab[:, 2048:3072], T.al[:], [], ["al"])
-    dma("Y", T.uz[:, 256:384], T.zz[0:8:2, :], [], ["z_a"])
-    dma("Y", T.uz[:, 384:512], T.zz[1:8:2, :], [], ["z_b"])
+    def rows(buf, src, key, t, rd=()):
+        a, p = 1024 * t, 32 * t
+        if t < 2:
+            dma("Y", buf[p:p + 8, :], src[:, a:a + 1024], rd, [key + "%d" % t])
+        else:
+            dma("Y", buf[p:p + 8, 0:512], src[:, a:a + 512], [], [key + "%d" % t])
+            dma("Y", buf[p + 1:p + 8, 512:1024], src[0:7, a + 512:a + 1024], [], [key + "%da" % t])
+            dma("Y", buf[p:p + 1, 512:1024], src[7:8, a + 512:a + 1024], [], [key + "%db" % t])
 
-    op("G", lambda: g.iota(T.qi[:], [[0, 8]], 0, 1), [], ["qi"])
-    op("G", lambda: g.iota(T.jj[:], [[1, 144]], 0, -1, allow_small_or_imprecise_dtypes=True), [], ["jj"])
-    op("G", lambda: g.iota(T.oi[:, 0:32], [[256, 2], [16, 8], [128, 2]], 0, 0), [], ["oi0"])
-    op("G", lambda: g.iota(T.oi[:, 32:40], [[2, 8]], 0, 0), [], ["oi1"])
-    op("G", lambda: g.iota(T.oi[:, 40:48], [[8, 2], [516, 2], [2, 2]], 16, 0), [], ["oi2"])
-    op("G", lambda: g.iota(T.xx[:], [[1, 16], [0, 16]], 0, 0, allow_small_or_imprecise_dtypes=True), [], ["xx"])
-    if MODE0 and MODE2:
-        op("G", lambda: g.iota(T.fa2[:], [[0, 1024]], 1, 0, allow_small_or_imprecise_dtypes=True), [], ["fa2_0", "fa2_1"])
-    send(lambda k: T.rpi[:, 64:96], lambda k: T.rrp[:], T.sem.h_rp, [0], ["rpi"])
-    send(lambda k: T.tab[:, 768 * k:768 * (k + 1)], lambda k: T.rtab[:, 768 * k:768 * (k + 1)], T.sem.h_tab, range(4), ["nx", "sg", "al"])
+    def con(n):
+        jq = T.jj[:, 0:128]
+        if n in ("kt", "six", "k2", "cc"):
+            v = {"kt": KK, "six": 0.0625, "k2": 2176 * KK, "cc": -0.5625 + 2.0 ** -13}[n]
+            op("V", lambda: V.memset(T[n][:], v), [], [n])
+        if n in ("q0", "q1", "q2"):
+            k = int(n[1])
+            ts(T.qi[:, k:k + 1], T.qi[:, k:k + 1], (15, 112, 7)[k], None, A.bitwise_and, None, [n], [n])
+        if n == "qf":
+            cp(T.qf[:], T.qi[:, 0:4], ["q0", "q1", "q2"], [n])
+        if n == "i1":
+            ts(T.i1[:], jq, 0.0, None, A.is_equal, None, ["jj"], [n])
+        if n == "big":
+            ts(T.big[:], T.jj[:, 0:16], T.qf[:, 1:2], 256.0, A.add, A.mult, ["jj", "qf"], [n])
+        if n == "msk":
+            ts(T.msk[:], T.big[:], 0.0, None, A.is_equal, None, ["big"], [n])
+        if n == "c0":
+            ts(T.col[:, 0:1], T.qf[:, 2:3], -16.0, T.qf[:, 3:4], A.mult, A.add, ["qf"], [n])
+        if n == "c1":
+            ts(T.col[:, 1:2], T.qf[:, 0:1], 129.0, -KK, A.add, A.mult, ["qf"], [n])
+        if n == "ew":
+            ts(T.ew[:], T.jj[:], T.col[:, 0:1], 15.0, A.add, A.is_equal, ["jj", "c0"], [n])
+        if n == "bw":
+            ts(T.bw[:], T.jj[:], T.qf[:, 0:1], 15.0, A.add, A.is_equal, ["jj", "qf"], [n])
+        if n == "sq":
+            act(T.sq[:], jq, AF.Abs, 48.0, 1.0, ["jj"], [n])
+        if n == "s32":
+            ts(T.s32[:], T.sq[:], 64.0, None, A.is_equal, None, ["sq"], [n])
+        if n == "ce16":
+            cp(T.ce16[:], T.cei[:], ["cei"], [n])
+        if n == "cf":
+            cp(T.cf[:], T.cei[:], ["cei"], [n])
 
-    op("V", lambda: V.memset(T.six[:], 0.125), [], ["six"])
-    ft = 0 if MODE0 else 2
-    for h in range(2 if MODE0 or MODE2 else 0):
-        act(T["fa%d" % ft][:, 512 * h:512 * (h + 1)], T.six[:], AF.Sigmoid, 0.0, 800.0, ["six"], ["fa%d_%d" % (ft, h)])
-    ts(T.qj[:, 0:1], T.qi[:, 0:1], 15, None, A.bitwise_and, None, ["qi"], ["qj0"])
-    ts(T.qj[:, 1:2], T.qi[:, 0:1], 112, None, A.bitwise_and, None, ["qi"], ["qj1"])
-    ts(T.qj[:, 2:3], T.qi[:, 0:1], 7, None, A.bitwise_and, None, ["qi"], ["qj2"])
-    ts(T.qj[:, 3:4], T.qi[:, 0:1], 3, 1, A.logical_shift_right, A.bitwise_and, ["qi"], ["qj3"])
-    cp(T.qf[:], T.qj[:], ["qj0", "qj1", "qj2", "qj3"], ["qf"])
-    ts(T.i2[:], T.jj[:, 0:128], 0.0, 2.0, A.is_equal, A.mult, ["jj"], ["i2"])
-    ts(T.big[:], T.jj[:, 0:16], T.qf[:, 1:2], 256.0, A.add, A.mult, ["jj", "qf"], ["big"])
-    ts(T.pp[:, 0:1], T.qf[:, 2:3], 32.0, T.qf[:, 3:4], A.mult, A.add, ["qf"], ["pp"])
-    ts(T.i1[:], T.jj[:, 0:128], 0.0, None, A.is_equal, None, ["jj"], ["i1"])
-    ts(T.o16[:, 0:32], T.oi[:, 0:32], T.qf[:, 0:1], None, A.add, None, ["oi0", "qf"], ["o1"])
+    def mul(eng, n):
+        src, f = {"i2": ("i1", 2.0), "i32": ("i1", 1.0), "dk": ("i1", -16 * KK), "ez": ("ew", 2.0 ** -12)}[n]
+        lin(eng, T[n][:], T[src][:], f, 0.0, [src], [n])
 
-    def dms(a, b):
-        for i in range(a, b):
-            ts(T.dm[:, 128 * i:128 * (i + 1)], T.jj[:, 0:128], T.big[:, i:i + 1], None, A.is_equal, None, ["jj", "big"], ["dm%d" % i])
-    DM = ["dm%d" % i for i in range(16)]
-    ts(T.msk[:], T.big[:], 0.0, None, A.is_equal, None, ["big"], ["msk"])
-    dms(0, 9)
-    for i in range(9, 16):
-        act(T.dm[:, 128 * i:128 * (i + 1)], T.i1[:], AF.Copy, 0.0, T.msk[:, i:i + 1], ["i1", "msk"], ["dm%d" % i])
-    ts(T.o16[:, 32:48], T.oi[:, 32:48], T.pp[:, 0:1], None, A.add, None, ["oi1", "oi2", "pp"], ["o2"])
-    cp(T.ce16[:], T.cei[:], ["cei"], ["ce16"])
-
-    def pick(eng, out, src, rd, wr, scale=1.0):
+    def diag(eng, i):
+        o = T.dm[:, 128 * i:128 * (i + 1)]
         if eng == "S":
-            act(out, src, AF.Copy, 0.0, scale, rd, wr)
+            act(o, T.i1[:], AF.Copy, 0.0, T.msk[:, i:i + 1], ["i1", "msk"], ["dm%d" % i])
         else:
-            cp(out, src, rd, wr)
+            ts(o, T.jj[:, 0:128], T.big[:, i:i + 1], None, A.is_equal, None, ["jj", "big"], ["dm%d" % i])
 
-    def gather1(a, key, eng):
-        pick(eng, T.uz1[:, a:a + 256], T.uz[:, a:a + 256].indirect(T.o16[:, 0:16]), [key + "_a", key + "_b", "o1"], [key + "1"])
+    def spread(out, ek, buf, key, t, bank, start, stop):
+        p = 32 * t
+        mms([(out, T[ek][p:p + 8, 15 - h:143 - h], buf[p:p + 8, h:1024:16]) for h in range(16)],
+            [ek] + [key + "%d%s" % (t, x) for x in ("", "a", "b")], [bank], start, stop)
 
-    def turn(a, key):
-        op("V", lambda: V.transpose(T.uzt[:, a:a + 256], T.uz1[:, a:a + 256]), [key + "1"], [key + "t"])
+    def pe_u(t):
+        spread(T.psu[:, 64 * t:64 * (t + 1)], "ew", T.us, "u", t, "psu", True, True)
 
-    def lists1(a, key, eng):
-        gather1(a, key, eng)
-        turn(a, key)
+    def cp_u(eng, a, b):
+        lin(eng, T.ul[:, 64 * a:64 * b], T.psu[:, 64 * a:64 * b], 1.0, 0.0, ["psu"], ["ul%d" % t for t in range(a, b)])
 
-    def lists2(a, key, lst, b, eng):
-        sc = -1.0 if key == "z" else 1.0
-        if b == 0:
-            pick(eng, lst[:, 0:128], T.uzt[:, a:a + 256].indirect(T.o16[:, 32:40]), [key + "t", "o2"], [key + "l0"], sc)
-        else:
-            pick(eng, lst[:, 128:256], T.uzt[:, a:a + 768].indirect(T.o16[:, 40:48]), ["ut", "zt", "uzr0", "uzr1", "o2"], [key + "l1"], sc)
+    def pe_o():
+        mms([(T.psc[:, 0:64], T.i32[:], T.cc[:])], ["i32", "cc"], ["psc"], True, False)
 
-    psm, psr = [T.psm0, T.psm1], [T.psr0, T.psr1]
+    def pe_z(t):
+        spread(T.psc[:, 0:64], "ez", T.zs, "z", t, "psc", False, False)
+
+    DM = ["dm%d" % i for i in range(16)]
+    psm, pss = [T.psm0, T.psm1], [T.pss0, T.pss1]
 
     def tabs(t):
-        mk_ = ("mm", "m1", "rm", "m3" if MODE2 else "rm")[t]
-        return (T.tab, "nx", "sg", "al", T[mk_], mk_) if t < 2 else (T.rtab, "rtab", "rtab", "rtab", T[mk_], mk_)
+        return (T.tab, "nx", "sg", "al", T.mm, "mm") if t < 2 else (T.rtab, "rtab", "rtab", "rtab", T.rm, "rm")
 
     def cells(t):
         if t == 0:
-            return T.cei[:], "cei", T.ce16, "ce16"
+            return T.cf[:], "cf", T.ce16, "ce16"
         if t == 2:
             return T.c2[:], "c2", T.c216, "c216"
         return T["cn%d" % (t - 1)][:, 0:64], "cn%d" % (t - 1), T["co%d" % (t - 1)], "co%d" % (t - 1)
+
+    def parts(name, a, b):
+        return [name + "%d" % h for h in range(a // 8, b // 8)]
 
     def g1(t, eng, a, b):
         M, mk_ = tabs(t)[4:6]
         c16, ck = cells(t)[2:4]
         src = M[:].indirect(c16[:, a:b])
-        keys = ["ng%d" % h for h in range(a // 32, b // 32)]
         if eng == "S":
-            act(T.ng[:, 16 * a:16 * b], src, AF.Relu, -0.125, 2.0 if t == 0 else 1.0, [mk_, ck], keys)
-        elif t == 0:
-            ts(T.ng[:, 16 * a:16 * b], src, 2.0, -0.125, A.mult, A.add, [mk_, ck], keys)
+            act(T.ng[:, 16 * a:16 * b], src, AF.Relu, -0.0625, 1.0, [mk_, ck], parts("ng", a, b))
         else:
-            ts(T.ng[:, 16 * a:16 * b], src, -0.125, 0.0, A.add, A.max, [mk_, ck], keys)
+            ts(T.ng[:, 16 * a:16 * b], src, -0.0625, 0.0, A.add, A.max, [mk_, ck], parts("ng", a, b))
 
-    def g2(t, eng="S", a=0, b=64):
+    def g2(t, eng, a, b):
         tb, nk = tabs(t)[0:2]
         c16, ck = cells(t)[2:4]
-        pick(eng, T.dg[:, 16 * a:16 * b], tb[:, 0:1024].indirect(c16[:, a:b]), [nk, ck], ["dg%d" % h for h in range(a // 16, b // 16)])
-
-    def ndense(t, h):
-        M, mk_ = tabs(t)[4:6]
-        act(T.nd[:, 512 * h:512 * (h + 1)], M[:, 512 * h:512 * (h + 1)], AF.Relu, -0.125, 1.0, [mk_ + "h%d" % h if (0, MODE0, 0, MODE2)[t] else mk_], ["nd%d" % h])
-
-    def pe_m(t, h):
-        if t == 0:
-            mms([(psm[h][:], T.i2[:], T.mm[:, 512 * h:512 * (h + 1)])], ["i2", "mm"], ["psm%d" % h])
-        else:
-            op("P", lambda: P.matmul(psm[h][:], T.i1[:], T.nd[:, 512 * h:512 * (h + 1)], False, True), ["i1", "nd%d" % h], ["psm%d" % h])
-
-    def pe_six(h):
-        op("P", lambda: P.matmul(psm[h][:], T.i1[:], T.six[:], True, False), ["i1", "six"], ["psm%d" % h])
+        lin(eng, T.dg[:, 16 * a:16 * b], tb[:, 0:1024].indirect(c16[:, a:b]), 1.0, 0.0, [nk, ck], parts("dg", a, b))
 
     def pe_a(t):
-        mms([(T.psa[:, 0:64], T.i1[:], T.six[:, 0:64])] +
+        mms([(T.psa[:, 0:64], T.i1[:], T.six[:])] +
             [(T.psa[:, 0:64], T.dm[:, 128 * i:128 * (i + 1)], T.ng[:, i:1024:16]) for i in range(16)],
-            ["i1", "six", "ng0", "ng1"] + DM, ["psa"])
+            ["i1", "six"] + parts("ng", 0, 64) + DM, ["psa"])
 
-    def v_a(t):
-        tt(T.xv[:], T.psa[:, 0:64], T.ul[:, 64 * t:64 * (t + 1)], A.mult, ["psa", "ul%d" % (t // 2)], ["xv"])
-        ts(T.v16[:], T.xv[:], 8.0, 255.0, A.mult, A.min, ["xv"], ["v16"])
-        tt(T.sel[:], T.oh[:].indirect(T.v16[:]), T.dg[:], A.mult, ["oh", "v16", "dg0", "dg1", "dg2", "dg3"], ["sel"])
+    def pe_d(b):
+        mms([(pss[b][:, 64 * i:64 * (i + 1)], T.i1[:], T.dg[:, 8 * b + i:1024:16]) for i in range(8)],
+            ["i1"] + parts("dg", 0, 64), ["pss%d" % b], True, False)
 
-    def pe_b(t):
-        mms([(T.psb[:, 0:64], T.bw[:, 15 - i:143 - i], T.sel[:, i:1024:16]) for i in range(16)], ["bw", "sel"], ["psb"])
+    def pe_p(b):
+        mms([(pss[b][:, 64 * i:64 * (i + 1)], T.bc[:, 128 * (8 * b + i):128 * (8 * b + i + 1)], T.pb[:]) for i in range(8)],
+            ["pb", "bc%d" % (2 * b), "bc%d" % (2 * b + 1)], ["pss%d" % b], False, True)
 
-    def pr(t, h):
-        return "psr%d" % (h + (2 if t == 0 else 0))
+    def sel(eng, b):
+        lin(eng, T.sel[:, 512 * b:512 * (b + 1)], pss[b][:], 1.0, T.col[:, 1:2], ["pss%d" % b, "c1"], ["sel%d" % b])
+
+    def pe_y(t):
+        c, ck = cells(t)[0:2]
+        mms([(T.psa[:, 64:128], T.i1[:], T.k2[:]), (T.psa[:, 64:128], T.dk[:], T.pb[:]), (T.psa[:, 64:128], T.i32[:], c)],
+            ["i1", "k2", "dk", "pb", "i32", ck], ["psa"], True, False)
+
+    def pe_b(b):
+        mms([(T.psa[:, 64:128], T.bw[:, 15 - i:143 - i], T.sel[:, 64 * i:64 * (i + 1)]) for i in range(8 * b, 8 * b + 8)],
+            ["bw", "sel%d" % b], ["psa"], False, b == 1)
+
+    def floor(t, h):
+        M, mk_ = tabs(t)[4:6]
+        ts(T.nd[:, 512 * h:512 * (h + 1)], M[:, 512 * h:512 * (h + 1)], 0.0625, None, A.max, None, [mk_], ["nd%d" % h])
+
+    def pe_m(t, h):
+        src, k = (T.mm, "mm") if t == 0 else (T.nd, "nd%d" % h)
+        mms([(psm[h][:], T.i2[:], src[:, 512 * h:512 * (h + 1)])], ["i2", k], ["psm%d" % h])
 
     def rho(t, h):
         tb, _, sk = tabs(t)[0:3]
-        tt(T[pr(t, h)][:], tb[:, 1024 + 512 * h:1536 + 512 * h], psm[h][:], A.mult, [sk, "psm%d" % h], [pr(t, h)])
+        tt(psm[h][:], tb[:, 1024 + 512 * h:1536 + 512 * h], psm[h][:], A.mult, [sk, "psm%d" % h], ["psm%d" % h])
 
-    def fnull(t, h):
-        act(T["ff%d" % t][:, 512 * h:512 * (h + 1)], T[pr(t, h)][:], AF.Identity, 2.0, -1.0, [pr(t, h)], ["fn%d_%d" % (t, h)])
+    def fnull(t, eng, h):
+        lin(eng, T["ff%d" % t][:, 256 + 512 * h:768 + 512 * h], psm[h][:], -1.0, 2.0, ["psm%d" % h], ["fn%d_%d" % (t, h)])
+
+    def edge(t, eng, h):
+        a = 1280 * (1 - h)
+        lin(eng, T["ff%d" % t][:, a:a + 256], psm[h][:, 256 * h:256 * (h + 1)], -1.0, 2.0, ["psm%d" % h], ["fe%d_%d" % (t, h)])
+
+    def fnull3(eng, h):
+        lin(eng, T.fl[:, 1024 * h:1024 * (h + 1):2], psm[h][:], -1.0, 2.0, ["psm%d" % h], ["fm%d" % h])
 
     def freal(t, h):
         tb, ak = tabs(t)[0], tabs(t)[3]
-        tt(T["ff%d" % t][:, 1024 + 512 * h:1536 + 512 * h], tb[:, 2048 + 512 * h:2560 + 512 * h], T[pr(t, h)][:], A.mult,
-           [ak, pr(t, h)], ["fr%d_%d" % (t, h)])
+        o = T["ff%d" % t][:, 1536 + 512 * h:2048 + 512 * h] if t < 3 else T.fl[:, 1024 * h + 1:1024 * (h + 1):2]
+        tt(o, tb[:, 2048 + 512 * h:2560 + 512 * h], psm[h][:], A.mult, [ak, "psm%d" % h], ["fr%d_%d" % (t, h)])
 
-    def pe_sum(t, a, b):
-        op("P", lambda: P.matmul(T.psr2[:, a:b], T.i32[:], T["ww%d" % t][:, a:b], t == 0, t == 2 and b == 512),
-           ["i32", "w%d_0" % t], ["psr2"])
+    def sm(t, names):
+        cn, co = T["cn%d" % t], T["co%d" % t]
+        for n in names.split():
+            if n == "xv":
+                tt(T.xv[:], T.psa[:, 0:64], T.ul[:, 64 * t:64 * (t + 1)], A.mult, ["psa", "ul%d" % t], ["xv"])
+            if n == "pb":
+                ts(T.pb[:], T.xv[:], 15.0, 128.53125, A.min, A.add, ["xv"], ["pb"])
+            if n == "d16":
+                ts(T.d16[:], T.psa[:, 64:128], 8 * KK + 256, None, A.add, None, ["psa"], ["d16"])
+            if n == "yi":
+                cp(T.yi[:], T.psa[:, 64:128], ["psa"], ["yi"])
+            if n == "par":
+                ts(T.par[:], T.yi[:], 1, None, A.bitwise_and, None, ["yi"], ["par"])
+            if n == "ee":
+                tt(T.ee[:], T.par[:, 16:48], T.v2[:, 32 * t:32 * (t + 1)], A.add, ["par", "v2_%d" % (t // 2)], ["ee"])
+            if n == "e16":
+                cp(T.e16[:], T.ee[:], ["ee"], ["e16"])
+            if n == "da":
+                ts(T.ib[:, 0:64], T.yi[:], 1023, None, A.bitwise_and, None, ["yi"], ["ibe"])
+            if n == "db":
+                ts(T.ib[:, 64:128], T.yi[:], 1023, None, A.bitwise_and, None, ["yi"], ["ibd"])
+            if n == "sn":
+                ts(T.sn[:], T.par[:], 2.0, -1.0, A.mult, A.add, ["par"], ["sn"])
+            if n == "ra":
+                tt(T.rb[:, 0:64], T.psc[:, 0:64], T.sn[:], A.mult, ["psc", "sn"], ["rbe"])
+            if n == "rb":
+                ts(T.rb[:, 64:128], T.psc[:, 0:64], -0.5, 1280.0, A.is_lt, A.mult, ["psc"], ["rbd"])
+            if n == "cn":
+                tt(cn[:], T.ib[:], T.rb[:], A.add, ["ibe", "ibd", "rbe", "rbd"], ["cn%d" % t])
+            if n == "co":
+                a = 64 * (t % 2)
+                cp(co[:, a:128], cn[:, a:128], ["cn%d" % t], ["co%d" % t])
+            if n == "m2":
+                ts(T.sn[:], T.ib[:, 64:128], -2.0, None, A.mult, None, ["ibd"], ["sn"])
+            if n == "on":
+                ts(co[:, 64:128], T.psc[:, 0:64], -1.0, None, A.mult, None, ["psc"], ["co%d" % t])
+            if n == "v2":
+                src, a, b, rd = (T.rpi[:, 0:64], 0, 64, "rpi") if t == 0 else (T.rrp[:], 64, 96, "rrp")
+                ts(T.v2[:, a:b], src, 2.0, None, A.mult, None, [rd], ["v2_%d" % (t // 2)])
+            if n == "c16":
+                cp(T.c216[:], T.psc[:, 64:128], ["psc"], ["c216"])
 
-    def v_b(t):
-        c, ck = cells(t)[0:2]
-        tt(T.yi[:], T.psb[:, 0:64], c, A.add, ["psb", ck], ["yi"])
-        ts(T.ib[:, 64:128], T.yi[:], 1023, None, A.bitwise_and, None, ["yi"], ["ibd"])
-        if t < 3:
-            ts(T.par[:], T.yi[:], 1, None, A.bitwise_and, None, ["yi"], ["par"])
-        cp(T.d16[:], T.ib[:, 64:128], ["ibd"], ["d16"])
-        if t < 3:
-            tt(T.ee[:], T.par[:, 16:48], T.v2[:, 32 * t:32 * (t + 1)], A.add, ["par", "v2_%d" % (t // 2)], ["ee"])
-            ts(T.ib[:, 0:64], T.yi[:], 1022, None, A.bitwise_and, None, ["yi"], ["ibe"])
-            cp(T.e16[:], T.ee[:], ["ee"], ["e16"])
+    def cells2(eng):
+        lin(eng, T.c2[:], T.psc[:, 64:128], 1.0, 0.0, ["psc"], ["c2"])
 
-    def g4(t, a, b, keys, eng="S"):
-        src = T["ff%d" % t][:, 0:1024].indirect(T.d16[:, a:b])
-        rd = ["fn%d_0" % t, "fn%d_1" % t, "d16"]
-        if eng == "S":
-            act(T.rg[:, 16 * a:16 * b], src, AF.Identity, 256.0, -128.0, rd, keys)
-        else:
-            ts(T.rg[:, 16 * a:16 * b], src, -128.0, 256.0, A.mult, A.add, rd, keys)
+    def pe_s(h):
+        m = ("i32", "s32")[h]
+        mms([(T.psc[:, 64 + 32 * h:96 + 32 * h], T[m][:], T.cn1[:, 32 * h:32 * h + 32])], [m, "cn1"], ["psc"])
 
-    def oldm(t, eng):
-        M, mk_ = tabs(max(t, 1))[4:6]
-        if eng == "S":
-            act(T.old[:], M[:].indirect(T.e16[:]), AF.Copy, 0.0, 1.0, [mk_, "e16"], ["old"])
-        else:
-            cp(T.old[:], M[:].indirect(T.e16[:]), [mk_, "e16"], ["old"])
+    def null_at(t, a, b):
+        return T["ff%d" % t][:, 0:1536].indirect(T.d16[:, a:b]), ["fn%d_0" % t, "fn%d_1" % t, "fe%d_0" % t, "fe%d_1" % t, "d16"]
+
+    def g4(t, eng, a, b):
+        src, rd = null_at(t, a, b)
+        lin(eng, T.rg[:, 16 * a:16 * b], src, 1 / 32, 0.0, rd, parts("rg", a, b))
 
     def fac(t):
-        ts(T.fac[:], T.rg[:, 256:768], 256.0, 0.5, A.is_le, A.max, ["rg1"], ["fac"])
+        src, rd = null_at(t, 16, 48) if t == 1 else (T.rg[:, 256:768], parts("rg", 16, 48))
+        ts(T.fac[:], src, 0.0, 0.5, A.is_ge, A.max, rd, ["fac"])
+
+    def old(t, eng, h):
+        M, mk_ = tabs(t + 1)[4:6]
+        e, ek = (T.re16, "re16") if t == 1 else (T.e16, "e16")
+        lin(eng, T.old[:, 256 * h:256 * (h + 1)], M[:].indirect(e[:, 16 * h:16 * (h + 1)]), 1.0, 0.0, [mk_, ek], ["old%d" % h])
 
     def scat(t):
-        M, mk_ = tabs(max(t, 1))[4:6]
-        tt(M[:].indirect(T.e16[:]), T.old[:], T.fac[:], A.mult, ["old", "fac", "e16"], [mk_])
+        M, mk_ = tabs(t + 1)[4:6]
+        e, f = ("re16", "rfac") if t == 1 else ("e16", "fac")
+        tt(M[:].indirect(T[e][:]), T.old[:], T[f][:], A.mult, ["old0", "old1", f, e], [mk_])
 
     def pe_c(t):
-        op("P", lambda: P.matmul(T.psa[:, 64:128], T.i1[:], T.zl[:, 64 * t:64 * (t + 1)], True, False), ["i1", "zl%d" % (t // 2)], ["psa"])
+        mms([(T.psc[:, 0:64], T.dm[:, 128 * i:128 * (i + 1)], T.rg[:, i:1024:16]) for i in range(16)],
+            parts("rg", 0, 64) + DM, ["psc"], False, t < 3)
 
-        def fn():
-            ins = None
-            for i in range(16):
-                ins = P.matmul(T.psa[:, 64:128], T.dm[:, 128 * i:128 * (i + 1)], T.rg[:, i:1024:16], False, i == 15)
-            return ins
-        op("P", fn, ["rg0", "rg1", "rg2"] + DM, ["psa"])
+    def pe_e():
+        mms([(T.psc[:, 0:64], T.i32[:], T.sn[:])], ["i32", "sn"], ["psc"], False, True)
 
-    def v_r(t):
-        cn, co = T["cn%d" % t], T["co%d" % t]
-        if t < 3:
-            ts(T.rr[:], T.psa[:, 64:128], 0.0, None, A.is_gt, None, ["psa"], ["rr"])
-        ts(T.rb[:, 64:128], T.psa[:, 64:128], 0.0, 1024.0, A.is_gt, A.mult, ["psa"], ["rbd"])
-        if t < 3:
-            tt(T.rb[:, 0:64], T.rr[:], T.par[:], A.not_equal, ["rr", "par"], ["rbe"])
-        if t < 3:
-            tt(cn[:, 0:64], T.ib[:, 0:64], T.rb[:, 0:64], A.add, ["ibe", "rbe"], ["cn%d" % t])
-        tt(cn[:, 64:128], T.ib[:, 64:128], T.rb[:, 64:128], A.add, ["ibd", "rbd"], ["on%d" % t])
-        if t in (0, 2):
-            cp(co[:, 0:64], cn[:, 0:64], ["cn%d" % t], ["co%d" % t])
-        if t == 1:
-            cp(T.c2[:, 0:32], T.cn1[:, 0:32], ["cn1"], ["c2c"])
-        cp(co[:, 64:128], cn[:, 64:128], ["on%d" % t], ["oo%d" % t])
+    def factor(t, h):
+        off = T["co%d" % t][:, 64 + 32 * h:96 + 32 * h]
+        if t == 3:
+            return T.fl[:].indirect(off), ["fm0", "fm1", "fr3_0", "fr3_1", "co3"]
+        return T["ff%d" % t][:, 256:2560].indirect(off), [k % t for k in ("fn%d_0", "fn%d_1", "fe%d_0", "fr%d_0", "fr%d_1", "co%d")]
 
-    def clip(t, a, b):
-        w = T["ww%d" % t]
-        keys = ["w%d_%d" % (t, h) for h in range(a // 512, b // 512)]
-        ts(w[:, a:b], w[:, a:b], 0.125, 4.0, A.max, A.min, keys, keys)
-
-    def sclip(t, a, b, k):
-        w = T["ww%d" % t]
-        keys = ["w%d_%d" % (t, h) for h in range(a // 512, b // 512)]
-        if k == 0 and t == 0:
-            src = T.ff0[:].indirect(T.co0[:, 64 + a // 16:64 + b // 16])
-            act(w[:, a:b], src, AF.Relu, 4.0, -1.0, ["fn0_0", "fn0_1", "fr0_0", "fr0_1", "oo0"], keys)
-        else:
-            f, bias, scale = ((AF.Relu, 4.0, -1.0), (AF.Relu, 3.875, -1.0), (AF.Identity, 0.125, 1.0))[k]
-            act(w[:, a:b], w[:, a:b], f, bias, scale, keys, keys)
-
-    def weights(t, a, b):
-        w = T["ww%d" % t]
-        src = T["ff%d" % t][:].indirect(T["co%d" % t][:, 64 + a // 16:64 + b // 16])
-        rd = ["fn%d_0" % t, "fn%d_1" % t, "fr%d_0" % t, "fr%d_1" % t, "oo%d" % t]
-        keys = ["w%d_%d" % (t, h) for h in range(a // 512, b // 512)]
+    def weights(t, h):
+        w, key = T["ww%d" % t][:, 512 * h:512 * (h + 1)], ["w%d_%d" % (t, h)]
+        src, rd = factor(t, h)
         if t == 0:
-            ts(w[:, a:b], src, 0.125, 4.0, A.max, A.min, rd, keys)
-            return
-        if t == 2 and a == 512:
-            prev, pk = T.wr[:], ["wr0", "wr1"]
+            ts(w, src, 0.125, 4.0, A.max, A.min, rd, key)
+        elif t == 2 and h == 1:
+            tt(w, src, T.wr[:], A.mult, rd + ["wr0", "wr1"], key)
         else:
-            prev, pk = T["ww%d" % (t - 1)][:, a:b], ["w%d_%d" % (t - 1, h) for h in range(a // 512, b // 512)]
-        tt(w[:, a:b], src, prev, A.mult, rd + pk, keys)
+            tt(w, src, T["ww%d" % (t - 1)][:, 512 * h:512 * (h + 1)], A.mult, rd + ["w%d_%d" % (t - 1, h)], key)
+
+    def clip(t, h):
+        w, key = T["ww%d" % t][:, 512 * h:512 * (h + 1)], ["w%d_%d" % (t, h)]
+        ts(w, w, 0.125, 4.0, A.max, A.min, key, key)
+
+    def sclip(t, h, k):
+        w, key = T["ww%d" % t][:, 512 * h:512 * (h + 1)], ["w%d_%d" % (t, h)]
+        f, bias, scale = ((AF.Relu, 4.0, -1.0), (AF.Relu, 3.875, -1.0), (AF.Identity, 0.125, 1.0))[k]
+        src, rd = factor(t, h) if t == 0 and k == 0 else (w, key)
+        act(w, src, f, bias, scale, rd, key)
+
+    def pe_sum(t, a, b):
+        op("P", lambda: P.matmul(T.pst[:, a:b], T.i32[:], T["ww%d" % t][:, a:b], t == 0, t == 2 and b == 512),
+           ["i32", "w%d_0" % t], ["pst"])
 
     def out_hi(t):
-        w = T["ww%d" % t]
-        dma("G", T.tl[0:112, 512:1024], w[16:128, 512:1024], ["w%d_1" % t], ["tl1"], True)
-        dma("G", T.tl[112:128, 512:1024], w[0:16, 512:1024], ["w%d_1" % t], ["tl2"], True)
+        w, rd = T["ww%d" % t], ["w%d_1" % t]
+        if t < 2:
+            dma("YG"[t], T.tl[:, 512:1024], w[:, 512:1024], rd, ["tl1", "tl2"], t == 1)
+        else:
+            dma("G", T.tl[0:112, 512:1024], w[16:128, 512:1024], rd, ["tl1"], True)
+            dma("G", T.tl[112:128, 512:1024], w[0:16, 512:1024], rd, ["tl2"], True)
 
-    def reports_s(t):
-        fa, fk = T["fa%d" % t], ["fa%d_0" % t, "fa%d_1" % t]
-        act(T.xr[:], T["ff%d" % t][:, 0:1024].indirect(T.d16[:, 16:48]), AF.Relu, 128.0, 2048.0, ["fn%d_0" % t, "fn%d_1" % t, "d16"], ["xr"])
-        op("S", lambda: S.activation(fa[:].indirect(T.e16[:]), T.xr[:], AF.Sigmoid), ["xr", "e16"], fk)
-        g4(t, 0, 64, ["rg0", "rg1", "rg2"], "V")
-        pe_c(t)
-        freal(t, 0)
-        freal(t, 1)
+    def move_w1():
+        dma("Y", T.wr[16:128, :], T.ww1[0:112, 512:1024], ["w1_1"], ["wr0"])
+        dma("Y", T.wr[0:16, :], T.ww1[112:128, 512:1024], ["w1_1"], ["wr1"])
 
-    def dense(t, h):
-        M, mk_ = tabs(t + 1)[4:6]
-        tt(M[:, 512 * h:512 * (h + 1)], T["fa%d" % t][:, 512 * h:512 * (h + 1)], psm[h][:], A.mult, ["fa%d_%d" % (t, h), "psm%d" % h], [mk_ + "h%d" % h] + [mk_] * h)
+    def out_lo():
+        tt(T.fin[:], T.ww3[:, 0:512], T.pst[:], A.add, ["w3_0", "pst"], ["fin"])
+        dma("Y", T.tl[:, 0:512], T.fin[:], ["fin"], ["tl0"])
 
-    def reports(t, eng, fill):
-        g4(t, 16, 48, ["rg1"])
-        if eng == "S":
-            freal(t, 0)
-        oldm(t, eng)
-        fac(t)
-        if eng == "S":
-            freal(t, 1)
-        g4(t, 0, 16, ["rg0"])
-        g4(t, 48, 64, ["rg2"])
-        scat(t)
-        pe_c(t)
+    def send_m():
+        send(lambda k: T.mm[:, 256 * k:256 * (k + 1)], lambda k: T.rm[:, 256 * k:256 * (k + 1)], T.sem.h_m, range(4), ["mm"])
 
-    g1(0, "S", 0, 32)
-    g2(0)
-    pe_m(0, 0)
-    g1(0, "V", 32, 64)
-    pe_a(0)
-    pe_m(0, 1)
-    lists1(0, "u", "V")
-    ts(T.oh[:], T.xx[:], T.qf[:, 0:1], None, A.is_equal, None, ["xx", "qf"], ["oh"])
-    lists2(0, "u", T.ul, 0, "V")
-    ts(T.bw[:], T.jj[:], T.qf[:, 0:1], 15.0, A.add, A.is_equal, ["jj", "qf"], ["bw"])
-    v_a(0)
-    pe_b(0)
-    gather1(256, "z", "S")
-    if not MODE0:
-        act(T.m1[:], T.mm[:], AF.Copy, 0.0, 2.0, ["mm"], ["m1"])
-    rho(0, 0)
-    fnull(0, 0)
-    rho(0, 1)
-    fnull(0, 1)
-    ts(T.v2[:, 0:64], T.rpi[:, 0:64], 2.0, None, A.mult, None, ["rpi"], ["v2_0"])
-    turn(256, "z")
-    lists2(256, "z", T.zl, 0, "S")
-    v_b(0)
-    dma("Y", T.uzt[16:128, 512:1024], T.uzt[0:112, 0:512], ["ut", "zt"], ["uzr0"])
-    dma("Y", T.uzt[0:16, 512:1024], T.uzt[112:128, 0:512], ["ut", "zt"], ["uzr1"])
-    if MODE0:
-        reports_s(0)
-        v_r(0)
-        g2(1, "S", 0, 32)
-        dense(0, 0)
-        dense(0, 1)
-        pe_six(0)
-        g1(1, "S", 0, 32)
-        g1(1, "V", 32, 64)
-        pe_a(1)
-        g2(1, "S", 32, 64)
-        pe_six(1)
-        weights(0, 0, 512)
-        ndense(1, 0)
-        ndense(1, 1)
-        v_a(1)
-        pe_m(1, 0)
-        pe_m(1, 1)
-        pe_b(1)
-        rho(1, 0)
-        fnull(1, 0)
-        rho(1, 1)
-        fnull(1, 1)
-        v_b(1)
-        reports(1, "V", None)
-        lo0 = 512
-    else:
-        reports(0, "V", None)
-        send(lambda k: T.m1[:, 256 * k:256 * (k + 1)], lambda k: T.rm[:, 256 * k:256 * (k + 1)], T.sem.h_m, range(4), ["m1"])
-        pe_six(0)
-        ndense(1, 0)
-        v_r(0)
-        pe_m(1, 0)
-        g1(1, "S", 0, 32)
-        g1(1, "V", 32, 64)
-        g2(1)
-        pe_a(1)
-        pe_six(1)
-        rho(1, 0)
-        freal(0, 0)
-        ndense(1, 1)
-        v_a(1)
-        pe_m(1, 1)
-        pe_b(1)
-        fnull(1, 0)
-        rho(1, 1)
-        fnull(1, 1)
-        freal(0, 1)
-        v_b(1)
-        lo0 = 512
-    send(lambda k: T.e16[:], lambda k: T.re16[:], T.sem.h_e, [0], ["e16"])
-    g4(1, 16, 48, ["rg1"])
-    send(lambda k: T.rg[:, 256 + 128 * k:384 + 128 * k], lambda k: T.rrg[:, 128 * k:128 * (k + 1)], T.sem.h_f, range(4), ["rg1"])
-    g4(1, 0, 16, ["rg0"], "V")
-    g4(1, 48, 64, ["rg2"], "V")
-    pe_c(1)
-    freal(1, 0)
-    freal(1, 1)
-    sclip(0, lo0, 1024, 0)
-    v_r(1)
-    dma("Y", T.c2[16:128, 32:64], T.cn1[0:112, 32:64], ["cn1"], ["c2a"])
-    dma("Y", T.c2[0:16, 32:64], T.cn1[112:128, 32:64], ["cn1"], ["c2b"])
-    sclip(0, lo0, 1024, 1)
-    sclip(0, lo0, 1024, 2)
-    lists2(0, "u", T.ul, 1, "S")
-    lists2(256, "z", T.zl, 1, "S")
-    sclip(0, 0, 512, 0)
-    act(T.old[:], T.rm[:].indirect(T.re16[:]), AF.Copy, 0.0, 1.0, ["rm", "re16"], ["old"])
-    sclip(0, 0, 512, 1)
-    sclip(0, 0, 512, 2)
-    pe_six(0)
-    pe_six(1)
-    dma("Y", T.tl[:, 512:1024], T.ww0[:, 512:1024], ["w0_1"], ["tl1", "tl2"])
-    weights(1, 512, 1024)
-    ts(T.i32[:], T.jj[:, 0:128], 0.0, None, A.is_equal, None, ["jj"], ["i32"])
-    clip(1, 512, 1024)
-    ts(T.v2[:, 64:96], T.rrp[:], 2.0, None, A.mult, None, ["rrp"], ["v2_1"])
-    cp(T.c216[:], T.c2[:], ["c2a", "c2b", "c2c"], ["c216", "c2"])
-    g2(2, "S", 0, 32)
-    ts(T.fac[:], T.rrg[:], 256.0, 0.5, A.is_le, A.max, ["rrg"], ["fac"])
-    tt(T.rm[:].indirect(T.re16[:]), T.old[:], T.fac[:], A.mult, ["old", "fac", "re16"], ["rm"])
-    dma("Y", T.wr[16:128, :], T.ww1[0:112, 512:1024], ["w1_1"], ["wr0"])
-    dma("Y", T.wr[0:16, :], T.ww1[112:128, 512:1024], ["w1_1"], ["wr1"])
-    dma("G", T.tl[:, 512:1024], T.ww1[:, 512:1024], ["w1_1"], ["tl1", "tl2"], True)
-    g1(2, "S", 0, 32)
-    g1(2, "V", 32, 64)
-    g2(2, "S", 32, 64)
-    ndense(2, 0)
-    ndense(2, 1)
-    pe_a(2)
-    weights(1, 0, 512)
-    pe_m(2, 0)
-    pe_m(2, 1)
-    v_a(2)
-    sclip(1, 0, 512, 0)
-    sclip(1, 0, 512, 1)
-    pe_b(2)
-    rho(2, 0)
-    fnull(2, 0)
-    rho(2, 1)
-    fnull(2, 1)
-    pe_sum(0, 0, 512)
-    v_b(2)
-    if MODE2:
-        reports_s(2)
-        pe_sum(1, 256, 512)
-        v_r(2)
-        g2(3, "S", 0, 32)
-        dense(2, 0)
-        dense(2, 1)
-        pe_six(0)
-        pe_six(1)
-        g1(3, "S", 0, 64)
-        pe_a(3)
-        g2(3, "S", 32, 64)
-        weights(2, 512, 1024)
-        weights(2, 0, 512)
-        clip(2, 512, 1024)
-        out_hi(2)
-        ndense(3, 0)
-        ndense(3, 1)
-        v_a(3)
-        pe_m(3, 0)
-        pe_m(3, 1)
-        sclip(2, 0, 512, 0)
-        pe_b(3)
-        rho(3, 0)
-        sclip(2, 0, 512, 1)
-        sclip(2, 0, 512, 2)
-        fnull(3, 0)
-    else:
-        reports(2, "S", None)
-        sclip(1, 0, 512, 2)
-        pe_six(0)
-        pe_sum(1, 0, 256)
-        ndense(3, 0)
-        v_r(2)
-        pe_m(3, 0)
-        g1(3, "S", 0, 64)
-        g2(3, "S", 0, 48)
-        pe_a(3)
-        pe_six(1)
-        pe_sum(1, 256, 512)
-        weights(2, 512, 1024)
-        weights(2, 0, 512)
-        clip(2, 512, 1024)
-        out_hi(2)
-        g2(3, "V", 48, 64)
-        ndense(3, 1)
-        v_a(3)
-        sclip(2, 0, 512, 0)
-        sclip(2, 0, 512, 1)
-        pe_m(3, 1)
-        pe_b(3)
-        rho(3, 0)
-        sclip(2, 0, 512, 2)
-        fnull(3, 0)
-    rho(3, 1)
-    fnull(3, 1)
-    pe_sum(2, 0, 256)
-    v_b(3)
-    g4(3, 0, 32, ["rg0"], "V")
-    g4(3, 32, 64, ["rg1", "rg2"])
-    pe_c(3)
-    pe_sum(2, 256, 512)
-    freal(3, 0)
-    freal(3, 1)
-    v_r(3)
-    weights(3, 512, 1024)
-    clip(3, 512, 1024)
-    out_hi(3)
-    weights(3, 0, 512)
-    clip(3, 0, 512)
-    tt(T.fin[:], T.ww3[:, 0:512], T.psr2[:], A.add, ["w3_0", "psr2"], ["fin"])
-    dma("Y", T.tl[:, 0:512], T.fin[:], ["fin"], ["tl0"])
+    def send_f():
+        send(lambda k: T.fac[:, 128 * k:128 * (k + 1)], lambda k: T.rfac[:, 128 * k:128 * (k + 1)], T.sem.h_f, range(4), ["fac"])
+
+    def send_e():
+        send(lambda k: T.e16[:], lambda k: T.re16[:], T.sem.h_e, [0], ["e16"])
+
+    dma("S", T.cei[:], T.ce[:], [], ["cei"])
+    rows(T.us, T.uu, "u", 0)
+    dma("S", T.mm[:], T.mj[:], [], ["mm"])
+    dma("Y", T.tab[:, 0:1024], T.nx[:], [], ["nx"])
+    dma("Y", T.tab[:, 1024:2048], T.sg[:], [], ["sg"])
+    dma("Y", T.rpi[:], T.rp[:], [], ["rpi"])
+    dma("S", T.tab[:, 2048:3072], T.al[:], [], ["al"])
+    rows(T.zs, T.zz, "z", 0)
+    for t in range(1, 4):
+        rows(T.us, T.uu, "u", t, ["al"])
+        rows(T.zs, T.zz, "z", t)
+    op("G", lambda: g.iota(T.qi[:], [[0, 8]], 0, 1), [], ["q0", "q1", "q2"])
+    op("G", lambda: g.iota(T.jj[:], [[1, 144]], 0, -1, allow_small_or_imprecise_dtypes=True), [], ["jj"])
+    con("kt")
+    for k in range(4):
+        op("G", lambda k=k: g.affine_select(T.bc[:, 512 * k:512 * (k + 1)], T.kt[:], [[-1, 4], [-16, 8], [0, 16]], A.is_equal, 0.0, -4 * k, 1),
+           ["kt"], ["bc%d" % k])
+    send(lambda k: T.rpi[:, 64:96], lambda k: T.rrp[:], T.sem.h_rp, [0], ["rpi"])
+    send(lambda k: T.tab[:, 768 * k:768 * (k + 1)], lambda k: T.rtab[:, 768 * k:768 * (k + 1)], T.sem.h_tab, range(4), ["nx", "sg", "al"])
+
+    con("cc"); con("q2"); con("q0"); con("q1"); con("k2"); con("sq"); con("i1"); con("qf"); con("six"); mul("S", "i2"); con("c0")
+    con("big"); con("ew"); con("msk"); diag("V", 9); diag("V", 10); diag("V", 8); diag("V", 6); con("bw"); pe_u(0); con("ce16")
+    diag("S", 11); diag("V", 0); diag("V", 4); diag("S", 2); diag("V", 12); diag("V", 15); diag("S", 5); con("c1"); diag("V", 7)
+    diag("S", 1); diag("V", 13); diag("V", 3)
+    pe_m(0, 1); g1(0, "S", 0, 32); g1(0, "V", 32, 64); pe_m(0, 0); diag("V", 14); mul("S", "i32"); g2(0, "V", 32, 64); g2(0, "S", 0, 32)
+    pe_a(0); rho(0, 0); cp_u("S", 0, 1); mul("S", "ez"); pe_o(); pe_d(1); sm(0, "xv"); pe_d(0); fnull(0, "S", 0)
+    sm(0, "pb"); con("cf"); mul("V", "dk"); rho(0, 1); pe_p(0); pe_p(1); sm(0, "v2"); pe_y(0); sel("S", 0); sel("V", 1)
+    edge(0, "S", 1); fnull(0, "S", 1); edge(0, "V", 0); pe_b(0); freal(0, 0); pe_b(1); pe_z(0); sm(0, "d16 yi")
+    pe_u(1); g4(0, "S", 0, 32); g4(0, "V", 32, 48); sm(0, "par"); g4(0, "V", 48, 64); sm(0, "ee db da")
+    pe_c(0); sm(0, "e16"); fac(0); sm(0, "sn"); old(0, "S", 0); old(0, "S", 1); sm(0, "ra rb"); cp_u("S", 1, 2)
+    sm(0, "cn"); scat(0); sm(0, "co"); send_m()
+    floor(1, 0); g1(1, "S", 32, 64); g1(1, "V", 0, 32); pe_m(1, 0)
+    g2(1, "S", 0, 48); floor(1, 1); freal(0, 1); pe_a(1); g2(1, "V", 48, 64); pe_m(1, 1); sclip(0, 0, 0); sm(1, "xv"); pe_d(1)
+    sm(1, "pb"); pe_d(0); rho(1, 0); pe_p(0); rho(1, 1); pe_p(1); pe_o(); sel("S", 0); pe_y(1); con("s32"); sel("V", 1)
+    edge(1, "S", 1); fnull(1, "S", 1); fnull(1, "V", 0); pe_b(0); pe_b(1); sclip(0, 1, 0); edge(1, "V", 0); pe_u(2)
+    sm(1, "yi d16 par"); g4(1, "S", 0, 48); fac(1); pe_u(3); pe_z(1); sm(1, "ee"); g4(1, "V", 48, 64); send_f()
+    sm(1, "e16"); sclip(0, 0, 1); cp_u("V", 2, 4); sm(1, "da"); freal(1, 0); pe_c(1); send_e(); sclip(0, 1, 1)
+    sm(1, "db sn"); freal(1, 1); sm(1, "rb"); sclip(0, 1, 2); sm(1, "ra cn"); sclip(0, 0, 2); out_hi(0); sm(1, "co")
+    pe_s(0); pe_s(1); pe_sum(0, 0, 512); sm(1, "c16"); weights(1, 1); cells2("S"); g2(2, "S", 16, 64); weights(1, 0); pe_o()
+    pe_z(2); clip(1, 1); move_w1(); out_hi(1); old(1, "V", 1); old(1, "S", 0); sclip(1, 0, 0); scat(1)
+    g2(2, "S", 0, 16); sclip(1, 0, 1); pe_d(1); sm(2, "v2"); pe_d(0); g1(2, "S", 0, 32); g1(2, "V", 32, 64); floor(2, 0)
+    floor(2, 1); pe_a(2); pe_m(2, 0); pe_m(2, 1); sm(2, "xv pb"); rho(2, 0); pe_p(0); rho(2, 1); pe_p(1)
+    edge(2, "S", 0); pe_y(2); sel("S", 0); sel("V", 1); sclip(1, 0, 2); fnull(2, "V", 0); pe_b(0); fnull(2, "S", 1); pe_b(1)
+    freal(2, 0); pe_sum(1, 0, 256); edge(2, "S", 1); sm(2, "yi d16 par"); g4(2, "S", 0, 32)
+    g4(2, "V", 32, 64); sm(2, "ee db da sn"); pe_c(2); sm(2, "e16"); fac(2); old(2, "S", 1)
+    pe_sum(1, 256, 512); old(2, "S", 0); sm(2, "ra rb cn"); scat(2); sm(2, "co")
+    floor(3, 0); g1(3, "S", 32, 64); g1(3, "V", 0, 32); pe_m(3, 0); g2(3, "S", 0, 32); pe_o(); g2(3, "V", 32, 64)
+    pe_a(3); freal(2, 1); pe_d(1); sm(3, "xv"); pe_d(0); sm(3, "pb"); floor(3, 1); rho(3, 0); pe_p(0)
+    pe_p(1); weights(2, 1); pe_m(3, 1); sel("S", 0); pe_y(3); sel("S", 1); rho(3, 1); pe_b(0); fnull(3, "S", 0); clip(2, 1)
+    pe_b(1); fnull(3, "S", 1); pe_z(3); edge(3, "V", 0); out_hi(2); edge(3, "S", 1); sm(3, "d16"); weights(2, 0)
+    g4(3, "S", 0, 48); sm(3, "yi"); g4(3, "V", 48, 64); sm(3, "db"); freal(3, 1); fnull3("S", 0); sm(3, "m2")
+    clip(2, 0); pe_c(3); fnull3("S", 1); freal(3, 0); pe_e(); pe_sum(2, 0, 256); sm(3, "on"); pe_sum(2, 256, 512)
+    weights(3, 1); weights(3, 0); clip(3, 1); clip(3, 0); out_hi(3); out_lo()
     emit(g, T, ops, ext)

@@ -12,7 +12,9 @@ SCRATCH = {
     "rm": ("sbuf", [128, 1024], "bfloat16"),
     "rpi": ("sbuf", [128, 96], "int32"),
     "rrp": ("sbuf", [128, 32], "int32"),
-    "v2": ("sbuf", [128, 96], "int32"),
+    "v2": ("sbuf", [128, 96], "float16"),
+    "yh": ("sbuf", [128, 64], "float16"),
+    "ih": ("sbuf", [128, 256], "float16"),
     "cei": ("sbuf", [128, 64], "int32"),
     "ce16": ("sbuf", [128, 64], "uint16"),
     "cf": ("sbuf", [128, 64], "float32"),
@@ -55,7 +57,7 @@ SCRATCH = {
     "ib": ("sbuf", [128, 128], "int32"),
     "par": ("sbuf", [128, 64], "int32"),
     "sn": ("sbuf", [128, 64], "float32"),
-    "ee": ("sbuf", [128, 32], "int32"),
+    "sd": ("sbuf", [128, 64], "float32"),
     "d16": ("sbuf", [128, 64], "uint16"),
     "e16": ("sbuf", [128, 32], "uint16"),
     "rb": ("sbuf", [128, 128], "int32"),
@@ -63,9 +65,9 @@ SCRATCH = {
     "c216": ("sbuf", [128, 64], "uint16"),
     "fl": ("sbuf", [128, 2048], "float32"),
     "wr": ("sbuf", [128, 512], "float32"),
-    "fin": ("sbuf", [128, 512], "float32"),
+    "fin": ("sbuf", [128, 1024], "float32"),
 }
-for _n in ("psa", "psc", "pss0", "pss1", "psm0", "psm1", "pst", "psu"):
+for _n in ("psa", "psc", "pss0", "pss1", "psm0", "psm1", "pst0", "pst1"):
     SCRATCH[_n] = ("psum", [128, 512], "float32")
 for _t in range(4):
     SCRATCH["ff%d" % _t] = ("sbuf", [128, 2560], "float32")
@@ -74,51 +76,38 @@ for _t in range(4):
     SCRATCH["co%d" % _t] = ("sbuf", [128, 128], "uint16")
 
 NDMA = 60
-SEMAPHORES = ["eV", "eS", "eP", "eG", "h_tab", "h_rp", "h_m", "a_tab", "a_rp", "a_m", "h_e", "h_f", "a_e", "a_f", "sent"] + ["d%d" % i for i in range(NDMA)]
+SENDS = {
+    "rp": [("l", "rrp", 0, 32, 1, "rrp")],
+    "tab": [("a", "rtab", 0, 1024, 2, "rnx"), ("b", "rtab", 1024, 2048, 4, "rsg"), ("c", "rtab", 2048, 3072, 4, "ral")],
+    "m": [("a", "rm", 0, 512, 2, "rm"), ("l", "rm", 512, 1024, 2, "rm2")],
+    "e": [("b", "re16", 0, 32, 1, "re16")],
+    "f": [("a", "rfac", 0, 256, 2, "rfac"), ("l", "rfac", 256, 512, 2, "rfac2")],
+}
+SEMAPHORES = ["eV", "eS", "eP", "eG", "sent"] + ["d%d" % i for i in range(NDMA)] + [
+    x + p[5] for x in ("h_", "a_") for pieces in SENDS.values() for p in pieces]
 
 
 def helpers(src, dst, T, topo):
-    def per_die(cands):
-        out = {}
-        for c in cands:
-            if T.rank_of(c) is None and topo.may_write(src, c) and topo.may_write(c, dst):
-                out.setdefault(topo.die(c), c)
-        return [out[d] for d in sorted(out)]
-    near = per_die(topo.cores_of(src))
-    far = per_die([c for c in range(SIM_CORES) if topo.mates(c, dst)])
-    return near + far
+    own = [c for c in topo.cores_of(src) if T.rank_of(c) is None]
+    same = [c for c in own if topo.die(c) == topo.die(src)]
+    a, b = [c for c in same if topo.may_write(c, dst)][:2]
+    l = [c for c in own if c not in same and topo.may_write(c, dst)][0]
+    c = [x for x in same if x not in (a, b)][0]
+    f = [x for x in range(SIM_CORES) if topo.mates(x, dst) and topo.die(x) == topo.die(c) and topo.may_write(c, x) and topo.may_write(x, dst)][0]
+    return {"a": a, "b": b, "l": l, "c": c, "f": f}
 
 
-def masks(src, hs, topo):
-    off = topo.engines(src, hs[2])
-    on = [e for e in topo.engines(src, hs[0]) if e not in off]
-    sets = [on[:len(on) // 2], on[len(on) // 2:], off[:len(off) // 2], off[len(off) // 2:]]
-    return [sum(1 << e for e in s) for s in sets], [len(s) for s in sets]
-
-
-def helper_program(g, core, src, dst, k, hs, T, topo):
-    _, cnt = masks(src, hs, topo)
-    rid, pid = topo.addr(dst, core)
-    m = topo.mask(core, dst)
-    n = len(topo.engines(core, dst))
+def helper_program(g, core, src, dst, role, hs, T, topo):
+    to = hs["f"] if role == "c" else dst
+    rid, pid = topo.addr(to, core)
     sent = 0
-    if k == 0:
-        g.wait_ge(T.sem.h_rp, cnt[k])
-        g.remote_dma(T.rrp[:], T.rrp[:], T.sem.a_rp, T.sem.sent, pid, rid, m)
-        sent += n
-    g.wait_ge(T.sem.h_tab, cnt[k])
-    g.remote_dma(T.rtab[:, 768 * k:768 * (k + 1)], T.rtab[:, 768 * k:768 * (k + 1)], T.sem.a_tab, T.sem.sent, pid, rid, m)
-    sent += n
-    g.wait_ge(T.sem.h_m, cnt[k])
-    g.remote_dma(T.rm[:, 256 * k:256 * (k + 1)], T.rm[:, 256 * k:256 * (k + 1)], T.sem.a_m, T.sem.sent, pid, rid, m)
-    sent += n
-    g.wait_ge(T.sem.h_f, cnt[k])
-    g.remote_dma(T.rfac[:, 128 * k:128 * (k + 1)], T.rfac[:, 128 * k:128 * (k + 1)], T.sem.a_f, T.sem.sent, pid, rid, m)
-    sent += n
-    if k == 0:
-        g.wait_ge(T.sem.h_e, cnt[k])
-        g.remote_dma(T.re16[:], T.re16[:], T.sem.a_e, T.sem.sent, pid, rid, m)
-        sent += n
+    for pieces in SENDS.values():
+        for h, buf, a, b, share, key in pieces:
+            if h != ("c" if role == "f" else role):
+                continue
+            g.wait_ge(T.sem["h_" + key], len(topo.engines(hs["c"], core)) if role == "f" else len(topo.engines(src, core)) // share)
+            g.remote_dma(T[buf][:, a:b], T[buf][:, a:b], T.sem[("h_" if role == "c" else "a_") + key], T.sem.sent, pid, rid, topo.mask(core, to))
+            sent += len(topo.engines(core, to))
     g.wait_ge(T.sem.sent, sent)
 
 
@@ -193,16 +182,14 @@ def rank_program(g, core, T, topo):
         for s in range(N):
             src, dst = T.cores[s], T.cores[(s - HOP) % N]
             hs = helpers(src, dst, T, topo)
-            if core in hs:
-                helper_program(g, core, src, dst, hs.index(core), hs, T, topo)
+            for role in hs:
+                if hs[role] == core:
+                    helper_program(g, core, src, dst, role, hs, T, topo)
         return
     dst = T.cores[(rank - HOP) % N]
     hs = helpers(core, dst, T, topo)
-    mk, cnt = masks(core, hs, topo)
     hin = helpers(T.cores[(rank + HOP) % N], core, T, topo)
-    nin = [len(topo.engines(h, core)) for h in hin]
-    ext = {"rtab": ("a_tab", sum(nin)), "rrp": ("a_rp", nin[0]), "rm": ("a_m", sum(nin)),
-           "re16": ("a_e", nin[0]), "rfac": ("a_f", sum(nin))}
+    ext = {p[5]: ("a_" + p[5], len(topo.engines(hin["f" if p[0] == "c" else p[0]], core))) for pieces in SENDS.values() for p in pieces}
 
     ops = []
     V, S, P = g.vector, g.scalar, g.tensor
@@ -246,15 +233,18 @@ def rank_program(g, core, T, topo):
             return ins
         op("P", fn, rd, wr)
 
-    def send(src_of, dst_of, sem, ks, rd):
+    def send(name, buf, first, rd):
         def fn(s):
-            tr = []
-            for k in ks:
-                rid, pid = topo.addr(hs[k], core)
-                tr.append(RemoteDMATransfer(dst_ids=[DstId(rid=rid, pnc=pid)], dma_engine_mask=mk[k], remote_sem=sem,
-                                            src=src_of(k), dst=dst_of(k)))
+            tr, used = [], 0
+            for h, far, a, b, share, key in SENDS[name]:
+                rid, pid = topo.addr(hs[h], core)
+                every = topo.engines(core, hs[h])
+                mine = every[used:used + len(every) // share]
+                used += len(mine)
+                tr.append(RemoteDMATransfer(dst_ids=[DstId(rid=rid, pnc=pid)], dma_engine_mask=sum(1 << e for e in mine),
+                                            remote_sem=T.sem["h_" + key], src=buf[:, first + a:first + b], dst=T[far][:, a:b]))
             g.remote_dma_fused(tr, local_sem=s)
-            return sum(cnt[k] for k in ks)
+            return used
         op("G", fn, rd, [], "r")
 
     def rows(buf, src, key, t, rd=()):
@@ -278,6 +268,9 @@ def rank_program(g, core, T, topo):
             cp(T.qf[:], T.qi[:, 0:4], ["q0", "q1", "q2"], [n])
         if n == "i1":
             ts(T.i1[:], jq, 0.0, None, A.is_equal, None, ["jj"], [n])
+        if n in ("ih0", "ih1"):
+            k = int(n[2])
+            ts(T.ih[:, 128 * k:128 * (k + 1)], jq, 0.0, (1.0, -2.0)[k], A.is_equal, A.mult, ["jj"], [n])
         if n == "big":
             ts(T.big[:], T.jj[:, 0:16], T.qf[:, 1:2], 256.0, A.add, A.mult, ["jj", "qf"], [n])
         if n == "msk":
@@ -316,10 +309,10 @@ def rank_program(g, core, T, topo):
             [ek] + [key + "%d%s" % (t, x) for x in ("", "a", "b")], [bank], start, stop)
 
     def pe_u(t):
-        spread(T.psu[:, 64 * t:64 * (t + 1)], "ew", T.us, "u", t, "psu", True, True)
+        spread(T.pst0[:, 64 * t:64 * (t + 1)], "ew", T.us, "u", t, "psu", True, True)
 
     def cp_u(eng, a, b):
-        lin(eng, T.ul[:, 64 * a:64 * b], T.psu[:, 64 * a:64 * b], 1.0, 0.0, ["psu"], ["ul%d" % t for t in range(a, b)])
+        lin(eng, T.ul[:, 64 * a:64 * b], T.pst0[:, 64 * a:64 * b], 1.0, 0.0, ["psu"], ["ul%d" % t for t in range(a, b)])
 
     def pe_o():
         mms([(T.psc[:, 0:64], T.i32[:], T.cc[:])], ["i32", "cc"], ["psc"], True, False)
@@ -331,14 +324,14 @@ def rank_program(g, core, T, topo):
     psm, pss = [T.psm0, T.psm1], [T.pss0, T.pss1]
 
     def tabs(t):
-        return (T.tab, "nx", "sg", "al", T.mm, "mm") if t < 2 else (T.rtab, "rtab", "rtab", "rtab", T.rm, "rm")
+        return (T.tab, "nx", "sg", "al", T.mm, "mm") if t < 2 else (T.rtab, "rnx", "rsg", "ral", T.rm, "rm")
 
     def cells(t):
         if t == 0:
             return T.cf[:], "cf", T.ce16, "ce16"
         if t == 2:
             return T.c2[:], "c2", T.c216, "c216"
-        return T["cn%d" % (t - 1)][:, 0:64], "cn%d" % (t - 1), T["co%d" % (t - 1)], "co%d" % (t - 1)
+        return T["cn%d" % (t - 1)][:, 0:64], "cn%d" % (t - 1), T["co%d" % (t - 1)], "cu%d" % (t - 1)
 
     def parts(name, a, b):
         return [name + "%d" % h for h in range(a // 8, b // 8)]
@@ -422,27 +415,34 @@ def rank_program(g, core, T, topo):
                 cp(T.yi[:], T.psa[:, 64:128], ["psa"], ["yi"])
             if n == "par":
                 ts(T.par[:], T.yi[:], 1, None, A.bitwise_and, None, ["yi"], ["par"])
-            if n == "ee":
-                tt(T.ee[:], T.par[:, 16:48], T.v2[:, 32 * t:32 * (t + 1)], A.add, ["par", "v2_%d" % (t // 2)], ["ee"])
+            if n == "ya":
+                ts(T.yh[:, 0:32], T.psa[:, 80:112], 8 * KK + 512, None, A.add, None, ["psa"], ["ya"])
+            if n == "yb":
+                ts(T.yh[:, 32:64], T.psa[:, 80:112], 0.5, 4 * KK + 1151.75, A.mult, A.add, ["psa"], ["yb"])
             if n == "e16":
-                cp(T.e16[:], T.ee[:], ["ee"], ["e16"])
-            if n == "da":
-                ts(T.ib[:, 0:64], T.yi[:], 1023, None, A.bitwise_and, None, ["yi"], ["ibe"])
+                ts(T.e16[:], T.psa[:, 128:160], 1792.0, None, A.add, None, ["psa"], ["e16"])
             if n == "db":
                 ts(T.ib[:, 64:128], T.yi[:], 1023, None, A.bitwise_and, None, ["yi"], ["ibd"])
             if n == "sn":
                 ts(T.sn[:], T.par[:], 2.0, -1.0, A.mult, A.add, ["par"], ["sn"])
-            if n == "ra":
-                tt(T.rb[:, 0:64], T.psc[:, 0:64], T.sn[:], A.mult, ["psc", "sn"], ["rbe"])
-            if n == "rb":
-                ts(T.rb[:, 64:128], T.psc[:, 0:64], -0.5, 1280.0, A.is_lt, A.mult, ["psc"], ["rbd"])
-            if n == "cn":
-                tt(cn[:], T.ib[:], T.rb[:], A.add, ["ibe", "ibd", "rbe", "rbd"], ["cn%d" % t])
-            if n == "co":
-                a = 64 * (t % 2)
-                cp(co[:, a:128], cn[:, a:128], ["cn%d" % t], ["co%d" % t])
+            if n == "sd":
+                tt(T.sd[:], T.ib[:, 64:128], T.sn[:], A.mult, ["ibd", "sn"], ["sd"])
+            if n == "nc":
+                tt(T.ib[:, 0:64], T.psc[:, 0:64], T.sn[:], A.mult, ["psc", "sn"], ["ibe"])
+            if n == "nu":
+                cp(co[:, 0:64], T.ib[:, 0:64], ["ibe"], ["cu%d" % t])
+            if n == "nf":
+                cp(cn[:, 0:64], T.ib[:, 0:64], ["ibe"], ["cn%d" % t])
+            if n == "ne":
+                tt(T.rb[:, 0:64], T.ib[:, 0:64], T.ib[:, 64:128], A.not_equal, ["ibe", "ibd"], ["rbe"])
+            if n == "nm":
+                ts(T.rb[:, 64:128], T.rb[:, 0:64], 1280.0, None, A.mult, None, ["rbe"], ["rbd"])
+            if n == "na":
+                tt(cn[:, 64:128], T.rb[:, 64:128], T.ib[:, 64:128], A.add, ["rbd", "ibd"], ["cw%d" % t])
+            if n == "no":
+                cp(co[:, 64:128], cn[:, 64:128], ["cw%d" % t], ["co%d" % t])
             if n == "m2":
-                ts(T.sn[:], T.ib[:, 64:128], -2.0, None, A.mult, None, ["ibd"], ["sn"])
+                ts(T.sd[:], T.ib[:, 64:128], -2.0, None, A.mult, None, ["ibd"], ["sd"])
             if n == "on":
                 ts(co[:, 64:128], T.psc[:, 0:64], -1.0, None, A.mult, None, ["psc"], ["co%d" % t])
             if n == "v2":
@@ -450,6 +450,11 @@ def rank_program(g, core, T, topo):
                 ts(T.v2[:, a:b], src, 2.0, None, A.mult, None, [rd], ["v2_%d" % (t // 2)])
             if n == "c16":
                 cp(T.c216[:], T.psc[:, 64:128], ["psc"], ["c216"])
+
+    def pe_r(t):
+        o = T.psa[:, 128:160]
+        mms([(o, T.ih[:, 0:128], T.v2[:, 32 * t:32 * (t + 1)]), (o, T.ih[:, 0:128], T.yh[:, 0:32]), (o, T.ih[:, 128:256], T.yh[:, 32:64])],
+            ["ih0", "ih1", "v2_%d" % (t // 2), "ya", "yb"], ["psa"])
 
     def cells2(eng):
         lin(eng, T.c2[:], T.psc[:, 64:128], 1.0, 0.0, ["psc"], ["c2"])
@@ -472,24 +477,23 @@ def rank_program(g, core, T, topo):
     def old(t, eng, h):
         M, mk_ = tabs(t + 1)[4:6]
         e, ek = (T.re16, "re16") if t == 1 else (T.e16, "e16")
-        lin(eng, T.old[:, 256 * h:256 * (h + 1)], M[:].indirect(e[:, 16 * h:16 * (h + 1)]), 1.0, 0.0, [mk_, ek], ["old%d" % h])
+        lin(eng, T.old[:, 256 * h:256 * (h + 1)], M[:].indirect(e[:, 16 * h:16 * (h + 1)]), 1.0, 0.0, [mk_, ek] + ["rm2"] * (t == 1), ["old%d" % h])
 
-    def scat(t):
+    def scat(t, h):
         M, mk_ = tabs(t + 1)[4:6]
         e, f = ("re16", "rfac") if t == 1 else ("e16", "fac")
-        tt(M[:].indirect(T[e][:]), T.old[:], T[f][:], A.mult, ["old0", "old1", f, e], [mk_])
+        a, b = ((0, 16), (16, 32), (0, 32))[h]
+        tt(M[:].indirect(T[e][:, a:b]), T.old[:, 16 * a:16 * b], T[f][:, 16 * a:16 * b], A.mult, ["old0", "old1", f, e] + ["rfac2"] * (t == 1), [mk_])
 
     def pe_c(t):
         mms([(T.psc[:, 0:64], T.dm[:, 128 * i:128 * (i + 1)], T.rg[:, i:1024:16]) for i in range(16)],
-            parts("rg", 0, 64) + DM, ["psc"], False, t < 3)
+            parts("rg", 0, 64) + DM, ["psc"], False, False)
 
     def pe_e():
-        mms([(T.psc[:, 0:64], T.i32[:], T.sn[:])], ["i32", "sn"], ["psc"], False, True)
+        mms([(T.psc[:, 0:64], T.i32[:], T.sd[:])], ["i32", "sd"], ["psc"], False, True)
 
     def factor(t, h):
         off = T["co%d" % t][:, 64 + 32 * h:96 + 32 * h]
-        if t == 3:
-            return T.fl[:].indirect(off), ["fm0", "fm1", "fr3_0", "fr3_1", "co3"]
         return T["ff%d" % t][:, 256:2560].indirect(off), [k % t for k in ("fn%d_0", "fn%d_1", "fe%d_0", "fr%d_0", "fr%d_1", "co%d")]
 
     def weights(t, h):
@@ -506,48 +510,58 @@ def rank_program(g, core, T, topo):
         w, key = T["ww%d" % t][:, 512 * h:512 * (h + 1)], ["w%d_%d" % (t, h)]
         ts(w, w, 0.125, 4.0, A.max, A.min, key, key)
 
+    BOUNDS = ((AF.Relu, 4.0, -1.0), (AF.Relu, 3.875, -1.0), (AF.Identity, 0.125, 1.0))
+
     def sclip(t, h, k):
         w, key = T["ww%d" % t][:, 512 * h:512 * (h + 1)], ["w%d_%d" % (t, h)]
-        f, bias, scale = ((AF.Relu, 4.0, -1.0), (AF.Relu, 3.875, -1.0), (AF.Identity, 0.125, 1.0))[k]
+        f, bias, scale = BOUNDS[k]
         src, rd = factor(t, h) if t == 0 and k == 0 else (w, key)
         act(w, src, f, bias, scale, rd, key)
 
-    def pe_sum(t, a, b):
-        op("P", lambda: P.matmul(T.pst[:, a:b], T.i32[:], T["ww%d" % t][:, a:b], t == 0, t == 2 and b == 512),
-           ["i32", "w%d_0" % t], ["pst"])
-
-    def out_hi(t):
-        w, rd = T["ww%d" % t], ["w%d_1" % t]
-        if t < 2:
-            dma("YG"[t], T.tl[:, 512:1024], w[:, 512:1024], rd, ["tl1", "tl2"], t == 1)
-        else:
-            dma("G", T.tl[0:112, 512:1024], w[16:128, 512:1024], rd, ["tl1"], True)
-            dma("G", T.tl[112:128, 512:1024], w[0:16, 512:1024], rd, ["tl2"], True)
+    def pe_sum(t, k):
+        h, a = k // 2, 256 * (k % 2)
+        m = "s32" if h == 1 and t < 2 else "i32"
+        mms([(T["pst%d" % h][:, a:a + 256], T[m][:], T["ww%d" % t][:, 256 * k:256 * (k + 1)])], [m, "w%d_%d" % (t, h)],
+            ["pst%d" % h] + ["psu"] * (t + k == 0), t == 0 and a == 0, t == 2 and k in (0, 3))
 
     def move_w1():
         dma("Y", T.wr[16:128, :], T.ww1[0:112, 512:1024], ["w1_1"], ["wr0"])
         dma("Y", T.wr[0:16, :], T.ww1[112:128, 512:1024], ["w1_1"], ["wr1"])
 
-    def out_lo():
-        tt(T.fin[:], T.ww3[:, 0:512], T.pst[:], A.add, ["w3_0", "pst"], ["fin"])
-        dma("Y", T.tl[:, 0:512], T.fin[:], ["fin"], ["tl0"])
+    def last(n, k):
+        a = 256 * k
+        w, key = T.ww3[:, a:a + 256], ["w3_%d" % k]
+        if n == "w":
+            tt(w, T.fl[:].indirect(T.co3[:, 64 + 16 * k:80 + 16 * k]), T.ww2[:, a:a + 256], A.mult,
+               ["fm0", "fm1", "fr3_0", "fr3_1", "co3", "w2_%d" % (k // 2)], key)
+        if n == "c":
+            ts(w, w, 0.125, 4.0, A.max, A.min, key, key)
+        if n[0] == "s":
+            f, bias, scale = BOUNDS[int(n[1])]
+            act(w, w, f, bias, scale, key, key)
+        if n == "a":
+            tt(T.fin[:, a:a + 256], w, T["pst%d" % (k // 2)][:, a % 512:a % 512 + 256], A.add, key + ["pst%d" % (k // 2)], ["fin%d" % k])
+
+    def out(q, p, a, b):
+        src, to = {0: (slice(0, 128), slice(0, 128)), 1: (slice(16, 128), slice(0, 112)), 2: (slice(0, 16), slice(112, 128))}[p]
+        dma(q, T.tl[to, 256 * a:256 * b], T.fin[src, 256 * a:256 * b], ["fin%d" % k for k in range(a, b)], ["tl%d%d" % (p, a)])
 
     def send_m():
-        send(lambda k: T.mm[:, 256 * k:256 * (k + 1)], lambda k: T.rm[:, 256 * k:256 * (k + 1)], T.sem.h_m, range(4), ["mm"])
+        send("m", T.mm, 0, ["mm"])
 
     def send_f():
-        send(lambda k: T.fac[:, 128 * k:128 * (k + 1)], lambda k: T.rfac[:, 128 * k:128 * (k + 1)], T.sem.h_f, range(4), ["fac"])
+        send("f", T.fac, 0, ["fac"])
 
     def send_e():
-        send(lambda k: T.e16[:], lambda k: T.re16[:], T.sem.h_e, [0], ["e16"])
+        send("e", T.e16, 0, ["e16"])
 
     dma("S", T.cei[:], T.ce[:], [], ["cei"])
-    rows(T.us, T.uu, "u", 0)
-    dma("S", T.mm[:], T.mj[:], [], ["mm"])
+    dma("Y", T.mm[:], T.mj[:], [], ["mm"])
+    dma("S", T.us[0:8, :], T.uu[:, 0:1024], [], ["u0"])
     dma("Y", T.tab[:, 0:1024], T.nx[:], [], ["nx"])
     dma("Y", T.tab[:, 1024:2048], T.sg[:], [], ["sg"])
     dma("Y", T.rpi[:], T.rp[:], [], ["rpi"])
-    dma("S", T.tab[:, 2048:3072], T.al[:], [], ["al"])
+    dma("Y", T.tab[:, 2048:3072], T.al[:], [], ["al"])
     rows(T.zs, T.zz, "z", 0)
     for t in range(1, 4):
         rows(T.us, T.uu, "u", t, ["al"])
@@ -558,40 +572,43 @@ def rank_program(g, core, T, topo):
     for k in range(4):
         op("G", lambda k=k: g.affine_select(T.bc[:, 512 * k:512 * (k + 1)], T.kt[:], [[-1, 4], [-16, 8], [0, 16]], A.is_equal, 0.0, -4 * k, 1),
            ["kt"], ["bc%d" % k])
-    send(lambda k: T.rpi[:, 64:96], lambda k: T.rrp[:], T.sem.h_rp, [0], ["rpi"])
-    send(lambda k: T.tab[:, 768 * k:768 * (k + 1)], lambda k: T.rtab[:, 768 * k:768 * (k + 1)], T.sem.h_tab, range(4), ["nx", "sg", "al"])
+    send("tab", T.tab, 0, ["nx", "sg", "al"])
+    send("rp", T.rpi, 64, ["rpi"])
 
-    con("cc"); con("q2"); con("q0"); con("q1"); con("k2"); con("sq"); con("i1"); con("qf"); con("six"); mul("S", "i2"); con("c0")
-    con("big"); con("ew"); con("msk"); diag("V", 9); diag("V", 10); diag("V", 8); diag("V", 6); con("bw"); pe_u(0); con("ce16")
-    diag("S", 11); diag("V", 0); diag("V", 4); diag("S", 2); diag("V", 12); diag("V", 15); diag("S", 5); con("c1"); diag("V", 7)
-    diag("S", 1); diag("V", 13); diag("V", 3)
-    pe_m(0, 1); g1(0, "S", 0, 32); g1(0, "V", 32, 64); pe_m(0, 0); diag("V", 14); mul("S", "i32"); g2(0, "V", 32, 64); g2(0, "S", 0, 32)
-    pe_a(0); rho(0, 0); cp_u("S", 0, 1); mul("S", "ez"); pe_o(); pe_d(1); sm(0, "xv"); pe_d(0); fnull(0, "S", 0)
-    sm(0, "pb"); con("cf"); mul("V", "dk"); rho(0, 1); pe_p(0); pe_p(1); sm(0, "v2"); pe_y(0); sel("S", 0); sel("V", 1)
-    edge(0, "S", 1); fnull(0, "S", 1); edge(0, "V", 0); pe_b(0); freal(0, 0); pe_b(1); pe_z(0); sm(0, "d16 yi")
-    pe_u(1); g4(0, "S", 0, 32); g4(0, "V", 32, 48); sm(0, "par"); g4(0, "V", 48, 64); sm(0, "ee db da")
-    pe_c(0); sm(0, "e16"); fac(0); sm(0, "sn"); old(0, "S", 0); old(0, "S", 1); sm(0, "ra rb"); cp_u("S", 1, 2)
-    sm(0, "cn"); scat(0); sm(0, "co"); send_m()
-    floor(1, 0); g1(1, "S", 32, 64); g1(1, "V", 0, 32); pe_m(1, 0)
-    g2(1, "S", 0, 48); floor(1, 1); freal(0, 1); pe_a(1); g2(1, "V", 48, 64); pe_m(1, 1); sclip(0, 0, 0); sm(1, "xv"); pe_d(1)
-    sm(1, "pb"); pe_d(0); rho(1, 0); pe_p(0); rho(1, 1); pe_p(1); pe_o(); sel("S", 0); pe_y(1); con("s32"); sel("V", 1)
-    edge(1, "S", 1); fnull(1, "S", 1); fnull(1, "V", 0); pe_b(0); pe_b(1); sclip(0, 1, 0); edge(1, "V", 0); pe_u(2)
-    sm(1, "yi d16 par"); g4(1, "S", 0, 48); fac(1); pe_u(3); pe_z(1); sm(1, "ee"); g4(1, "V", 48, 64); send_f()
-    sm(1, "e16"); sclip(0, 0, 1); cp_u("V", 2, 4); sm(1, "da"); freal(1, 0); pe_c(1); send_e(); sclip(0, 1, 1)
-    sm(1, "db sn"); freal(1, 1); sm(1, "rb"); sclip(0, 1, 2); sm(1, "ra cn"); sclip(0, 0, 2); out_hi(0); sm(1, "co")
-    pe_s(0); pe_s(1); pe_sum(0, 0, 512); sm(1, "c16"); weights(1, 1); cells2("S"); g2(2, "S", 16, 64); weights(1, 0); pe_o()
-    pe_z(2); clip(1, 1); move_w1(); out_hi(1); old(1, "V", 1); old(1, "S", 0); sclip(1, 0, 0); scat(1)
-    g2(2, "S", 0, 16); sclip(1, 0, 1); pe_d(1); sm(2, "v2"); pe_d(0); g1(2, "S", 0, 32); g1(2, "V", 32, 64); floor(2, 0)
-    floor(2, 1); pe_a(2); pe_m(2, 0); pe_m(2, 1); sm(2, "xv pb"); rho(2, 0); pe_p(0); rho(2, 1); pe_p(1)
-    edge(2, "S", 0); pe_y(2); sel("S", 0); sel("V", 1); sclip(1, 0, 2); fnull(2, "V", 0); pe_b(0); fnull(2, "S", 1); pe_b(1)
-    freal(2, 0); pe_sum(1, 0, 256); edge(2, "S", 1); sm(2, "yi d16 par"); g4(2, "S", 0, 32)
-    g4(2, "V", 32, 64); sm(2, "ee db da sn"); pe_c(2); sm(2, "e16"); fac(2); old(2, "S", 1)
-    pe_sum(1, 256, 512); old(2, "S", 0); sm(2, "ra rb cn"); scat(2); sm(2, "co")
-    floor(3, 0); g1(3, "S", 32, 64); g1(3, "V", 0, 32); pe_m(3, 0); g2(3, "S", 0, 32); pe_o(); g2(3, "V", 32, 64)
-    pe_a(3); freal(2, 1); pe_d(1); sm(3, "xv"); pe_d(0); sm(3, "pb"); floor(3, 1); rho(3, 0); pe_p(0)
-    pe_p(1); weights(2, 1); pe_m(3, 1); sel("S", 0); pe_y(3); sel("S", 1); rho(3, 1); pe_b(0); fnull(3, "S", 0); clip(2, 1)
-    pe_b(1); fnull(3, "S", 1); pe_z(3); edge(3, "V", 0); out_hi(2); edge(3, "S", 1); sm(3, "d16"); weights(2, 0)
-    g4(3, "S", 0, 48); sm(3, "yi"); g4(3, "V", 48, 64); sm(3, "db"); freal(3, 1); fnull3("S", 0); sm(3, "m2")
-    clip(2, 0); pe_c(3); fnull3("S", 1); freal(3, 0); pe_e(); pe_sum(2, 0, 256); sm(3, "on"); pe_sum(2, 256, 512)
-    weights(3, 1); weights(3, 0); clip(3, 1); clip(3, 0); out_hi(3); out_lo()
+    con("q1"); con("q0"); con("q2"); con("six"); con("cc"); con("sq"); con("qf"); con("i1"); con("big"); mul("S", "i2")
+    con("c1"); con("c0"); mul("S", "dk"); mul("S", "i32"); con("msk"); diag("V", 0); diag("V", 1); con("ew"); diag("V", 2)
+    diag("V", 3); diag("S", 10); diag("S", 11); pe_u(0); diag("S", 12); con("ce16"); diag("V", 4); diag("S", 13); diag("V", 5)
+    diag("V", 6); diag("S", 14); diag("V", 7); diag("V", 8); diag("S", 15); diag("V", 9)
+    g1(0, "V", 32, 64); g1(0, "S", 0, 32)
+    pe_m(0, 0); g2(0, "V", 32, 64); g2(0, "S", 0, 32); pe_a(0); rho(0, 0); cp_u("S", 0, 1); pe_m(0, 1); pe_d(0)
+    sm(0, "xv v2"); pe_d(1); edge(0, "S", 0); sm(0, "pb"); con("cf"); con("bw"); fnull(0, "S", 0); con("ih1")
+    con("k2"); rho(0, 1); pe_p(0); pe_p(1); con("ih0"); sel("S", 0); pe_y(0); sel("V", 1); mul("S", "ez"); fnull(0, "S", 1)
+    pe_b(0); freal(0, 0); pe_b(1); edge(0, "S", 1); pe_o(); pe_z(0); sm(0, "d16 yi ya yb")
+    g4(0, "S", 16, 48); sm(0, "par db"); pe_r(0); g4(0, "V", 48, 64); sm(0, "e16"); g4(0, "V", 0, 16)
+    old(0, "S", 0); sm(0, "sn"); fac(0); pe_c(0); old(0, "S", 1); sm(0, "sd"); freal(0, 1); pe_e(); pe_u(1); scat(0, 0); cp_u("S", 1, 2)
+    sm(0, "nc"); pe_o(); pe_z(1); con("s32"); sm(0, "nu"); scat(0, 1); g2(1, "S", 0, 16); sm(0, "nf"); send_m()
+    g1(1, "V", 32, 64); g1(1, "S", 0, 32); sm(0, "ne"); g2(1, "S", 16, 48); floor(1, 0); pe_a(1); floor(1, 1); g2(1, "V", 48, 64)
+    pe_m(1, 1); sm(0, "nm"); sm(1, "xv"); pe_m(1, 0); sm(1, "pb"); pe_d(0); rho(1, 1); pe_d(1); sm(0, "na"); pe_p(0); rho(1, 0)
+    pe_p(1); sm(0, "no"); sel("S", 0); pe_y(1); sel("V", 1); edge(1, "S", 1); edge(1, "S", 0); pe_b(0); fnull(1, "S", 0)
+    fnull(1, "V", 1); pe_b(1); pe_u(2); sm(1, "d16 ya yi yb"); g4(1, "S", 0, 64); fac(1); pe_r(1)
+    pe_u(3); sm(1, "e16 par"); freal(1, 0); send_e(); sm(1, "sn"); send_f(); sm(1, "db")
+    freal(1, 1); sclip(0, 1, 0); pe_c(1); sm(1, "sd"); weights(0, 0); pe_e(); sclip(0, 1, 1); sm(1, "nc"); cp_u("S", 2, 4)
+    sm(1, "ne nf"); sclip(0, 1, 2); sm(1, "nm"); pe_s(0); pe_s(1); sm(1, "na"); pe_sum(0, 0); sm(2, "v2"); sm(1, "no c16")
+    cells2("V"); pe_sum(0, 2); weights(1, 1); g2(2, "S", 0, 16); pe_o(); pe_z(2); weights(1, 0); old(1, "S", 1)
+    old(1, "S", 0); pe_sum(0, 3); clip(1, 1); g2(2, "S", 16, 64); scat(1, 2); pe_sum(0, 1); move_w1(); pe_d(0); pe_d(1)
+    g1(2, "V", 32, 64); g1(2, "S", 0, 32); floor(2, 1); floor(2, 0); pe_a(2)
+    clip(1, 0); pe_m(2, 0); sm(2, "xv"); pe_m(2, 1); sm(2, "pb"); rho(2, 0); pe_p(0); rho(2, 1); pe_p(1); sel("S", 0); pe_y(2)
+    sel("V", 1); edge(2, "S", 1); fnull(2, "S", 0); pe_b(0); fnull(2, "V", 1); pe_b(1); edge(2, "S", 0); sm(2, "d16 yi yb ya")
+    g4(2, "S", 16, 48); sm(2, "par"); g4(2, "V", 0, 16); pe_r(2); pe_sum(1, 0)
+    sm(2, "sn e16"); g4(2, "V", 48, 64); old(2, "S", 0); pe_sum(1, 1); sm(2, "db"); fac(2); old(2, "S", 1); freal(2, 0)
+    pe_c(2); sm(2, "sd"); scat(2, 0); pe_e(); pe_sum(1, 2); sm(2, "nc"); pe_o(); pe_z(3); pe_sum(1, 3); sm(2, "nu"); scat(2, 1); g2(3, "S", 0, 16); sm(2, "ne")
+    g1(3, "S", 0, 32); g1(3, "V", 32, 64); sm(2, "nm"); g2(3, "S", 16, 64); floor(3, 0); pe_a(3); floor(3, 1); freal(2, 1)
+    pe_m(3, 0); sm(2, "na"); sm(3, "xv"); sm(2, "nf"); pe_m(3, 1); sm(2, "no"); sm(3, "pb"); rho(3, 0); pe_d(0); pe_p(0)
+    weights(2, 1); pe_d(1); edge(3, "S", 0); pe_p(1); sel("S", 0); rho(3, 1); pe_y(3); sel("S", 1); weights(2, 0); pe_b(0)
+    fnull(3, "S", 0); pe_b(1); clip(2, 1); edge(3, "S", 1); fnull(3, "S", 1); sm(3, "yi d16"); clip(2, 0)
+    pe_sum(2, 2); g4(3, "S", 0, 32); g4(3, "V", 32, 64); sm(3, "db")
+    fnull3("S", 1); freal(3, 0); pe_c(3); sm(3, "m2"); freal(3, 1); fnull3("S", 0); pe_e(); pe_sum(2, 1); pe_sum(2, 0); sm(3, "on")
+    last("w", 2); pe_sum(2, 3); last("w", 3); last("s0", 2); last("w", 1); last("s0", 3); last("w", 0); last("s1", 2)
+    last("c", 1); last("s1", 3); last("c", 0); last("s2", 2); last("a", 1); last("s2", 3); last("a", 0); out("Y", 0, 0, 2)
+    last("a", 2); last("a", 3); out('S', 1, 2, 4); out("Y", 2, 2, 4)
     emit(g, T, ops, ext)

from concourse.bass import DstId, RemoteDMATransfer
from concourse.mybir import AluOpType as A, ActivationFunctionType as AF

SIM_CORES = 256
HOP = 3
KK = 98304.0

SCRATCH = {
    "tab": ("sbuf", [128, 3072], "bfloat16"),
    "rtab": ("sbuf", [128, 3072], "bfloat16"),
    "mm": ("sbuf", [128, 1024], "bfloat16"),
    "rm": ("sbuf", [128, 1024], "bfloat16"),
    "rpi": ("sbuf", [128, 96], "int32"),
    "rrp": ("sbuf", [128, 32], "int32"),
    "v2": ("sbuf", [128, 96], "float16"),
    "yh": ("sbuf", [128, 64], "float16"),
    "ih": ("sbuf", [128, 256], "float16"),
    "cei": ("sbuf", [128, 64], "int32"),
    "ce16": ("sbuf", [128, 64], "uint16"),
    "cf": ("sbuf", [128, 64], "float32"),
    "us": ("sbuf", [128, 1024], "bfloat16"),
    "zs": ("sbuf", [128, 1024], "bfloat16"),
    "ul": ("sbuf", [128, 256], "bfloat16"),
    "qi": ("sbuf", [128, 8], "int32"),
    "qf": ("sbuf", [128, 4], "float32"),
    "col": ("sbuf", [128, 4], "float32"),
    "jj": ("sbuf", [128, 144], "bfloat16"),
    "big": ("sbuf", [128, 16], "bfloat16"),
    "msk": ("sbuf", [128, 16], "float32"),
    "kt": ("sbuf", [128, 512], "bfloat16"),
    "six": ("sbuf", [128, 64], "bfloat16"),
    "k2": ("sbuf", [128, 64], "bfloat16"),
    "cc": ("sbuf", [128, 64], "float32"),
    "dm": ("sbuf", [128, 2048], "bfloat16"),
    "bc": ("sbuf", [128, 2048], "bfloat16"),
    "bw": ("sbuf", [128, 144], "bfloat16"),
    "ew": ("sbuf", [128, 144], "bfloat16"),
    "ez": ("sbuf", [128, 144], "bfloat16"),
    "i1": ("sbuf", [128, 128], "bfloat16"),
    "i2": ("sbuf", [128, 128], "bfloat16"),
    "dk": ("sbuf", [128, 128], "bfloat16"),
    "i32": ("sbuf", [128, 128], "float32"),
    "sq": ("sbuf", [128, 128], "float32"),
    "s32": ("sbuf", [128, 128], "float32"),
    "re16": ("sbuf", [128, 32], "uint16"),
    "rfac": ("sbuf", [128, 512], "bfloat16"),
    "ng": ("sbuf", [128, 1024], "bfloat16"),
    "dg": ("sbuf", [128, 1024], "bfloat16"),
    "sel": ("sbuf", [128, 1024], "bfloat16"),
    "rg": ("sbuf", [128, 1024], "bfloat16"),
    "nd": ("sbuf", [128, 1024], "bfloat16"),
    "old": ("sbuf", [128, 512], "bfloat16"),
    "fac": ("sbuf", [128, 512], "bfloat16"),
    "xv": ("sbuf", [128, 64], "float32"),
    "pb": ("sbuf", [128, 64], "bfloat16"),
    "yi": ("sbuf", [128, 64], "int32"),
    "ib": ("sbuf", [128, 128], "int32"),
    "par": ("sbuf", [128, 64], "int32"),
    "sn": ("sbuf", [128, 64], "float32"),
    "sd": ("sbuf", [128, 64], "float32"),
    "d16": ("sbuf", [128, 64], "uint16"),
    "e16": ("sbuf", [128, 32], "uint16"),
    "rb": ("sbuf", [128, 128], "int32"),
    "c2": ("sbuf", [128, 64], "float32"),
    "c216": ("sbuf", [128, 64], "uint16"),
    "fl": ("sbuf", [128, 2048], "float32"),
    "wr": ("sbuf", [128, 512], "float32"),
    "fin": ("sbuf", [128, 1024], "float32"),
}
for _n in ("psa", "psc", "pss0", "pss1", "psm0", "psm1", "pst0", "pst1"):
    SCRATCH[_n] = ("psum", [128, 512], "float32")
for _t in range(4):
    SCRATCH["ff%d" % _t] = ("sbuf", [128, 2560], "float32")
    SCRATCH["ww%d" % _t] = ("sbuf", [128, 1024], "float32")
    SCRATCH["cn%d" % _t] = ("sbuf", [128, 128], "float32")
    SCRATCH["co%d" % _t] = ("sbuf", [128, 128], "uint16")

NDMA = 60
SENDS = {
    "rp": [("l", "rrp", 0, 32, 1, "rrp")],
    "tab": [("a", "rtab", 0, 1024, 2, "rnx"), ("b", "rtab", 1024, 2048, 4, "rsg"), ("c", "rtab", 2048, 3072, 4, "ral")],
    "m": [("a", "rm", 0, 512, 2, "rm"), ("l", "rm", 512, 1024, 2, "rm2")],
    "e": [("b", "re16", 0, 32, 1, "re16")],
    "f": [("a", "rfac", 0, 256, 2, "rfac"), ("l", "rfac", 256, 512, 2, "rfac2")],
}
SEMAPHORES = ["eV", "eS", "eP", "eG", "sent"] + ["d%d" % i for i in range(NDMA)] + [
    x + p[5] for x in ("h_", "a_") for pieces in SENDS.values() for p in pieces]


def helpers(src, dst, T, topo):
    own = [c for c in topo.cores_of(src) if T.rank_of(c) is None]
    same = [c for c in own if topo.die(c) == topo.die(src)]
    a, b = [c for c in same if topo.may_write(c, dst)][:2]
    l = [c for c in own if c not in same and topo.may_write(c, dst)][0]
    c = [x for x in same if x not in (a, b)][0]
    f = [x for x in range(SIM_CORES) if topo.mates(x, dst) and topo.die(x) == topo.die(c) and topo.may_write(c, x) and topo.may_write(x, dst)][0]
    return {"a": a, "b": b, "l": l, "c": c, "f": f}


def helper_program(g, core, src, dst, role, hs, T, topo):
    to = hs["f"] if role == "c" else dst
    rid, pid = topo.addr(to, core)
    sent = 0
    for pieces in SENDS.values():
        for h, buf, a, b, share, key in pieces:
            if h != ("c" if role == "f" else role):
                continue
            g.wait_ge(T.sem["h_" + key], len(topo.engines(hs["c"], core)) if role == "f" else len(topo.engines(src, core)) // share)
            g.remote_dma(T[buf][:, a:b], T[buf][:, a:b], T.sem[("h_" if role == "c" else "a_") + key], T.sem.sent, pid, rid, topo.mask(core, to))
            sent += len(topo.engines(core, to))
    g.wait_ge(T.sem.sent, sent)


def emit(g, T, ops, ext):
    q = {"V": g.vector, "S": g.scalar, "P": g.tensor, "G": g, "Y": g.sync}
    writer, readers = dict(ext), {}
    known = {e: {} for e in q}
    clock, waits, marked = {}, [], set()
    for k in ext.values():
        clock[k] = {k: 1}
    for n, (eng, fn, rd, wr, kind) in enumerate(ops):
        deps = set()
        for key in rd:
            if key in writer:
                deps.add(writer[key])
            if key.startswith("ps"):
                deps.update(r for r in readers.get(key, ()) if ops[r][0] != eng)
        for key in wr:
            if key in writer:
                deps.add(writer[key])
            deps.update(readers.get(key, ()))
        need = []
        for d in sorted(deps, key=lambda x: -x if isinstance(x, int) else 1):
            if isinstance(d, int) and ops[d][4] == "c":
                have = known[eng].get(ops[d][0], -1) >= d or (eng == "P" and ops[d][0] == "P" and "psu" not in wr)
            else:
                have = d in known[eng]
            if not have:
                need.append(d)
                marked.add(d)
                for a, b in clock[d].items():
                    known[eng][a] = max(known[eng].get(a, -1), b)
        waits.append(need)
        c = dict(known[eng])
        c[eng if kind == "c" else n] = n
        clock[n] = c
        for key in rd:
            readers.setdefault(key, []).append(n)
        for key in wr:
            writer[key] = n
            readers[key] = []
    where, count, nd = {}, {e: 0 for e in q}, 0
    left = []
    for n, (eng, fn, rd, wr, kind) in enumerate(ops):
        for d in waits[n]:
            s, v = where[d] if isinstance(d, int) else (T.sem[d[0]], d[1])
            q[eng].wait_ge(s, v)
        if kind == "c":
            ins = fn()
            if n in marked:
                count[eng] += 1
                ins.then_inc(T.sem["e" + eng], 1)
                where[n] = (T.sem["e" + eng], count[eng])
        else:
            s = T.sem["d%d" % nd]
            nd += 1
            if kind == "d":
                fn().then_inc(s, 16)
                where[n] = (s, 16)
            else:
                where[n] = (s, fn(s))
            if n not in marked:
                left.append(where[n])
    for s, v in left:
        g.wait_ge(s, v)


def rank_program(g, core, T, topo):
    N = len(T.cores)
    rank = T.rank_of(core)
    if rank is None:
        for s in range(N):
            src, dst = T.cores[s], T.cores[(s - HOP) % N]
            hs = helpers(src, dst, T, topo)
            for role in hs:
                if hs[role] == core:
                    helper_program(g, core, src, dst, role, hs, T, topo)
        return
    dst = T.cores[(rank - HOP) % N]
    hs = helpers(core, dst, T, topo)
    hin = helpers(T.cores[(rank + HOP) % N], core, T, topo)
    ext = {p[5]: ("a_" + p[5], len(topo.engines(hin["f" if p[0] == "c" else p[0]], core))) for pieces in SENDS.values() for p in pieces}

    ops = []
    V, S, P = g.vector, g.scalar, g.tensor

    def op(eng, fn, rd, wr, kind="c"):
        ops.append((eng, fn, rd, wr, kind))

    def dma(eng, out, in_, rd, wr, add=False):
        qq = {"S": g.scalar, "Y": g.sync, "G": g}[eng]
        if add:
            op(eng, lambda: qq.dma_start(out, in_, accum_op=A.add), rd, wr, "d")
        else:
            op(eng, lambda: qq.dma_start(out, in_), rd, wr, "d")

    def ts(out, in0, s1, s2, o0, o1, rd, wr):
        if o1 is None:
            op("V", lambda: V.tensor_scalar(out, in0, s1, None, o0), rd, wr)
        else:
            op("V", lambda: V.tensor_scalar(out, in0, s1, s2, o0, o1), rd, wr)

    def tt(out, a, b, o, rd, wr):
        op("V", lambda: V.tensor_tensor(out, a, b, o), rd, wr)

    def cp(out, a, rd, wr):
        op("V", lambda: V.tensor_copy(out, a), rd, wr)

    def act(out, a, f, bias, scale, rd, wr):
        op("S", lambda: S.activation(out, a, f, bias=bias, scale=scale), rd, wr)

    def lin(eng, out, src, scale, bias, rd, wr):
        if eng == "S":
            act(out, src, AF.Identity, bias, scale, rd, wr)
        else:
            ts(out, src, scale, bias, A.mult, A.add, rd, wr)

    def mms(lst, rd, wr, start=True, stop=True):
        def fn():
            ins = None
            for n, (o, l, r) in enumerate(lst):
                ins = P.matmul(o, l, r, start and n == 0, stop and n == len(lst) - 1)
            return ins
        op("P", fn, rd, wr)

    def send(name, buf, first, rd):
        def fn(s):
            tr, used = [], 0
            for h, far, a, b, share, key in SENDS[name]:
                rid, pid = topo.addr(hs[h], core)
                every = topo.engines(core, hs[h])
                mine = every[used:used + len(every) // share]
                used += len(mine)
                tr.append(RemoteDMATransfer(dst_ids=[DstId(rid=rid, pnc=pid)], dma_engine_mask=sum(1 << e for e in mine),
                                            remote_sem=T.sem["h_" + key], src=buf[:, first + a:first + b], dst=T[far][:, a:b]))
            g.remote_dma_fused(tr, local_sem=s)
            return used
        op("G", fn, rd, [], "r")

    def rows(buf, src, key, t, rd=()):
        a, p = 1024 * t, 32 * t
        if t < 2:
            dma("Y", buf[p:p + 8, :], src[:, a:a + 1024], rd, [key + "%d" % t])
        else:
            dma("Y", buf[p:p + 8, 0:512], src[:, a:a + 512], [], [key + "%d" % t])
            dma("Y", buf[p + 1:p + 8, 512:1024], src[0:7, a + 512:a + 1024], [], [key + "%da" % t])
            dma("Y", buf[p:p + 1, 512:1024], src[7:8, a + 512:a + 1024], [], [key + "%db" % t])

    def con(n):
        jq = T.jj[:, 0:128]
        if n in ("kt", "six", "k2", "cc"):
            v = {"kt": KK, "six": 0.0625, "k2": 2176 * KK, "cc": -0.5625 + 2.0 ** -13}[n]
            op("V", lambda: V.memset(T[n][:], v), [], [n])
        if n in ("q0", "q1", "q2"):
            k = int(n[1])
            ts(T.qi[:, k:k + 1], T.qi[:, k:k + 1], (15, 112, 7)[k], None, A.bitwise_and, None, [n], [n])
        if n == "qf":
            cp(T.qf[:], T.qi[:, 0:4], ["q0", "q1", "q2"], [n])
        if n == "i1":
            ts(T.i1[:], jq, 0.0, None, A.is_equal, None, ["jj"], [n])
        if n in ("ih0", "ih1"):
            k = int(n[2])
            ts(T.ih[:, 128 * k:128 * (k + 1)], jq, 0.0, (1.0, -2.0)[k], A.is_equal, A.mult, ["jj"], [n])
        if n == "big":
            ts(T.big[:], T.jj[:, 0:16], T.qf[:, 1:2], 256.0, A.add, A.mult, ["jj", "qf"], [n])
        if n == "msk":
            ts(T.msk[:], T.big[:], 0.0, None, A.is_equal, None, ["big"], [n])
        if n == "c0":
            ts(T.col[:, 0:1], T.qf[:, 2:3], -16.0, T.qf[:, 3:4], A.mult, A.add, ["qf"], [n])
        if n == "c1":
            ts(T.col[:, 1:2], T.qf[:, 0:1], 129.0, -KK, A.add, A.mult, ["qf"], [n])
        if n == "ew":
            ts(T.ew[:], T.jj[:], T.col[:, 0:1], 15.0, A.add, A.is_equal, ["jj", "c0"], [n])
        if n == "bw":
            ts(T.bw[:], T.jj[:], T.qf[:, 0:1], 15.0, A.add, A.is_equal, ["jj", "qf"], [n])
        if n == "sq":
            act(T.sq[:], jq, AF.Abs, 48.0, 1.0, ["jj"], [n])
        if n == "s32":
            ts(T.s32[:], T.sq[:], 64.0, None, A.is_equal, None, ["sq"], [n])
        if n == "ce16":
            cp(T.ce16[:], T.cei[:], ["cei"], [n])
        if n == "cf":
            cp(T.cf[:], T.cei[:], ["cei"], [n])

    def mul(eng, n):
        src, f = {"i2": ("i1", 2.0), "i32": ("i1", 1.0), "dk": ("i1", -16 * KK), "ez": ("ew", 2.0 ** -12)}[n]
        lin(eng, T[n][:], T[src][:], f, 0.0, [src], [n])

    def diag(eng, i):
        o = T.dm[:, 128 * i:128 * (i + 1)]
        if eng == "S":
            act(o, T.i1[:], AF.Copy, 0.0, T.msk[:, i:i + 1], ["i1", "msk"], ["dm%d" % i])
        else:
            ts(o, T.jj[:, 0:128], T.big[:, i:i + 1], None, A.is_equal, None, ["jj", "big"], ["dm%d" % i])

    def spread(out, ek, buf, key, t, bank, start, stop):
        p = 32 * t
        mms([(out, T[ek][p:p + 8, 15 - h:143 - h], buf[p:p + 8, h:1024:16]) for h in range(16)],
            [ek] + [key + "%d%s" % (t, x) for x in ("", "a", "b")], [bank], start, stop)

    def pe_u(t):
        spread(T.pst0[:, 64 * t:64 * (t + 1)], "ew", T.us, "u", t, "psu", True, True)

    def cp_u(eng, a, b):
        lin(eng, T.ul[:, 64 * a:64 * b], T.pst0[:, 64 * a:64 * b], 1.0, 0.0, ["psu"], ["ul%d" % t for t in range(a, b)])

    def pe_o():
        mms([(T.psc[:, 0:64], T.i32[:], T.cc[:])], ["i32", "cc"], ["psc"], True, False)

    def pe_z(t):
        spread(T.psc[:, 0:64], "ez", T.zs, "z", t, "psc", False, False)

    DM = ["dm%d" % i for i in range(16)]
    psm, pss = [T.psm0, T.psm1], [T.pss0, T.pss1]

    def tabs(t):
        return (T.tab, "nx", "sg", "al", T.mm, "mm") if t < 2 else (T.rtab, "rnx", "rsg", "ral", T.rm, "rm")

    def cells(t):
        if t == 0:
            return T.cf[:], "cf", T.ce16, "ce16"
        if t == 2:
            return T.c2[:], "c2", T.c216, "c216"
        return T["cn%d" % (t - 1)][:, 0:64], "cn%d" % (t - 1), T["co%d" % (t - 1)], "cu%d" % (t - 1)

    def parts(name, a, b):
        return [name + "%d" % h for h in range(a // 8, b // 8)]

    def g1(t, eng, a, b):
        M, mk_ = tabs(t)[4:6]
        c16, ck = cells(t)[2:4]
        src = M[:].indirect(c16[:, a:b])
        if eng == "S":
            act(T.ng[:, 16 * a:16 * b], src, AF.Relu, -0.0625, 1.0, [mk_, ck], parts("ng", a, b))
        else:
            ts(T.ng[:, 16 * a:16 * b], src, -0.0625, 0.0, A.add, A.max, [mk_, ck], parts("ng", a, b))

    def g2(t, eng, a, b):
        tb, nk = tabs(t)[0:2]
        c16, ck = cells(t)[2:4]
        lin(eng, T.dg[:, 16 * a:16 * b], tb[:, 0:1024].indirect(c16[:, a:b]), 1.0, 0.0, [nk, ck], parts("dg", a, b))

    def pe_a(t):
        mms([(T.psa[:, 0:64], T.i1[:], T.six[:])] +
            [(T.psa[:, 0:64], T.dm[:, 128 * i:128 * (i + 1)], T.ng[:, i:1024:16]) for i in range(16)],
            ["i1", "six"] + parts("ng", 0, 64) + DM, ["psa"])

    def pe_d(b):
        mms([(pss[b][:, 64 * i:64 * (i + 1)], T.i1[:], T.dg[:, 8 * b + i:1024:16]) for i in range(8)],
            ["i1"] + parts("dg", 0, 64), ["pss%d" % b], True, False)

    def pe_p(b):
        mms([(pss[b][:, 64 * i:64 * (i + 1)], T.bc[:, 128 * (8 * b + i):128 * (8 * b + i + 1)], T.pb[:]) for i in range(8)],
            ["pb", "bc%d" % (2 * b), "bc%d" % (2 * b + 1)], ["pss%d" % b], False, True)

    def sel(eng, b):
        lin(eng, T.sel[:, 512 * b:512 * (b + 1)], pss[b][:], 1.0, T.col[:, 1:2], ["pss%d" % b, "c1"], ["sel%d" % b])

    def pe_y(t):
        c, ck = cells(t)[0:2]
        mms([(T.psa[:, 64:128], T.i1[:], T.k2[:]), (T.psa[:, 64:128], T.dk[:], T.pb[:]), (T.psa[:, 64:128], T.i32[:], c)],
            ["i1", "k2", "dk", "pb", "i32", ck], ["psa"], True, False)

    def pe_b(b):
        mms([(T.psa[:, 64:128], T.bw[:, 15 - i:143 - i], T.sel[:, 64 * i:64 * (i + 1)]) for i in range(8 * b, 8 * b + 8)],
            ["bw", "sel%d" % b], ["psa"], False, b == 1)

    def floor(t, h):
        M, mk_ = tabs(t)[4:6]
        ts(T.nd[:, 512 * h:512 * (h + 1)], M[:, 512 * h:512 * (h + 1)], 0.0625, None, A.max, None, [mk_], ["nd%d" % h])

    def pe_m(t, h):
        src, k = (T.mm, "mm") if t == 0 else (T.nd, "nd%d" % h)
        mms([(psm[h][:], T.i2[:], src[:, 512 * h:512 * (h + 1)])], ["i2", k], ["psm%d" % h])

    def rho(t, h):
        tb, _, sk = tabs(t)[0:3]
        tt(psm[h][:], tb[:, 1024 + 512 * h:1536 + 512 * h], psm[h][:], A.mult, [sk, "psm%d" % h], ["psm%d" % h])

    def fnull(t, eng, h):
        lin(eng, T["ff%d" % t][:, 256 + 512 * h:768 + 512 * h], psm[h][:], -1.0, 2.0, ["psm%d" % h], ["fn%d_%d" % (t, h)])

    def edge(t, eng, h):
        a = 1280 * (1 - h)
        lin(eng, T["ff%d" % t][:, a:a + 256], psm[h][:, 256 * h:256 * (h + 1)], -1.0, 2.0, ["psm%d" % h], ["fe%d_%d" % (t, h)])

    def fnull3(eng, h):
        lin(eng, T.fl[:, 1024 * h:1024 * (h + 1):2], psm[h][:], -1.0, 2.0, ["psm%d" % h], ["fm%d" % h])

    def freal(t, h):
        tb, ak = tabs(t)[0], tabs(t)[3]
        o = T["ff%d" % t][:, 1536 + 512 * h:2048 + 512 * h] if t < 3 else T.fl[:, 1024 * h + 1:1024 * (h + 1):2]
        tt(o, tb[:, 2048 + 512 * h:2560 + 512 * h], psm[h][:], A.mult, [ak, "psm%d" % h], ["fr%d_%d" % (t, h)])

    def sm(t, names):
        cn, co = T["cn%d" % t], T["co%d" % t]
        for n in names.split():
            if n == "xv":
                tt(T.xv[:], T.psa[:, 0:64], T.ul[:, 64 * t:64 * (t + 1)], A.mult, ["psa", "ul%d" % t], ["xv"])
            if n == "pb":
                ts(T.pb[:], T.xv[:], 15.0, 128.53125, A.min, A.add, ["xv"], ["pb"])
            if n == "d16":
                ts(T.d16[:], T.psa[:, 64:128], 8 * KK + 256, None, A.add, None, ["psa"], ["d16"])
            if n == "yi":
                cp(T.yi[:], T.psa[:, 64:128], ["psa"], ["yi"])
            if n == "par":
                ts(T.par[:], T.yi[:], 1, None, A.bitwise_and, None, ["yi"], ["par"])
            if n == "ya":
                ts(T.yh[:, 0:32], T.psa[:, 80:112], 8 * KK + 512, None, A.add, None, ["psa"], ["ya"])
            if n == "yb":
                ts(T.yh[:, 32:64], T.psa[:, 80:112], 0.5, 4 * KK + 1151.75, A.mult, A.add, ["psa"], ["yb"])
            if n == "e16":
                ts(T.e16[:], T.psa[:, 128:160], 1792.0, None, A.add, None, ["psa"], ["e16"])
            if n == "db":
                ts(T.ib[:, 64:128], T.yi[:], 1023, None, A.bitwise_and, None, ["yi"], ["ibd"])
            if n == "sn":
                ts(T.sn[:], T.par[:], 2.0, -1.0, A.mult, A.add, ["par"], ["sn"])
            if n == "sd":
                tt(T.sd[:], T.ib[:, 64:128], T.sn[:], A.mult, ["ibd", "sn"], ["sd"])
            if n == "nc":
                tt(T.ib[:, 0:64], T.psc[:, 0:64], T.sn[:], A.mult, ["psc", "sn"], ["ibe"])
            if n == "nu":
                cp(co[:, 0:64], T.ib[:, 0:64], ["ibe"], ["cu%d" % t])
            if n == "nf":
                cp(cn[:, 0:64], T.ib[:, 0:64], ["ibe"], ["cn%d" % t])
            if n == "ne":
                tt(T.rb[:, 0:64], T.ib[:, 0:64], T.ib[:, 64:128], A.not_equal, ["ibe", "ibd"], ["rbe"])
            if n == "nm":
                ts(T.rb[:, 64:128], T.rb[:, 0:64], 1280.0, None, A.mult, None, ["rbe"], ["rbd"])
            if n == "na":
                tt(cn[:, 64:128], T.rb[:, 64:128], T.ib[:, 64:128], A.add, ["rbd", "ibd"], ["cw%d" % t])
            if n == "no":
                cp(co[:, 64:128], cn[:, 64:128], ["cw%d" % t], ["co%d" % t])
            if n == "m2":
                ts(T.sd[:], T.ib[:, 64:128], -2.0, None, A.mult, None, ["ibd"], ["sd"])
            if n == "on":
                ts(co[:, 64:128], T.psc[:, 0:64], -1.0, None, A.mult, None, ["psc"], ["co%d" % t])
            if n == "v2":
                src, a, b, rd = (T.rpi[:, 0:64], 0, 64, "rpi") if t == 0 else (T.rrp[:], 64, 96, "rrp")
                ts(T.v2[:, a:b], src, 2.0, None, A.mult, None, [rd], ["v2_%d" % (t // 2)])
            if n == "c16":
                cp(T.c216[:], T.psc[:, 64:128], ["psc"], ["c216"])

    def pe_r(t):
        o = T.psa[:, 128:160]
        mms([(o, T.ih[:, 0:128], T.v2[:, 32 * t:32 * (t + 1)]), (o, T.ih[:, 0:128], T.yh[:, 0:32]), (o, T.ih[:, 128:256], T.yh[:, 32:64])],
            ["ih0", "ih1", "v2_%d" % (t // 2), "ya", "yb"], ["psa"])

    def cells2(eng):
        lin(eng, T.c2[:], T.psc[:, 64:128], 1.0, 0.0, ["psc"], ["c2"])

    def pe_s(h):
        m = ("i32", "s32")[h]
        mms([(T.psc[:, 64 + 32 * h:96 + 32 * h], T[m][:], T.cn1[:, 32 * h:32 * h + 32])], [m, "cn1"], ["psc"])

    def null_at(t, a, b):
        return T["ff%d" % t][:, 0:1536].indirect(T.d16[:, a:b]), ["fn%d_0" % t, "fn%d_1" % t, "fe%d_0" % t, "fe%d_1" % t, "d16"]

    def g4(t, eng, a, b):
        src, rd = null_at(t, a, b)
        lin(eng, T.rg[:, 16 * a:16 * b], src, 1 / 32, 0.0, rd, parts("rg", a, b))

    def fac(t):
        src, rd = null_at(t, 16, 48) if t == 1 else (T.rg[:, 256:768], parts("rg", 16, 48))
        ts(T.fac[:], src, 0.0, 0.5, A.is_ge, A.max, rd, ["fac"])

    def old(t, eng, h):
        M, mk_ = tabs(t + 1)[4:6]
        e, ek = (T.re16, "re16") if t == 1 else (T.e16, "e16")
        lin(eng, T.old[:, 256 * h:256 * (h + 1)], M[:].indirect(e[:, 16 * h:16 * (h + 1)]), 1.0, 0.0, [mk_, ek] + ["rm2"] * (t == 1), ["old%d" % h])

    def scat(t, h):
        M, mk_ = tabs(t + 1)[4:6]
        e, f = ("re16", "rfac") if t == 1 else ("e16", "fac")
        a, b = ((0, 16), (16, 32), (0, 32))[h]
        tt(M[:].indirect(T[e][:, a:b]), T.old[:, 16 * a:16 * b], T[f][:, 16 * a:16 * b], A.mult, ["old0", "old1", f, e] + ["rfac2"] * (t == 1), [mk_])

    def pe_c(t):
        mms([(T.psc[:, 0:64], T.dm[:, 128 * i:128 * (i + 1)], T.rg[:, i:1024:16]) for i in range(16)],
            parts("rg", 0, 64) + DM, ["psc"], False, False)

    def pe_e():
        mms([(T.psc[:, 0:64], T.i32[:], T.sd[:])], ["i32", "sd"], ["psc"], False, True)

    def factor(t, h):
        off = T["co%d" % t][:, 64 + 32 * h:96 + 32 * h]
        return T["ff%d" % t][:, 256:2560].indirect(off), [k % t for k in ("fn%d_0", "fn%d_1", "fe%d_0", "fr%d_0", "fr%d_1", "co%d")]

    def weights(t, h):
        w, key = T["ww%d" % t][:, 512 * h:512 * (h + 1)], ["w%d_%d" % (t, h)]
        src, rd = factor(t, h)
        if t == 0:
            ts(w, src, 0.125, 4.0, A.max, A.min, rd, key)
        elif t == 2 and h == 1:
            tt(w, src, T.wr[:], A.mult, rd + ["wr0", "wr1"], key)
        else:
            tt(w, src, T["ww%d" % (t - 1)][:, 512 * h:512 * (h + 1)], A.mult, rd + ["w%d_%d" % (t - 1, h)], key)

    def clip(t, h):
        w, key = T["ww%d" % t][:, 512 * h:512 * (h + 1)], ["w%d_%d" % (t, h)]
        ts(w, w, 0.125, 4.0, A.max, A.min, key, key)

    BOUNDS = ((AF.Relu, 4.0, -1.0), (AF.Relu, 3.875, -1.0), (AF.Identity, 0.125, 1.0))

    def sclip(t, h, k):
        w, key = T["ww%d" % t][:, 512 * h:512 * (h + 1)], ["w%d_%d" % (t, h)]
        f, bias, scale = BOUNDS[k]
        src, rd = factor(t, h) if t == 0 and k == 0 else (w, key)
        act(w, src, f, bias, scale, rd, key)

    def pe_sum(t, k):
        h, a = k // 2, 256 * (k % 2)
        m = "s32" if h == 1 and t < 2 else "i32"
        mms([(T["pst%d" % h][:, a:a + 256], T[m][:], T["ww%d" % t][:, 256 * k:256 * (k + 1)])], [m, "w%d_%d" % (t, h)],
            ["pst%d" % h] + ["psu"] * (t + k == 0), t == 0 and a == 0, t == 2 and k in (0, 3))

    def move_w1():
        dma("Y", T.wr[16:128, :], T.ww1[0:112, 512:1024], ["w1_1"], ["wr0"])
        dma("Y", T.wr[0:16, :], T.ww1[112:128, 512:1024], ["w1_1"], ["wr1"])

    def last(n, k):
        a = 256 * k
        w, key = T.ww3[:, a:a + 256], ["w3_%d" % k]
        if n == "w":
            tt(w, T.fl[:].indirect(T.co3[:, 64 + 16 * k:80 + 16 * k]), T.ww2[:, a:a + 256], A.mult,
               ["fm0", "fm1", "fr3_0", "fr3_1", "co3", "w2_%d" % (k // 2)], key)
        if n == "c":
            ts(w, w, 0.125, 4.0, A.max, A.min, key, key)
        if n[0] == "s":
            f, bias, scale = BOUNDS[int(n[1])]
            act(w, w, f, bias, scale, key, key)
        if n == "a":
            tt(T.fin[:, a:a + 256], w, T["pst%d" % (k // 2)][:, a % 512:a % 512 + 256], A.add, key + ["pst%d" % (k // 2)], ["fin%d" % k])

    def out(q, p, a, b):
        src, to = {0: (slice(0, 128), slice(0, 128)), 1: (slice(16, 128), slice(0, 112)), 2: (slice(0, 16), slice(112, 128))}[p]
        dma(q, T.tl[to, 256 * a:256 * b], T.fin[src, 256 * a:256 * b], ["fin%d" % k for k in range(a, b)], ["tl%d%d" % (p, a)])

    def send_m():
        send("m", T.mm, 0, ["mm"])

    def send_f():
        send("f", T.fac, 0, ["fac"])

    def send_e():
        send("e", T.e16, 0, ["e16"])

    dma("S", T.cei[:], T.ce[:], [], ["cei"])
    dma("Y", T.mm[:], T.mj[:], [], ["mm"])
    dma("S", T.us[0:8, :], T.uu[:, 0:1024], [], ["u0"])
    dma("Y", T.tab[:, 0:1024], T.nx[:], [], ["nx"])
    dma("Y", T.tab[:, 1024:2048], T.sg[:], [], ["sg"])
    dma("Y", T.rpi[:], T.rp[:], [], ["rpi"])
    dma("Y", T.tab[:, 2048:3072], T.al[:], [], ["al"])
    rows(T.zs, T.zz, "z", 0)
    for t in range(1, 4):
        rows(T.us, T.uu, "u", t, ["al"])
        rows(T.zs, T.zz, "z", t)
    op("G", lambda: g.iota(T.qi[:], [[0, 8]], 0, 1), [], ["q0", "q1", "q2"])
    op("G", lambda: g.iota(T.jj[:], [[1, 144]], 0, -1, allow_small_or_imprecise_dtypes=True), [], ["jj"])
    con("kt")
    for k in range(4):
        op("G", lambda k=k: g.affine_select(T.bc[:, 512 * k:512 * (k + 1)], T.kt[:], [[-1, 4], [-16, 8], [0, 16]], A.is_equal, 0.0, -4 * k, 1),
           ["kt"], ["bc%d" % k])
    send("tab", T.tab, 0, ["nx", "sg", "al"])
    send("rp", T.rpi, 64, ["rpi"])

    con("q1"); con("q0"); con("q2"); con("six"); con("cc"); con("sq"); con("qf"); con("i1"); con("big"); mul("S", "i2")
    con("c1"); con("c0"); mul("S", "dk"); mul("S", "i32"); con("msk"); diag("V", 0); diag("V", 1); con("ew"); diag("V", 2)
    diag("V", 3); diag("S", 10); diag("S", 11); pe_u(0); diag("S", 12); con("ce16"); diag("V", 4); diag("S", 13); diag("V", 5)
    diag("V", 6); diag("S", 14); diag("V", 7); diag("V", 8); diag("S", 15); diag("V", 9)
    g1(0, "V", 32, 64); g1(0, "S", 0, 32)
    pe_m(0, 0); g2(0, "V", 32, 64); g2(0, "S", 0, 32); pe_a(0); rho(0, 0); cp_u("S", 0, 1); pe_m(0, 1); pe_d(0)
    sm(0, "xv v2"); pe_d(1); edge(0, "S", 0); sm(0, "pb"); con("cf"); con("bw"); fnull(0, "S", 0); con("ih1")
    con("k2"); rho(0, 1); pe_p(0); pe_p(1); con("ih0"); sel("S", 0); pe_y(0); sel("V", 1); mul("S", "ez"); fnull(0, "S", 1)
    pe_b(0); freal(0, 0); pe_b(1); edge(0, "S", 1); pe_o(); pe_z(0); sm(0, "d16 yi ya yb")
    g4(0, "S", 16, 48); sm(0, "par db"); pe_r(0); g4(0, "V", 48, 64); sm(0, "e16"); g4(0, "V", 0, 16)
    old(0, "S", 0); sm(0, "sn"); fac(0); pe_c(0); old(0, "S", 1); sm(0, "sd"); freal(0, 1); pe_e(); pe_u(1); scat(0, 0); cp_u("S", 1, 2)
    sm(0, "nc"); pe_o(); pe_z(1); con("s32"); sm(0, "nu"); scat(0, 1); g2(1, "S", 0, 16); sm(0, "nf"); send_m()
    g1(1, "V", 32, 64); g1(1, "S", 0, 32); sm(0, "ne"); g2(1, "S", 16, 48); floor(1, 0); pe_a(1); floor(1, 1); g2(1, "V", 48, 64)
    pe_m(1, 1); sm(0, "nm"); sm(1, "xv"); pe_m(1, 0); sm(1, "pb"); pe_d(0); rho(1, 1); pe_d(1); sm(0, "na"); pe_p(0); rho(1, 0)
    pe_p(1); sm(0, "no"); sel("S", 0); pe_y(1); sel("V", 1); edge(1, "S", 1); edge(1, "S", 0); pe_b(0); fnull(1, "S", 0)
    fnull(1, "V", 1); pe_b(1); pe_u(2); sm(1, "d16 ya yi yb"); g4(1, "S", 0, 64); fac(1); pe_r(1)
    pe_u(3); sm(1, "e16 par"); freal(1, 0); send_e(); sm(1, "sn"); send_f(); sm(1, "db")
    freal(1, 1); sclip(0, 1, 0); pe_c(1); sm(1, "sd"); weights(0, 0); pe_e(); sclip(0, 1, 1); sm(1, "nc"); cp_u("S", 2, 4)
    sm(1, "ne nf"); sclip(0, 1, 2); sm(1, "nm"); pe_s(0); pe_s(1); sm(1, "na"); pe_sum(0, 0); sm(2, "v2"); sm(1, "no c16")
    cells2("V"); pe_sum(0, 2); weights(1, 1); g2(2, "S", 0, 16); pe_o(); pe_z(2); weights(1, 0); old(1, "S", 1)
    old(1, "S", 0); pe_sum(0, 3); clip(1, 1); g2(2, "S", 16, 64); scat(1, 2); pe_sum(0, 1); move_w1(); pe_d(0); pe_d(1)
    g1(2, "V", 32, 64); g1(2, "S", 0, 32); floor(2, 1); floor(2, 0); pe_a(2)
    clip(1, 0); pe_m(2, 0); sm(2, "xv"); pe_m(2, 1); sm(2, "pb"); rho(2, 0); pe_p(0); rho(2, 1); pe_p(1); sel("S", 0); pe_y(2)
    sel("V", 1); edge(2, "S", 1); fnull(2, "S", 0); pe_b(0); fnull(2, "V", 1); pe_b(1); edge(2, "S", 0); sm(2, "d16 yi yb ya")
    g4(2, "S", 16, 48); sm(2, "par"); g4(2, "V", 0, 16); pe_r(2); pe_sum(1, 0)
    sm(2, "sn e16"); g4(2, "V", 48, 64); old(2, "S", 0); pe_sum(1, 1); sm(2, "db"); fac(2); old(2, "S", 1); freal(2, 0)
    pe_c(2); sm(2, "sd"); scat(2, 0); pe_e(); pe_sum(1, 2); sm(2, "nc"); pe_o(); pe_z(3); pe_sum(1, 3); sm(2, "nu"); scat(2, 1); g2(3, "S", 0, 16); sm(2, "ne")
    g1(3, "S", 0, 32); g1(3, "V", 32, 64); sm(2, "nm"); g2(3, "S", 16, 64); floor(3, 0); pe_a(3); floor(3, 1); freal(2, 1)
    pe_m(3, 0); sm(2, "na"); sm(3, "xv"); sm(2, "nf"); pe_m(3, 1); sm(2, "no"); sm(3, "pb"); rho(3, 0); pe_d(0); pe_p(0)
    weights(2, 1); pe_d(1); edge(3, "S", 0); pe_p(1); sel("S", 0); rho(3, 1); pe_y(3); sel("S", 1); weights(2, 0); pe_b(0)
    fnull(3, "S", 0); pe_b(1); clip(2, 1); edge(3, "S", 1); fnull(3, "S", 1); sm(3, "yi d16"); clip(2, 0)
    pe_sum(2, 2); g4(3, "S", 0, 32); g4(3, "V", 32, 64); sm(3, "db")
    fnull3("S", 1); freal(3, 0); pe_c(3); sm(3, "m2"); freal(3, 1); fnull3("S", 0); pe_e(); pe_sum(2, 1); pe_sum(2, 0); sm(3, "on")
    last("w", 2); pe_sum(2, 3); last("w", 3); last("s0", 2); last("w", 1); last("s0", 3); last("w", 0); last("s1", 2)
    last("c", 1); last("s1", 3); last("c", 0); last("s2", 2); last("a", 1); last("s2", 3); last("a", 0); out("Y", 0, 0, 2)
    last("a", 2); last("a", 3); out('S', 1, 2, 4); out("Y", 2, 2, 4)
    emit(g, T, ops, ext)
